import numpy as np, ml_dtypes
CORES = [3,7,11,15,131,135,139,143]
N = 8
import mx_ref
BF = ml_dtypes.bfloat16
def gentries(a):
    return np.ascontiguousarray(a.reshape(8, 16, -1).transpose(0, 2, 1)).reshape(8, -1)
def gtable(e):
    e = np.asarray(e); return np.ascontiguousarray(e.reshape(8, -1, 16).transpose(0, 2, 1)).reshape(128, -1).astype(np.int32)
def gcols(t, e):
    v = np.concatenate([t.reshape(8, 16, -1, 4), np.zeros((8, 16, 1, 4), BF)], axis=2)
    return np.ascontiguousarray(np.stack([v[g][:, e[g]] for g in range(8)])).reshape(128, -1)
def tile(rs):
    return np.stack(rs, axis=2).reshape(128, -1).astype(BF)
def pick(q, e):
    c = np.concatenate([q[0].reshape(128, -1, 4), np.zeros((128, 1, 4), np.uint8)], axis=1); s = np.concatenate([q[1], np.ones((16, 1), np.uint8)], axis=1)
    return (np.ascontiguousarray(c[:, e].reshape(128, -1)), np.ascontiguousarray(s[:, e]))
def join(*qs):
    return (np.concatenate([q[0] for q in qs], axis=1), np.concatenate([q[1] for q in qs], axis=1))
def put(q, e, v):
    c, s = q[0].reshape(128, -1, 4).copy(), q[1].copy(); c[:, e] = v[0].reshape(128, -1, 4); s[:, e] = v[1]
    return (c.reshape(128, -1), s)
def pk(c, s):
    return (np.ascontiguousarray(c), mx_ref.live(s))
def emit(q):
    return q[0], q[1]
def packed(v, rng):
    q = [mx_ref.quantize(np.ascontiguousarray(v[r])) for r in range(N)]
    return np.stack([a for a, b in q]), np.stack([mx_ref.plane(b, rng) for a, b in q])
def values_of_codes():
    e, c = np.zeros((128, 128, 4), np.float32), np.zeros((128, 2, 4), np.uint8)
    e[np.arange(128), np.arange(128), 0] = 1
    c[:127, :, 0] = np.arange(256).reshape(2, 128).T[:127]
    return mx_ref.matmul(mx_ref.quantize(e.reshape(128, 512).astype(BF)), (c.reshape(128, 8), np.full((16, 2), 127, np.uint8))).T.reshape(-1).astype(np.float64)
CODE_VALUE, SCALE_VALUE = values_of_codes(), 2.0 ** (np.arange(256) - 127.0)
def decode(q):
    return (CODE_VALUE[q[0]].reshape(16, 8, -1, 4) * SCALE_VALUE[q[1]][:, None, :, None] + 0.0).reshape(128, -1).astype(np.float32)
def f(rng, *shape):
    return mx_ref.flush((rng.standard_normal(shape, dtype=np.float32) * np.exp2(rng.integers(-2, 3, shape[:-1] + (1,)))).astype(BF))
def wide(rng, *shape, cols=0):
    v = rng.standard_normal(shape, dtype=np.float32) * np.exp2(rng.integers(-12, 13, shape)).astype(np.float32)
    if cols: v *= np.repeat(np.exp2(rng.integers(-cols, cols + 1, shape[:-2] + (1, shape[-1] // 4))) * (rng.random(shape[:-2] + (1, shape[-1] // 4)) > 0.0625), 4, axis=-1).astype(np.float32)
    return mx_ref.flush(v.astype(BF))
C = 288
STEP = [4, 1, 2]
def numbers_of(rng):
    return {"x": np.array(f(rng, N, 128, 4 * C)), "u": np.array(f(rng, N, 128, 512)), "v": np.array(f(rng, N, 128, 512))}
def stored(w):
    return {"wl": np.stack([gtable(w[r]) for r in range(N)])}
def joined(k):
    w = np.zeros_like(k)
    np.put_along_axis(w, k[..., 0::2], k[..., 1::2], axis=-1)
    np.put_along_axis(w, k[..., 1::2], k[..., 0::2], axis=-1)
    return w
def wiring(rng):
    return stored(joined(rng.permuted(np.tile(np.arange(3 * C), (N, 8, 1)), axis=2)))
def edges(rng):
    w = np.zeros((N, 8, 3 * C), np.int64)
    c, i = np.arange(C), np.arange(3 * C)
    for r in range(N):
        a = C + rng.permutation(2 * C)
        k = [i ^ 1, 3 * C - 1 - i, (i + 3 * (C // 2)) % (3 * C), np.concatenate([c + C, c, (c ^ 1) + 2 * C]), np.concatenate([C - 1 - c, c + 2 * C, c + C]),
             joined(np.concatenate([rng.permutation(C), C + rng.permutation(2 * C)])), joined(np.concatenate([np.stack([c, a[:C]], axis=1).reshape(-1), a[C:]])), joined(rng.permutation(3 * C))]
        w[r, rng.permutation(8)] = np.stack(k)
    return stored(w)
def layers(rng):
    return np.array(f(rng, N, 128, 2048)).reshape(N, 8, 16, 4, 8, 16, 4)
def weights(rng, w):
    c, p = packed(np.ascontiguousarray(w).reshape(N, 128, 2048), rng)
    return {"wc": c, "ws": p}
def blank(d):
    u = d["u"].reshape(N, 128, 128, 4)
    u[:, :, 0::16] = 0
    u[:, :, 1::16] = 0
    return u
def setup_inputs(rng):
    return {**numbers_of(rng), **wiring(rng), **weights(rng, layers(rng))}
def setup_inputs_ties(rng):
    d = numbers_of(rng)
    o = rng.permutation(N)
    k = rng.integers(-1, 2, (N, 8, 2, C)).astype(np.float32)
    k[o[1]] = 1
    x = d["x"].reshape(N, 8, 16, C, 4)
    x[:, :, :3] = 0
    x[:, :, :2, :, 0] = k.astype(BF)
    x[:, :, 2, :, 0] = 1.96875 * 2.0 ** 7
    x[:, :, 3] = (np.array([9.0, 11.0, 5.0, 7.0]) * 2.0 ** -9).astype(np.float32).astype(BF)
    a = np.exp2(rng.integers(-3, 4, (1, 8, 1)).astype(np.float32))
    x[:, :, 8:] = 0
    x[:, :, 8, :, 0] = (-1.125 * a).astype(BF)
    x[:, :, 10, :, 0] = (-0.0703125 * a).astype(BF)
    c = np.ones(N, np.float32)
    c[o[0]] = 0
    c[o[2]] = -1
    u = blank(d)
    for h in range(0, 128, 16):
        for i in range(2): u[:, h + i, h + i, 0] = c.astype(BF)
    w = layers(rng)
    w[:, :, 2] = 0
    w[:, :, :, :, :, :4] = 0
    w[:, :, :, :, :, 8:] = 0
    for g in range(8):
        w[:, g, 8, 0, g, 8, 0] = -28.0
        for b in range(4):
            w[:, g, 10, b, g, 9, 0] = -2.0 ** (b - 5)
            w[:, g, 3, b, g, 3, b] = 64.0
    return {"x": x.reshape(N, 128, 4 * C), "u": u.reshape(N, 128, 512), "v": d["v"], **wiring(rng), **weights(rng, w)}
def setup_inputs_near(rng):
    d = numbers_of(rng)
    o = np.zeros(N, np.int64)
    for i, r in enumerate(rng.permutation([r for r in range(N) if r < (r ^ STEP[0])])):
        o[[r, r ^ STEP[0]]] = rng.permutation([0, 3] if i % 2 == 0 else [1, 2])
    x = d["x"].astype(np.float32).reshape(N, 8, 16, C, 4)
    x[:, :, :8] = 0
    u = blank(d)
    at = [0, C - 1, int(rng.integers(C)), int(rng.integers(C))]
    for r in range(N):
        s = rng.integers(-1, 2, (2, 8, C)).astype(np.float32)
        k = 2.0 ** -30 if o[r] in (0, 3) else 1.0
        for i in range(2):
            if o[r] == 2: x[r, :, 2 * i, :, 0] = s[i] * 2.0 ** -8
            else:
                x[r, :, 2 * i, :, 0] = 1.125 * k * s[i]
                x[r, :, 2 * i + 1, :, 0] = -1.25 * k * s[i]
                for g, j in zip(rng.permutation(8)[:4], at): x[r, g, 2 * i, j, 0] = 2.0 ** 30 * rng.choice([-1.0, 1.0])
            for h in range(0, 128, 16):
                u[r, h + 2 * i, h + i, 0] = 1.125 * k
                u[r, h + 2 * i + 1, h + i, 0] = k
        if o[r] == 2: x[r, :, 4, :, 0] = 1.96875 * 2.0 ** 8
        x[r, :, 5, :, 0] = rng.choice([-1.0, 1.0], (8, C)) * 2.0 ** -30
        x[r, :, 6, :, 0] = 2.0 ** -28
    w = layers(rng)
    w[:, :, :8] = 0
    w[:, :, :, :, :, :8] = 0
    for g in range(8):
        w[:, g, 5, 0, g, 0, 0] = 2.0 ** -8
        w[:, g, 5, 0, g, 2, 0] = 2.0 ** -8
        w[:, g, 5, 0, g, 6, 0] = 32.0
    return {"x": x.reshape(N, 128, 4 * C).astype(BF), "u": u.reshape(N, 128, 512), "v": d["v"], **wiring(rng), **weights(rng, w)}
def setup_inputs_late(rng):
    d = numbers_of(rng)
    c = (rng.permutation(N) % 2 * 2.0 - 1.0).astype(np.float32).astype(BF)
    x = d["x"].reshape(N, 8, 16, C, 4)
    x[:, :, :2] = c[:, None, None, None, None]
    u = blank(d)
    for h in range(0, 128, 16):
        for i in range(2): u[:, h + i, h + i, 0] = 1
    w = layers(rng)
    w[:, :, :, :, :, :2] = (w[:, :, :, :, :, :2].astype(np.float32) * 4).astype(BF)
    return {"x": x.reshape(N, 128, 4 * C), "u": u.reshape(N, 128, 512), "v": d["v"], **edges(rng), **weights(rng, w)}
def setup_inputs_ends(rng):
    d = numbers_of(rng)
    e = [0, STEP[0], STEP[1], STEP[0] ^ STEP[1]]
    e = e + [STEP[2] ^ i for i in e[:N - 4]]
    n = N // 4
    o = np.zeros(N, np.int64)
    o[np.array(e) ^ int(rng.integers(N))] = np.concatenate([np.full(n, 3), np.full(n, 2), rng.permutation(np.arange(2 * n) % 2)])
    x = np.zeros((N, 128, C, 4))
    u = blank(d).astype(np.float32)
    v = rng.choice([-1.0, 1.0], (N, 128, 512))
    w = np.zeros((N, 128, 4, 128, 4), np.float32)
    p = np.arange(128)
    for r in range(N):
        x[r] = (0.9 + 0.02 * rng.random((128, C, 4))) * 2.0 ** 30
        if o[r] == 0: x[r] *= -1
        if o[r] == 1: x[r] *= (1.0 - 2.0 * (np.arange(C) % 2))[None, :, None]
        if o[r] == 2: x[r] *= rng.choice([-1.0, 1.0], (128, C, 4))
        if o[r] == 3:
            x[r] = (1.0 + 0.125 * rng.integers(0, 8, (128, C, 4))) * 2.0 ** -30 * rng.choice([-1.0, 1.0], (1, C, 1))
            x[r, 0::8, :, 0] = 1.5 * 2.0 ** -29
        for i in range(2):
            h = rng.permutation(8)
            u[r, :, i::16] = np.where(h < 2, 0.0, h % 2 * 2.0 - 1.0)[None, :, None] * (2.0 ** -30 if o[r] == 3 else 2.0 ** 30)
        v[r] *= 2.0 ** 30 if o[r] % 2 == 0 else 2.0 ** -30
        for b in range(4): w[r, p, b, p, b] = [-0.25, -0.25, 2.0 ** -8, 256.0][o[r]]
    return {"x": x.astype(np.float32).reshape(N, 128, 4 * C).astype(BF), "u": u.reshape(N, 128, 512).astype(BF), "v": v.astype(np.float32).astype(BF), **edges(rng), **weights(rng, w.astype(BF))}
def setup_inputs_spread(rng):
    d = setup_inputs(rng)
    d["x"] = wide(rng, N, 128, 4 * C, cols=6)
    return d
def check_inputs(d):
    b = []
    for k in ("x", "u", "v"):
        a = np.abs(d[k].astype(np.float32))
        if not (np.isfinite(a).all() and ((a == 0) | (a >= 2.0 ** -30) & (a <= 2.0 ** 30)).all()): b.append("a value of " + k)
    none, least, most = [emit(mx_ref.quantize(np.full((128, 16), k, np.float32).astype(BF)))[1][0, 0] for k in (0.0, 2.0 ** -8, 2.0 ** 8)]
    for r in range(N):
        e, i = gentries(d["wl"][r]), np.arange(3 * C)
        if not ((e >= 0) & (e < 3 * C)).all(): b.append("an entry of wl")
        elif (e == i).any() or (np.take_along_axis(e, e, axis=1) != i).any(): b.append("wl: ports that aren't wired in pairs")
        if ((d["wc"][r] == 0x7F) | (d["wc"][r] == 0xFF)).any(): b.append("wc: a code that is no number")
        s = mx_ref.live(d["ws"][r])
        if ((s != none) & ((s < least) | (s > most))).any(): b.append("ws: a scale out of range")
    return b
def rewired(w, a, b):
    c, d = np.arange(C), w[:, :C]
    active = d < C
    same = a == np.take_along_axis(a, np.minimum(d, C - 1), axis=1)
    turn, cross, swap = active & same, active & ~same, ~active & b
    to = np.concatenate([np.where(turn | swap, c + C, c),
                         np.where(turn, c + 2 * C, np.where(cross, d + C, np.where(swap, c, c + C))),
                         np.where(turn, c, np.where(cross, d + 2 * C, c + 2 * C))], axis=1)
    new = np.zeros_like(to)
    np.put_along_axis(new, to, np.take_along_axis(to, w, axis=1), axis=1)
    return new
def reference(x, u, v, wl, wc, ws):
    qu = [mx_ref.quantize(u[r]) for r in range(N)]
    lay = [pk(wc[r], ws[r]) for r in range(N)]
    wire = [gentries(wl[r]).astype(np.int64) for r in range(N)]
    now = [x[r] for r in range(N)]
    for step in STEP:
        made = []
        for r in range(N):
            s = mx_ref.matmul(qu[r], mx_ref.quantize(now[r]))
            wire[r] = rewired(wire[r], s[0::16] > 0, s[1::16] > 0)
            one, two = gcols(now[r], wire[r][:, C:2 * C] % C), gcols(now[r], wire[r][:, 2 * C:] % C)
            z = mx_ref.quantize(((one.astype(np.float32) + two.astype(np.float32)) * np.float32(0.5)).astype(BF))
            made.append(mx_ref.quantize(tile([mx_ref.matmul(pick(lay[r], np.arange(128 * b, 128 * b + 128)), z) * np.float32(0.03125) for b in range(4)])))
        for r in range(N):
            p = r ^ step
            m = np.take_along_axis(wire[p], wire[r][:, :C], axis=1) % C
            now[r] = (now[r].astype(np.float32) + gcols(decode(made[p]).astype(BF), m).astype(np.float32)).astype(BF)
    y, ow = np.zeros((N, 128, C), np.float32), np.zeros((N, 8, 3 * C), np.float32)
    oc, osc = np.zeros((N, 128, 4 * C), np.uint8), np.zeros((N, 16, C), np.uint8)
    for r in range(N):
        q = mx_ref.quantize(now[r])
        y[r] = mx_ref.matmul(mx_ref.quantize(v[r]), q)
        ow[r] = wire[r]
        oc[r], osc[r] = emit(q)
    return {"y": y, "ow": ow, "oc": oc, "osc": osc}

@@ -1,0 +1,431 @@
+from concourse.mybir import dt, AluOpType as A, ActivationFunctionType as F
+
+C = 288
+STEP = [4, 1, 2]
+HUGE = 1e29
+BIG = 2097152.0
+CUT = [(0, 160), (160, 288)]
+
+_f, _b, _i, _u = "float32", "bfloat16", "int32", "uint16"
+_q, _s = "float8_e4m3fn_x4", "uint8"
+
+
+def _scratch():
+    d = {}
+
+    def sb(name, n, t):
+        d[name] = ("sbuf", [128, n], t)
+    sb("ut", 512, _b); sb("vt", 512, _b); sb("wi", 54, _i)
+    sb("wq", 512, _q); sb("wsc", 512, _s)
+    sb("uq", 128, _q); sb("us", 128, _s); sb("u2", 256, _q); sb("u2s", 256, _s)
+    sb("vq", 128, _q); sb("vs", 128, _s)
+    sb("ones", 512, _b); sb("et", 2048, _b); sb("eq", 512, _q); sb("esc", 512, _s)
+    sb("cr", C, _f); sb("cr0", C, _f); sb("t0", 2 * C, _f); sb("t1", 2 * C, _f); sb("t2", 2 * C, _f); sb("t3", 2 * C, _b)
+    sb("ei", 16, _i); sb("ea", 16, _i); sb("e0", 16, _b); sb("e1", 16, _b); sb("mf", C, _b); sb("mn", 3 * C, _b)
+    sb("bp2", 8, _f); sb("bpn", 8, _f)
+    sb("i1", 18, _i); sb("i2", 18, _i); sb("i3", 18, _i); sb("cl", 18, _f); sb("ui", 16, _i); sb("uo", 16, _u)
+    sb("pt", 1536, _f)
+    sb("c1", 54, _f); sb("c2", 54, _f)
+    for r in range(2):
+        sb("new%d" % r, 54, _i); sb("off%d" % r, 54, _u)
+    sb("al", 18, _f); sb("tl", 18, _f); sb("tm", 18, _f); sb("dp", 18, _f); sb("do", 18, _u)
+    sb("qe", 36, _f); sb("ie", 36, _f); sb("ieo", 36, _u)
+    sb("pi", 1536, _f); sb("thr", C, _b); sb("nr", 3 * C, _f); sb("ns", 3 * C, _f); sb("er", 2 * C, _f); sb("es", 2 * C, _f)
+    sb("df", 54, _f); sb("dg", 54, _f); sb("base", 54, _f); sb("dl", 54, _f); sb("bd", 54, _f); sb("base2", 54, _f)
+    sb("a2", 2 * C, _b); sb("am", C, _b); sb("fr", C, _b); sb("fs", C, _b)
+    sb("st", 54, _f); sb("sel", 54, _i); sb("xi", 54, _i); sb("xo", 54, _u)
+    sb("n0", 54, _i); sb("n1", 54, _i); sb("dn", 54, _f); sb("bb", 54, _f); sb("b2", 54, _f)
+    sb("fx", 3 * C, _b); sb("fxs", 3 * C, _b); sb("nt", 54, _f)
+    sb("zn", 54, _i); sb("dz", 54, _f); sb("bz", 54, _f); sb("zf", 54, _f)
+    sb("zt", 1536, _f); sb("mr", C, _f); sb("ms", C, _f); sb("mo", 18, _u)
+    for r in range(4):
+        sb("x%d" % r, 4 * C, _b)
+    sb("qx", C, _q); sb("sx", C, _s); sb("qz", C, _q); sb("sz", C, _s)
+    sb("xh", 4 * C, _b); sb("zp", 4 * C, _b); sb("z", 4 * C, _b); sb("h", 4 * C, _b); sb("d", 4 * C, _b)
+    for r in range(3):
+        sb("za%d" % r, 36, _u); sb("zb%d" % r, 18, _u); sb("la%d" % r, 36, _u); sb("lb%d" % r, 18, _u)
+        sb("qh%d" % r, C, _q); sb("sh%d" % r, C, _s); sb("lq%d" % r, C, _q); sb("ls%d" % r, C, _s)
+    sb("yt", C, _f); sb("owt", 3 * C, _f)
+    d["ps"] = ("psum", [128, 4096], _f)
+    return d
+
+
+SCRATCH = _scratch()
+_DMAS = ["x", "u", "v", "w", "wc", "ws", "y0", "y1", "ow", "oc", "os0", "os1", "os2", "os3"]
+SEMAPHORES = (["qv", "qs", "qt", "qg", "loc"] + ["d" + n for n in _DMAS] +
+              ["r%s%d" % (n, r) for n in ("a", "b", "q0", "q1", "s") for r in range(3)])
+
+
+def rank_program(g, core, T, topo):
+    rank = T.rank_of(core)
+    if rank is None:
+        return
+    queue = {"v": g.vector, "s": g.scalar, "t": g.tensor, "g": g, "y": g.sync}
+    count = {"v": 0, "s": 0, "t": 0, "g": 0}
+    known = {q: {} for q in queue}
+    snap, wrote, read, total, waited = {}, {}, {}, {}, {}
+
+    def before(q, rd, wr):
+        own = "q" + q
+        deps = set(wrote[k] for k in rd if k in wrote)
+        for k in wr:
+            deps |= set(w for w in [wrote.get(k)] + read.get(k, []) if w and w[0] != own)
+        best = {}
+        for s, n in deps:
+            if n > known[q].get(s, 0):
+                best[s] = max(n, best.get(s, 0))
+        for s, n in sorted(best.items()):
+            if any(o != s and snap.get((o, m), {}).get(s, 0) >= n for o, m in best.items()):
+                continue
+            queue[q].wait_ge(T.sem[s], n)
+            waited[s] = max(n, waited.get(s, 0))
+            known[q][s] = n
+            for o, m in snap.get((s, n), {}).items():
+                known[q][o] = max(m, known[q].get(o, 0))
+
+    def after(q, tag, rd, wr):
+        snap[tag] = dict(known[q])
+        total[tag[0]] = max(total.get(tag[0], 0), tag[1])
+        for k in rd:
+            read.setdefault(k, []).append(tag)
+        for k in wr:
+            wrote[k] = tag
+            read[k] = []
+
+    def op(q, fn, rd, wr):
+        before(q, rd, wr)
+        count[q] += 1
+        fn(queue[q]).then_inc(T.sem["q" + q], 1)
+        after(q, ("q" + q, count[q]), rd, wr)
+
+    def dma(q, name, out, in_, rd, wr):
+        before(q, rd, wr)
+        queue[q].dma_start(out, in_).then_inc(T.sem["d" + name], 16)
+        after(q, ("d" + name, 16), rd, wr)
+
+    def tt(out, a, b, o, rd, wr):
+        op("v", lambda e: e.tensor_tensor(out, a, b, o), rd, wr)
+
+    def ts(out, a, s1, o1, rd, wr, s2=None, o2=None):
+        if o2 is None:
+            op("v", lambda e: e.tensor_scalar(out, a, s1, None, o1), rd, wr)
+        else:
+            op("v", lambda e: e.tensor_scalar(out, a, s1, s2, o1, o2), rd, wr)
+
+    def cp(out, a, rd, wr):
+        op("v", lambda e: e.tensor_copy(out, a), rd, wr)
+
+    def fill(out, c, wr):
+        op("v", lambda e: e.memset(out, c), [], wr)
+
+    def ac(out, a, rd, wr, scale=1.0, bias=0.0, func=F.Copy):
+        op("s", lambda e: e.activation(out, a, func, bias=bias, scale=scale), rd, wr)
+
+    def scan(out, mask, v, rd, wr):
+        op("v", lambda e: e.tensor_tensor_scan(out, mask, v, 0.0, A.add, A.max), rd, wr)
+
+    def quant(q, s, x, rd, wr):
+        op("v", lambda e: e.quantize_mx(q, s, x), rd, wr)
+
+    def mm(bank, n, w, ws, x, xs, rd):
+        op("t", lambda e: e.matmul_mx(T.ps[:, 512 * bank:512 * bank + n], w, ws, x, xs, True, True), rd, ["b%d" % bank])
+
+    def bank(b, n=C):
+        return T.ps[:, 512 * b:512 * b + n]
+
+    def k18(k):
+        return slice(18 * k, 18 * k + 18)
+
+    def kc(k):
+        return slice(C * k, C * k + C)
+
+    dma("s", "w", T.wi[:], T.wl[:], [], ["wi"])
+    dma("y", "x", T.x0[:], T.x[:], [], ["x0.%d" % b for b in range(4)])
+    dma("s", "u", T.ut[:], T.u[:], [], ["ut"])
+    dma("y", "wc", T.wq[:, 0:512].bitcast(dt.uint8), T.wc[:, 0:2048], [], ["wq"])
+    dma("y", "ws", T.wsc[:, 0:512], T.ws[:, 0:512], [], ["wsc"])
+    dma("y", "v", T.vt[:], T.v[:], [], ["vt"])
+
+    def iota(out, pattern, base, cm, wr, small=False):
+        if small:
+            op("g", lambda e: e.iota(out, pattern, base, cm, allow_small_or_imprecise_dtypes=True), [], wr)
+        else:
+            op("g", lambda e: e.iota(out, pattern, base, cm), [], wr)
+    iota(T.ei[:], [[1, 16]], 128, -1, ["ei"])
+    iota(T.cr[:], [[1, C]], 0, 0, ["cr"], True)
+    iota(T.i1[:], [[0, 18]], 0, 1, ["i1"])
+    iota(T.i2[:], [[16, 18]], C, 0, ["i2"])
+    iota(T.ui[:], [[1, 2], [16, 8]], 0, 0, ["ui"])
+    iota(T.ones[:], [[0, 512]], 1, 0, ["ones"], True)
+    for b in range(4):
+        op("g", lambda e: e.affine_select(T.et[:, 512 * b:512 * b + 512], T.ones[:], [[-1, 512]], A.is_equal, 0.0, b, 4),
+           ["ones"], ["et%d" % b])
+    fill(T.t3[:, 0:C], 0.0, ["t3a"])
+    fill(T.t3[:, C:2 * C], HUGE, ["t3b"])
+    ts(T.ea[:], T.ei[:], 15, A.bitwise_and, ["ei"], ["ea"])
+    ts(T.e0[:], T.ea[:], 0.0, A.is_equal, ["ea"], ["e0"], -4.0, A.mult)
+    ts(T.e1[:], T.ea[:], 1.0, A.is_equal, ["ea"], ["e1"], 2.0, A.mult)
+    ts(T.bp2[:, 0:1], T.ea[:, 15:16], 0.0, A.not_equal, ["ea"], ["bp2"], 2.0, A.mult)
+    ts(T.bpn[:, 0:1], T.ea[:, 15:16], 0.0, A.not_equal, ["ea"], ["bpn"], 2.0 * BIG, A.mult)
+    tt(T.mf[:, 0:16], T.e0[:], T.e1[:], A.add, ["e0", "e1"], ["mf"])
+    for n in (16, 32, 64, 128, 256):
+        m = min(n, C - n)
+        cp(T.mf[:, n:n + m], T.mf[:, 0:m], ["mf"], ["mf"])
+    for k in range(3):
+        ts(T.mn[:, kc(k)], T.mf[:], BIG, A.mult, ["mf"], ["mn"])
+    ts(T.i3[:], T.i1[:], 15, A.bitwise_and, ["i1"], ["i3"])
+    cp(T.uo[:], T.ui[:], ["ui"], ["uo"])
+    tt(T.cl[:], T.i3[:], T.i2[:], A.add, ["i3", "i2"], ["cl"])
+    bp2, bpn = T.bp2[:, 0:1], T.bpn[:, 0:1]
+    ac(T.t0[:, 0:C], T.cr[:], ["cr"], ["t0a"], 0.0, 512.0)
+    ac(T.t0[:, C:], T.cr[:], ["cr"], ["t0b"], 0.0, 2048.0 * 512)
+    ac(T.cr0[:], T.cr[:], ["cr"], ["cr0"], 2049.0)
+    ac(T.t1[:, 0:C], T.cr[:], ["cr"], ["t1a"], 2048.0, 1024.0 + 2048 * 512)
+    ac(T.t1[:, C:], T.cr[:], ["cr"], ["t1b"], 2048.0, 512.0)
+    ac(T.t2[:, 0:C], T.cr[:], ["cr"], ["t2a"], 2048.0, 2048.0 * 1024)
+    ac(T.t2[:, C:], T.cr[:], ["cr"], ["t2b"], 2048.0, 1024.0 + 2048 * 1024)
+    for k in range(2):
+        ac(T.pi[:, 512 * k + C:512 * k + 512], T.cr[:, 0:224], ["cr"], ["pig%d" % k])
+    for k in range(2):
+        ac(T.zt[:, 512 * k + C:512 * k + 512], T.cr[:, 0:224], ["cr"], ["ztg%d" % k])
+
+    ts(T.c1[:], T.wi[:], float(C), A.is_ge, ["wi"], ["c1"], 224.0, A.mult)
+    ts(T.c2[:], T.wi[:], 2.0 * C, A.is_ge, ["wi"], ["c2"], 224.0, A.mult)
+    tt(T.c1[:], T.c1[:], T.wi[:], A.add, ["c1", "wi"], ["c3"])
+    tt(T.new0[:], T.c1[:], T.c2[:], A.add, ["c3", "c2"], ["new0"])
+
+    def lists(r):
+        w0 = T["new%d" % (r % 2)][:, 0:18]
+        w = "new%d" % (r % 2)
+        tt(T.tl[:], w0, T.cl[:], A.subtract, [w, "cl"], ["tl"])
+        ts(T.al[:], w0, 512.0, A.is_lt, [w], ["al"])
+        tt(T.tm[:], T.tl[:], T.al[:], A.mult, ["tl", "al"], ["tm"])
+        ts(T.qe[:, 0:18], T.al[:], 576.0, A.mult, ["al"], ["qe0"], -288.0, A.add)
+        tt(T.dp[:], T.tm[:], T.cl[:], A.add, ["tm", "cl"], ["dp"])
+        ts(T.qe[:, 18:36], T.al[:], 288.0, A.mult, ["al"], ["qe1"], 288.0, A.add)
+        cp(T.do[:], T.dp[:], ["dp"], ["do"])
+
+    def lists2():
+        tt(T.ie[:, 0:18], T.qe[:, 0:18], T.dp[:], A.add, ["qe0", "dp"], ["ie0"])
+        tt(T.ie[:, 18:36], T.qe[:, 18:36], T.dp[:], A.add, ["qe1", "dp"], ["ie1"])
+        cp(T.ieo[:], T.ie[:], ["ie0", "ie1"], ["ieo"])
+
+    def pis():
+        for k in range(3):
+            row = T.cr0 if k == 0 else T.cr
+            t = T["t%d" % k]
+            tt(T.pi[:, 512 * k:512 * k + C], t[:, 0:2 * C].indirect(T.do[:, 0:18]), row[:], A.add,
+               ["do", "t%da" % k, "t%db" % k, "cr0" if k == 0 else "cr"], ["pi%d" % k])
+
+    def thr():
+        ac(T.thr[:], T.t3[:, 0:2 * C].indirect(T.do[:, 0:18]), ["do", "t3a", "t3b"], ["thr"])
+
+    def nrow(r):
+        o = "off%d" % (r % 2)
+        rd = ["pi0", "pi1", "pi2", "pig0", "pig1", o]
+        ac(T.nr[:, 0:2 * C], T.pi[:, 0:1024 + C].indirect(T[o][:, 0:36]), rd, ["nr0"])
+        cp(T.nr[:, 2 * C:3 * C], T.pi[:, 0:1024 + C].indirect(T[o][:, 36:54]), rd, ["nr1"])
+
+    def erow():
+        ac(T.er[:], T.nr[:, 0:3 * C].indirect(T.ieo[:, 0:36]), ["nr0", "nr1", "ieo"], ["er"])
+
+    def prep1():
+        ns = T.ns
+        scan(T.ns[:], T.mn[:], T.nr[:], ["mn", "nr0", "nr1"], ["ns"])
+        tt(T.df[:, 18:54], ns[:, 15:576:16], ns[:, 303:864:16], A.subtract, ["ns"], ["df1"])
+        tt(T.df[:, 0:18], ns[:, 591:864:16], ns[:, 15:288:16], A.subtract, ["ns"], ["df0"])
+        for k in (1, 2, 0):
+            tt(T.dg[:, k18(k)], T.df[:, k18(k)], T.al[:], A.mult, ["df0" if k == 0 else "df1", "al"], ["dg%d" % k])
+
+    def base():
+        tt(T.base[:], T.dg[:], T.ns[:, 15:864:16], A.add, ["dg0", "dg1", "dg2", "ns"], ["base"])
+
+    def halves(r):
+        for b in range(4):
+            ac(T.xh[:, kc(b)], T["x%d" % r][:, b:4 * C:4], ["x%d.%d" % (r, b)], ["xh%d" % b], 0.5)
+
+    def qstate(r):
+        quant(T.qx[:, 0:C], T.sx[:, 0:C], T["x%d" % r][:, 0:4 * C], ["x%d.%d" % (r, b) for b in range(4)], ["qx"])
+
+    def scores():
+        for k in (1, 0):
+            mm(k, C, T.u2[:, 128 * k:128 * k + 128], T.u2s[:, 128 * k:128 * k + 128], T.qx[:, 0:C], T.sx[:, 0:C],
+               ["u2", "u2s", "qx"])
+
+    lists(0)
+    cp(T.off0[:], T.new0[:], ["new0"], ["off0"])
+    lists2()
+    thr()
+    quant(T.uq[:, 0:128], T.us[:, 0:128], T.ut[:, 0:512], ["ut"], ["uq"])
+    op("s", lambda e: e.activation(T.u2s[:, 0:256], T.us[:, 0:128].indirect(T.uo[:, 0:16]), F.Copy), ["uq", "uo"], ["u2s"])
+    pis()
+    nrow(0)
+    op("v", lambda e: e.tensor_copy(T.u2[:, 0:256].bitcast(dt.uint32), T.uq[:, 0:128].bitcast(dt.uint32).indirect(T.uo[:, 0:16])),
+       ["uq", "uo"], ["u2"])
+    qstate(0)
+    scores()
+    erow()
+    prep1()
+    base()
+
+    for r in range(3):
+        peer = T.cores[rank ^ STEP[r]]
+        rid, pid = topo.addr(peer, core)
+        mask = topo.mask(core, peer)
+        arrive = len(topo.engines(peer, core))
+        last = r == 2
+
+        def send(dst, src, sem, rd):
+            before("g", rd, [])
+            g.remote_dma(out_ap=dst, in_ap=src, remote_sem=T.sem[sem], local_sem=T.sem.loc, pid=pid, routing_id=rid,
+                         dma_engine_mask=mask)
+            total["loc"] = total.get("loc", 0) + len(topo.engines(core, peer))
+
+        def arrival(sem, key):
+            wrote[key] = (sem, arrive)
+            snap[(sem, arrive)] = {}
+            total[sem] = arrive
+        arrival("ra%d" % r, "la")
+        arrival("rb%d" % r, "lb")
+        for i in range(2):
+            arrival("rq%d%d" % (i, r), "lq%d" % i)
+        arrival("rs%d" % r, "ls")
+        n = (r + 1) % 2
+        new, off, za, zb = T["new%d" % n], T["off%d" % n], T["za%d" % r], T["zb%d" % r]
+        lq, ls, qh, sh = T["lq%d" % r], T["ls%d" % r], T["qh%d" % r], T["sh%d" % r]
+
+        ac(T.a2[:, C:2 * C], bank(1), ["b1"], ["a2b"], func=F.Relu)
+        halves(r)
+        scan(T.es[:], T.mn[:, 0:2 * C], T.er[:], ["mn", "er"], ["es"])
+        tt(T.am[:], bank(0), T.thr[:], A.is_gt, ["b0", "thr"], ["am"])
+        tt(T.dl[:, 18:54], T.es[:, 15:576:16], T.base[:, 18:54], A.subtract, ["es", "base"], ["dl1"])
+        tt(T.dl[:, 0:18], T.base[:, 18:36], T.base[:, 0:18], A.subtract, ["base"], ["dl0"])
+        cp(T.a2[:, 0:C], T.am[:], ["am"], ["a2a"])
+        ts(T.bd[:], T.dl[:], bp2, A.mult, ["dl0", "dl1", "bp2", "bpn"], ["bd"], bpn, A.add)
+        tt(T.base2[:], T.base[:], T.bd[:], A.subtract, ["base", "bd"], ["base2"])
+        tt(T.fr[:], T.a2[:, 0:2 * C].indirect(T.do[:, 0:18]), T.am[:], A.not_equal, ["a2a", "a2b", "am", "do"], ["fr"])
+        scan(T.fs[:], T.mf[:], T.fr[:], ["mf", "fr"], ["fs"])
+
+        for k in (1, 2, 0):
+            tt(T.st[:, k18(k)], T.fs[:, 15:C:16], T.dl[:, k18(k)], A.mult, ["fs", "dl0", "dl1"], ["st%d" % k])
+        tt(T.sel[:], T.st[:], T.base2[:], A.add, ["st0", "st1", "st2", "base2"], ["sel"])
+        ts(T.xi[:], T.sel[:], 511, A.bitwise_and, ["sel"], ["xi"])
+        cp(T.xo[:], T.xi[:], ["xi"], ["xo"])
+        for k in (1, 2, 0):
+            ac(T.fx[:, kc(k)], T.fr[:, 0:C].indirect(T.xo[:, k18(k)]), ["fr", "xo"], ["fx%d" % k])
+        ts(T.zn[:], T.sel[:], 11, A.logical_shift_right, ["sel"], ["zn"], 511, A.bitwise_and)
+        tt(T.dz[:], T.zn[:], T.xi[:], A.subtract, ["zn", "xi"], ["dz"])
+        ts(T.bb[:], T.dz[:], bp2, A.mult, ["dz", "bp2"], ["bb"])
+        tt(T.bz[:], T.xi[:], T.bb[:], A.subtract, ["xi", "bb"], ["bz"])
+
+        def fscan(k):
+            scan(T.fxs[:, kc(k)], T.mf[:], T.fx[:, kc(k)], ["mf", "fx%d" % k], ["fxs%d" % k])
+
+        def zmul(k):
+            tt(T.zf[:, k18(k)], T.fxs[:, C * k + 15:C * k + C:16], T.dz[:, k18(k)], A.mult, ["fxs%d" % k, "dz"], ["zm%d" % k])
+
+        def zadd(k):
+            tt(T.zf[:, k18(k)], T.zf[:, k18(k)], T.bz[:, k18(k)], A.add, ["zm%d" % k, "bz"], ["zf%d" % k])
+
+        def zout(k):
+            cp(zb[:] if k == 0 else za[:, k18(k - 1)], T.zf[:, k18(k)], ["zf%d" % k], ["zo%d" % k])
+        fscan(1)
+        zmul(1)
+        fscan(2)
+        zadd(1)
+        zmul(2)
+        zout(1)
+        zadd(2)
+        zout(2)
+        send(T["la%d" % r][:], za[:], "ra%d" % r, ["zo1", "zo2"])
+
+        def hquant(i):
+            a, e = CUT[i]
+            quant(qh[:, a:e], sh[:, a:e], T.h[:, 4 * a:4 * e], ["h%d%d" % (i, b) for b in range(4)], ["qh%d" % i])
+            send(lq[:, a:e].bitcast(dt.uint8), qh[:, a:e].bitcast(dt.uint8), "rq%d%d" % (i, r), ["qh%d" % i])
+            if i == 1:
+                send(ls[:, 0:C], sh[:, 0:C], "rs%d" % r, ["qh0", "qh1"])
+        for i, (a, e) in enumerate(CUT):
+            for b in range(4):
+                ac(T.zp[:, C * b + a:C * b + e], T.xh[:, kc(b)].indirect(za[:, a // 16:e // 16]),
+                   ["xh%d" % b, "zo1"], ["zp%d%d" % (i, b)])
+                tt(T.z[:, 4 * a + b:4 * e:4], T.xh[:, kc(b)].indirect(za[:, 18 + a // 16:18 + e // 16]),
+                   T.zp[:, C * b + a:C * b + e], A.add, ["xh%d" % b, "zo2", "zp%d%d" % (i, b)], ["z%d" % i])
+            quant(T.qz[:, a:e], T.sz[:, a:e], T.z[:, 4 * a:4 * e], ["z%d" % i], ["qz%d" % i])
+        for i, (a, e) in enumerate(CUT):
+            for b in range(4):
+                k = (2 + 4 * i + b) % 8
+                mm(k, e - a, T.wq[:, 128 * b:128 * b + 128], T.wsc[:, 128 * b:128 * b + 128], T.qz[:, a:e], T.sz[:, a:e],
+                   ["wq", "wsc", "qz%d" % i])
+                ac(T.h[:, 4 * a + b:4 * e:4], bank(k, e - a), ["b%d" % k], ["h%d%d" % (i, b)], 0.03125)
+        fscan(0)
+        ts(T.n0[:], T.sel[:], 2047, A.bitwise_and, ["sel"], ["n0"])
+        ts(T.n1[:], T.sel[:], 11, A.logical_shift_right, ["sel"], ["n1"])
+        zmul(0)
+        tt(T.dn[:], T.n1[:], T.n0[:], A.subtract, ["n1", "n0"], ["dn"])
+        hquant(0)
+        zadd(0)
+        ts(T.bb[:], T.dn[:], bp2, A.mult, ["dn", "bp2"], ["bb"])
+        tt(T.nt[:], T.fxs[:, 15:3 * C:16], T.dn[:], A.mult, ["fxs0", "fxs1", "fxs2", "dn"], ["nt"])
+        zout(0)
+        send(T["lb%d" % r][:], zb[:], "rb%d" % r, ["zo0"])
+        tt(T.b2[:], T.n0[:], T.bb[:], A.subtract, ["n0", "bb"], ["b2"])
+        hquant(1)
+        tt(new[:], T.nt[:], T.b2[:], A.add, ["nt", "b2"], ["new%d" % n])
+        cp(off[:], new[:], ["new%d" % n], ["off%d" % n])
+
+        if r == 0:
+            iota(T.pt[:], [[C, 3], [1, 512]], 0, 0, ["pt"], True)
+        if not last:
+            lists(r + 1)
+            pis()
+            lists2()
+            thr()
+        for k in (1, 2):
+            ac(T.zt[:, 512 * k:512 * k + C], T.cr[:, 0:C].indirect(T["la%d" % r][:, k18(k - 1)]), ["cr", "la"], ["zt%d" % k])
+        if r == 0:
+            quant(T.eq[:, 0:512], T.esc[:, 0:512], T.et[:, 0:2048], ["et%d" % b for b in range(4)], ["eq"])
+        if last:
+            quant(T.vq[:, 0:128], T.vs[:, 0:128], T.vt[:, 0:512], ["vt"], ["vq"])
+        if not last:
+            nrow(r + 1)
+        ac(T.zt[:, 0:C], T.cr[:, 0:C].indirect(T["lb%d" % r][:, 0:18]), ["cr", "lb"], ["zt0"])
+        ac(T.mr[:], T.zt[:, 0:1024 + C].indirect(off[:, 0:18]), ["zt0", "zt1", "zt2", "ztg0", "ztg1", "off%d" % n], ["mr"])
+        if not last:
+            prep1()
+        scan(T.ms[:], T.mn[:, 0:C], T.mr[:], ["mn", "mr"], ["ms"])
+        if not last:
+            base()
+        ts(T.mo[:], T.ms[:, 15:C:16], bpn, A.subtract, ["ms", "bpn"], ["mo"])
+        if last:
+            ac(T.owt[:], T.pt[:, 0:1024 + C].indirect(off[:, 0:54]), ["pt", "off%d" % n], ["owt"])
+            dma("y", "ow", T.ow[:], T.owt[0:128:16, :], ["owt"], [])
+
+        x, y = "x%d" % r, "x%d" % (r + 1)
+        for b in range(4):
+            k = 2 + b
+            mm(k, C, T.eq[:, 128 * b:128 * b + 128], T.esc[:, 128 * b:128 * b + 128], lq[:, 0:C], ls[:, 0:C],
+               ["eq", "lq0", "lq1", "ls"])
+            ac(T.d[:, kc(b)], bank(k), ["b%d" % k], ["d%d" % b])
+        if not last:
+            erow()
+        for b in range(4):
+            tt(T[y][:, b:4 * C:4], T.d[:, kc(b)].indirect(T.mo[:, 0:18]), T[x][:, b:4 * C:4], A.add,
+               ["d%d" % b, "mo", "%s.%d" % (x, b)], ["%s.%d" % (y, b)])
+        qstate(r + 1)
+        if not last:
+            scores()
+
+    h = C // 2
+    for i in range(2):
+        mm(2 + i, h, T.vq[:, 0:128], T.vs[:, 0:128], T.qx[:, h * i:h * i + h], T.sx[:, h * i:h * i + h], ["vq", "qx"])
+    dma("y", "oc", T.oc[:, 0:4 * C], T.qx[:, 0:C].bitcast(dt.uint8), ["qx"], [])
+    for k in range(4):
+        dma("y", "os%d" % k, T.osc[4 * k:4 * k + 4, 0:C], T.sx[32 * k:32 * k + 4, 0:C], ["qx"], [])
+    cp(T.yt[:, h:C], bank(3, h), ["b3"], ["yt1"])
+    ac(T.yt[:, 0:h], bank(2, h), ["b2"], ["yt0"])
+    dma("s", "y0", T.y[:, 0:h], T.yt[:, 0:h], ["yt0"], [])
+    dma("s", "y1", T.y[:, h:C], T.yt[:, h:C], ["yt1"], [])
+    for s, m in sorted(total.items()):
+        if waited.get(s, 0) < m:
+            g.wait_ge(T.sem[s], m)

@@ -3,8 +3,9 @@ from concourse.mybir import dt, AluOpType as A, ActivationFunctionType as F
 C = 288
 STEP = [4, 1, 2]
 HUGE = 1e29
-BIG = 2097152.0
+B = 1024.0
 CUT = [(0, 160), (160, 288)]
+OPT = {"one": 1, "s2": 1}
 
 _f, _b, _i, _u = "float32", "bfloat16", "int32", "uint16"
 _q, _s = "float8_e4m3fn_x4", "uint8"
@@ -19,31 +20,27 @@ def _scratch():
     sb("wq", 512, _q); sb("wsc", 512, _s)
     sb("uq", 128, _q); sb("us", 128, _s); sb("u2", 256, _q); sb("u2s", 256, _s)
     sb("vq", 128, _q); sb("vs", 128, _s)
-    sb("ones", 512, _b); sb("et", 2048, _b); sb("eq", 512, _q); sb("esc", 512, _s)
-    sb("cr", C, _f); sb("cr0", C, _f); sb("t0", 2 * C, _f); sb("t1", 2 * C, _f); sb("t2", 2 * C, _f); sb("t3", 2 * C, _b)
-    sb("ei", 16, _i); sb("ea", 16, _i); sb("e0", 16, _b); sb("e1", 16, _b); sb("mf", C, _b); sb("mn", 3 * C, _b)
-    sb("bp2", 8, _f); sb("bpn", 8, _f)
-    sb("i1", 18, _i); sb("i2", 18, _i); sb("i3", 18, _i); sb("cl", 18, _f); sb("ui", 16, _i); sb("uo", 16, _u)
-    sb("pt", 1536, _f)
-    sb("c1", 54, _f); sb("c2", 54, _f)
-    for r in range(2):
-        sb("new%d" % r, 54, _i); sb("off%d" % r, 54, _u)
-    sb("al", 18, _f); sb("tl", 18, _f); sb("tm", 18, _f); sb("dp", 18, _f); sb("do", 18, _u)
-    sb("qe", 36, _f); sb("ie", 36, _f); sb("ieo", 36, _u)
-    sb("pi", 1536, _f); sb("thr", C, _b); sb("nr", 3 * C, _f); sb("ns", 3 * C, _f); sb("er", 2 * C, _f); sb("es", 2 * C, _f)
-    sb("df", 54, _f); sb("dg", 54, _f); sb("base", 54, _f); sb("dl", 54, _f); sb("bd", 54, _f); sb("base2", 54, _f)
-    sb("a2", 2 * C, _b); sb("am", C, _b); sb("fr", C, _b); sb("fs", C, _b)
-    sb("st", 54, _f); sb("sel", 54, _i); sb("xi", 54, _i); sb("xo", 54, _u)
-    sb("n0", 54, _i); sb("n1", 54, _i); sb("dn", 54, _f); sb("bb", 54, _f); sb("b2", 54, _f)
-    sb("fx", 3 * C, _b); sb("fxs", 3 * C, _b); sb("nt", 54, _f)
-    sb("zn", 54, _i); sb("dz", 54, _f); sb("bz", 54, _f); sb("zf", 54, _f)
-    sb("zt", 1536, _f); sb("mr", C, _f); sb("ms", C, _f); sb("mo", 18, _u)
+    sb("ones", 2048, _b); sb("et", 2048, _b); sb("eq", 512, _q); sb("esc", 512, _s)
+    sb("idn", 3 * C, _f); sb("unp", 3 * C, _f); sb("t3", 3 * C, _b)
+    sb("ei", 16, _i); sb("ea", 16, _i); sb("e0", 16, _b); sb("e1", 16, _b); sb("m16", 16, _b)
+    sb("mf", C, _b); sb("mn", 2 * C, _b)
+    sb("i1", 36, _i); sb("i2", 18, _i); sb("i3", 36, _i); sb("i4", 18, _f); sb("io16", 36, _u)
+    sb("c3", 18, _f); sb("c3m", 18, _f); sb("c31", 18, _f); sb("ui", 16, _i); sb("uo", 16, _u)
+    sb("k1", 54, _f); sb("k2", 54, _f); sb("w3", 54, _f); sb("p0", 54, _f); sb("zi", 18, _u); sb("off", 54, _u)
+    for n in ("e3", "act", "w0c", "tt", "qq", "a2x"):
+        sb(n, 18, _f)
+    for n in ("ap", "dp", "df", "dg", "bc", "dc", "sp", "sc", "pl", "cl"):
+        sb(n, 54, _f)
+    sb("eo", 36, _u); sb("po", 54, _u); sb("co", 54, _u)
+    sb("thr", C, _b); sb("a2", 3 * C, _b); sb("am", C, _b); sb("fr", C, _b); sb("fs", C, _b)
+    sb("tab", 3 * C, _f); sb("gw", 3 * C, _f); sb("gs", 3 * C, _f); sb("er", 2 * C, _f); sb("es", 2 * C, _f)
+    sb("zt", 3 * C, _f); sb("mr", C, _f); sb("ms", C, _f); sb("mo", 18, _u)
     for r in range(4):
         sb("x%d" % r, 4 * C, _b)
     sb("qx", C, _q); sb("sx", C, _s); sb("qz", C, _q); sb("sz", C, _s)
     sb("xh", 4 * C, _b); sb("zp", 4 * C, _b); sb("z", 4 * C, _b); sb("h", 4 * C, _b); sb("d", 4 * C, _b)
     for r in range(3):
-        sb("za%d" % r, 36, _u); sb("zb%d" % r, 18, _u); sb("la%d" % r, 36, _u); sb("lb%d" % r, 18, _u)
+        sb("zl%d" % r, 54, _u); sb("la%d" % r, 54, _u); sb("lb%d" % r, 18, _u)
         sb("qh%d" % r, C, _q); sb("sh%d" % r, C, _s); sb("lq%d" % r, C, _q); sb("ls%d" % r, C, _s)
     sb("yt", C, _f); sb("owt", 3 * C, _f)
     d["ps"] = ("psum", [128, 4096], _f)
@@ -51,9 +48,9 @@ def _scratch():
 
 
 SCRATCH = _scratch()
-_DMAS = ["x", "u", "v", "w", "wc", "ws", "y0", "y1", "ow", "oc", "os0", "os1", "os2", "os3"]
+_DMAS = ["x", "u", "v", "w", "wc", "ws", "y0", "y1", "ow", "oc0", "oc1", "os0", "os1", "os2", "os3"]
 SEMAPHORES = (["qv", "qs", "qt", "qg", "loc"] + ["d" + n for n in _DMAS] +
-              ["r%s%d" % (n, r) for n in ("a", "b", "q0", "q1", "s") for r in range(3)])
+              ["r%s%d" % (n, r) for n in ("a", "b", "q0", "q1", "s0", "s1") for r in range(3)])
 
 
 def rank_program(g, core, T, topo):
@@ -66,10 +63,9 @@ def rank_program(g, core, T, topo):
     snap, wrote, read, total, waited = {}, {}, {}, {}, {}
 
     def before(q, rd, wr):
-        own = "q" + q
         deps = set(wrote[k] for k in rd if k in wrote)
         for k in wr:
-            deps |= set(w for w in [wrote.get(k)] + read.get(k, []) if w and w[0] != own)
+            deps |= set(w for w in [wrote.get(k)] + read.get(k, []) if w)
         best = {}
         for s, n in deps:
             if n > known[q].get(s, 0):
@@ -122,7 +118,7 @@ def rank_program(g, core, T, topo):
         op("s", lambda e: e.activation(out, a, func, bias=bias, scale=scale), rd, wr)
 
     def scan(out, mask, v, rd, wr):
-        op("v", lambda e: e.tensor_tensor_scan(out, mask, v, 0.0, A.add, A.max), rd, wr)
+        op("v", lambda e: e.tensor_tensor_scan(out, v, mask, 0.0, A.max, A.add), rd, wr)
 
     def quant(q, s, x, rd, wr):
         op("v", lambda e: e.quantize_mx(q, s, x), rd, wr)
@@ -139,10 +135,19 @@ def rank_program(g, core, T, topo):
     def kc(k):
         return slice(C * k, C * k + C)
 
+    def k3(k, a=0, e=C):
+        return slice(3 * a + k, 3 * e, 3)
+
+    def keys(name, *ks):
+        return ["%s%s" % (name, k) for k in ks]
+
+    def xkeys(r, i):
+        return ["x%d.%d%d" % (r, i, b) for b in range(4)]
+
     dma("s", "w", T.wi[:], T.wl[:], [], ["wi"])
-    dma("y", "x", T.x0[:], T.x[:], [], ["x0.%d" % b for b in range(4)])
-    dma("s", "u", T.ut[:], T.u[:], [], ["ut"])
-    dma("y", "wc", T.wq[:, 0:512].bitcast(dt.uint8), T.wc[:, 0:2048], [], ["wq"])
+    dma("y", "u", T.ut[:], T.u[:], [], ["ut"])
+    dma("y", "x", T.x0[:], T.x[:], [], xkeys(0, 0) + xkeys(0, 1))
+    dma("y", "wc", T.wq[:, 0:512].bitcast(dt.uint8), T.wc[:, 0:2048], ["ut"], ["wq"])
     dma("y", "ws", T.wsc[:, 0:512], T.ws[:, 0:512], [], ["wsc"])
     dma("y", "v", T.vt[:], T.v[:], [], ["vt"])
 
@@ -152,121 +157,128 @@ def rank_program(g, core, T, topo):
         else:
             op("g", lambda e: e.iota(out, pattern, base, cm), [], wr)
     iota(T.ei[:], [[1, 16]], 128, -1, ["ei"])
-    iota(T.cr[:], [[1, C]], 0, 0, ["cr"], True)
-    iota(T.i1[:], [[0, 18]], 0, 1, ["i1"])
-    iota(T.i2[:], [[16, 18]], C, 0, ["i2"])
+    iota(T.i1[:], [[0, 36]], 0, 1, ["i1"])
+    iota(T.idn[:], [[1, 3 * C]], 0, 0, ["idn"], True)
+    iota(T.i2[:], [[48, 18]], 0, 0, ["i2"])
     iota(T.ui[:], [[1, 2], [16, 8]], 0, 0, ["ui"])
-    iota(T.ones[:], [[0, 512]], 1, 0, ["ones"], True)
-    for b in range(4):
-        op("g", lambda e: e.affine_select(T.et[:, 512 * b:512 * b + 512], T.ones[:], [[-1, 512]], A.is_equal, 0.0, b, 4),
-           ["ones"], ["et%d" % b])
-    fill(T.t3[:, 0:C], 0.0, ["t3a"])
-    fill(T.t3[:, C:2 * C], HUGE, ["t3b"])
+    fill(T.ones[:], 1.0, ["ones"])
+    op("g", lambda e: e.affine_select(T.et[:], T.ones[:], [[1, 4], [-1, 512]], A.is_equal, 0.0, 0, 4), ["ones"], ["et"])
     ts(T.ea[:], T.ei[:], 15, A.bitwise_and, ["ei"], ["ea"])
-    ts(T.e0[:], T.ea[:], 0.0, A.is_equal, ["ea"], ["e0"], -4.0, A.mult)
-    ts(T.e1[:], T.ea[:], 1.0, A.is_equal, ["ea"], ["e1"], 2.0, A.mult)
-    ts(T.bp2[:, 0:1], T.ea[:, 15:16], 0.0, A.not_equal, ["ea"], ["bp2"], 2.0, A.mult)
-    ts(T.bpn[:, 0:1], T.ea[:, 15:16], 0.0, A.not_equal, ["ea"], ["bpn"], 2.0 * BIG, A.mult)
-    tt(T.mf[:, 0:16], T.e0[:], T.e1[:], A.add, ["e0", "e1"], ["mf"])
-    for n in (16, 32, 64, 128, 256):
-        m = min(n, C - n)
-        cp(T.mf[:, n:n + m], T.mf[:, 0:m], ["mf"], ["mf"])
-    for k in range(3):
-        ts(T.mn[:, kc(k)], T.mf[:], BIG, A.mult, ["mf"], ["mn"])
     ts(T.i3[:], T.i1[:], 15, A.bitwise_and, ["i1"], ["i3"])
-    cp(T.uo[:], T.ui[:], ["ui"], ["uo"])
-    tt(T.cl[:], T.i3[:], T.i2[:], A.add, ["i3", "i2"], ["cl"])
-    bp2, bpn = T.bp2[:, 0:1], T.bpn[:, 0:1]
-    ac(T.t0[:, 0:C], T.cr[:], ["cr"], ["t0a"], 0.0, 512.0)
-    ac(T.t0[:, C:], T.cr[:], ["cr"], ["t0b"], 0.0, 2048.0 * 512)
-    ac(T.cr0[:], T.cr[:], ["cr"], ["cr0"], 2049.0)
-    ac(T.t1[:, 0:C], T.cr[:], ["cr"], ["t1a"], 2048.0, 1024.0 + 2048 * 512)
-    ac(T.t1[:, C:], T.cr[:], ["cr"], ["t1b"], 2048.0, 512.0)
-    ac(T.t2[:, 0:C], T.cr[:], ["cr"], ["t2a"], 2048.0, 2048.0 * 1024)
-    ac(T.t2[:, C:], T.cr[:], ["cr"], ["t2b"], 2048.0, 1024.0 + 2048 * 1024)
-    for k in range(2):
-        ac(T.pi[:, 512 * k + C:512 * k + 512], T.cr[:, 0:224], ["cr"], ["pig%d" % k])
-    for k in range(2):
-        ac(T.zt[:, 512 * k + C:512 * k + 512], T.cr[:, 0:224], ["cr"], ["ztg%d" % k])
+    ts(T.e0[:], T.ea[:], 0.0, A.is_equal, ["ea"], ["e0"], 2.0, A.mult)
+    ts(T.e1[:], T.ea[:], 15.0, A.is_equal, ["ea"], ["e1"], -4.0, A.mult)
+    cp(T.io16[:], T.i3[:], ["i3"], ["io16"])
+    tt(T.m16[:, 0:15], T.e0[:, 0:15], T.e1[:, 0:15], A.add, ["e0", "e1"], ["m16a"])
+    ts(T.m16[:, 15:16], T.e0[:, 15:16], -3.0, A.add, ["e0"], ["m16b"])
+    ac(T.mn[:], T.m16[:, 0:16].indirect(T.io16[:, 0:36]), ["m16a", "m16b", "io16"], ["mn"], B)
+    ts(T.i4[:], T.i3[:, 0:18], 3.0, A.mult, ["i3"], ["i4"])
+    for k in range(3):
+        fill(T.t3[:, k3(k)], 0.0 if k else HUGE, ["t3%d" % k])
+    fill(T.a2[:, k3(2)], 0.0, ["a2c"])
 
-    ts(T.c1[:], T.wi[:], float(C), A.is_ge, ["wi"], ["c1"], 224.0, A.mult)
-    ts(T.c2[:], T.wi[:], 2.0 * C, A.is_ge, ["wi"], ["c2"], 224.0, A.mult)
-    tt(T.c1[:], T.c1[:], T.wi[:], A.add, ["c1", "wi"], ["c3"])
-    tt(T.new0[:], T.c1[:], T.c2[:], A.add, ["c3", "c2"], ["new0"])
+    ts(T.k1[:], T.wi[:], float(C), A.is_ge, ["wi"], ["k1"], 3.0 * C - 1, A.mult)
+    ts(T.w3[:], T.wi[:], 3.0, A.mult, ["wi"], ["w3"], -B, A.add)
+    ts(T.k2[:], T.wi[:], 2.0 * C, A.is_ge, ["wi"], ["k2"], 3.0 * C - 1, A.mult)
+    tt(T.w3[:], T.w3[:], T.k1[:], A.subtract, ["w3", "k1"], ["w3"])
+    tt(T.c3[:], T.i4[:], T.i2[:], A.add, ["i4", "i2"], ["c3"])
+    tt(T.p0[:], T.w3[:], T.k2[:], A.subtract, ["w3", "k2"], keys("gs", 0, 1, 2))
+    ts(T.c3m[:], T.c3[:], -B, A.add, ["c3"], ["c3m"])
+    ts(T.off[:], T.p0[:], B, A.add, keys("gs", 0, 1, 2), ["off"])
 
-    def lists(r):
-        w0 = T["new%d" % (r % 2)][:, 0:18]
-        w = "new%d" % (r % 2)
-        tt(T.tl[:], w0, T.cl[:], A.subtract, [w, "cl"], ["tl"])
-        ts(T.al[:], w0, 512.0, A.is_lt, [w], ["al"])
-        tt(T.tm[:], T.tl[:], T.al[:], A.mult, ["tl", "al"], ["tm"])
-        ts(T.qe[:, 0:18], T.al[:], 576.0, A.mult, ["al"], ["qe0"], -288.0, A.add)
-        tt(T.dp[:], T.tm[:], T.cl[:], A.add, ["tm", "cl"], ["dp"])
-        ts(T.qe[:, 18:36], T.al[:], 288.0, A.mult, ["al"], ["qe1"], 288.0, A.add)
-        cp(T.do[:], T.dp[:], ["dp"], ["do"])
+    def wired(r, a, e):
+        return T.p0[:, 18 * a:18 * e] if r == 0 else T.gs[:, C * a + 15:C * e:16]
 
-    def lists2():
-        tt(T.ie[:, 0:18], T.qe[:, 0:18], T.dp[:], A.add, ["qe0", "dp"], ["ie0"])
-        tt(T.ie[:, 18:36], T.qe[:, 18:36], T.dp[:], A.add, ["qe1", "dp"], ["ie1"])
-        cp(T.ieo[:], T.ie[:], ["ie0", "ie1"], ["ieo"])
+    def agents(out, r, k, key):
+        ts(out, wired(r, k, k + 1), 1.0 / 3, A.mult, ["gs%d" % k], [key], (B - 1) / 3, A.add)
 
-    def pis():
-        for k in range(3):
-            row = T.cr0 if k == 0 else T.cr
-            t = T["t%d" % k]
-            tt(T.pi[:, 512 * k:512 * k + C], t[:, 0:2 * C].indirect(T.do[:, 0:18]), row[:], A.add,
-               ["do", "t%da" % k, "t%db" % k, "cr0" if k == 0 else "cr"], ["pi%d" % k])
+    def ahead1(r, z0, key):
+        ts(T.e3[:], z0, 3.0, A.mult, [key], ["e3"], -B, A.add)
+        tt(T.w0c[:], wired(r, 0, 1), T.c3m[:], A.subtract, ["gs0", "c3m"], ["w0c"])
+        tt(T.act[:], wired(r, 0, 1), T.e3[:], A.is_equal, ["gs0", "e3"], ["act"])
+        tt(T.df[:, 18:54], wired(r, 0, 2), wired(r, 1, 3), A.subtract, keys("gs", 0, 1, 2), ["df1"])
+        tt(T.tt[:], T.w0c[:], T.act[:], A.mult, ["w0c", "act"], ["tt"])
+        tt(T.df[:, 0:18], wired(r, 2, 3), wired(r, 0, 1), A.subtract, keys("gs", 0, 2), ["df0"])
+        tt(T.qq[:], T.tt[:], T.c3[:], A.add, ["tt", "c3"], ["qq"])
+        tt(T.dg[:, k18(1)], T.df[:, k18(1)], T.act[:], A.mult, ["df1", "act"], ["dg1"])
+        tt(T.ap[:, k18(1)], T.qq[:], T.act[:], A.add, ["qq", "act"], ["ap1"])
+        ts(T.ap[:, k18(2)], T.qq[:], 2.0, A.add, ["qq"], ["ap2"])
+        tt(T.dg[:, k18(2)], T.df[:, k18(2)], T.act[:], A.mult, ["df1", "act"], ["dg2"])
+        cp(T.eo[:], T.ap[:, 18:54], ["ap1", "ap2"], ["eo"])
 
-    def thr():
-        ac(T.thr[:], T.t3[:, 0:2 * C].indirect(T.do[:, 0:18]), ["do", "t3a", "t3b"], ["thr"])
-
-    def nrow(r):
-        o = "off%d" % (r % 2)
-        rd = ["pi0", "pi1", "pi2", "pig0", "pig1", o]
-        ac(T.nr[:, 0:2 * C], T.pi[:, 0:1024 + C].indirect(T[o][:, 0:36]), rd, ["nr0"])
-        cp(T.nr[:, 2 * C:3 * C], T.pi[:, 0:1024 + C].indirect(T[o][:, 36:54]), rd, ["nr1"])
+    def ahead2(r):
+        tt(T.dg[:, k18(0)], T.df[:, k18(0)], T.act[:], A.mult, ["df0", "act"], ["dg0"])
+        ts(T.a2x[:], T.act[:], 2.0, A.mult, ["act"], ["a2x"])
+        tt(T.ap[:, k18(0)], T.c31[:], T.act[:], A.subtract, ["c31", "act"], ["ap0"])
+        tt(T.bc[:], T.dg[:], wired(r, 0, 3), A.add, keys("dg", 0, 1, 2) + keys("gs", 0, 1, 2), ["bc"])
+        ts(T.dp[:, k18(0)], T.act[:], -2.0, A.mult, ["act"], ["dp0"], 1.0, A.add)
+        ts(T.dp[:, k18(1)], T.tt[:], -1.0, A.add, ["tt"], ["dp1"])
+        tt(T.dp[:, k18(2)], T.tt[:], T.a2x[:], A.add, ["tt", "a2x"], ["dp2"])
+        tt(T.dc[:, k18(0)], T.bc[:, k18(1)], T.bc[:, k18(0)], A.subtract, ["bc"], ["dc0"])
 
     def erow():
-        ac(T.er[:], T.nr[:, 0:3 * C].indirect(T.ieo[:, 0:36]), ["nr0", "nr1", "ieo"], ["er"])
+        ac(T.er[:], T.gw[:, 0:3 * C].indirect(T.eo[:, 0:36]), keys("gw", 0, 1, 2) + ["eo"], ["er"])
 
-    def prep1():
-        ns = T.ns
-        scan(T.ns[:], T.mn[:], T.nr[:], ["mn", "nr0", "nr1"], ["ns"])
-        tt(T.df[:, 18:54], ns[:, 15:576:16], ns[:, 303:864:16], A.subtract, ["ns"], ["df1"])
-        tt(T.df[:, 0:18], ns[:, 591:864:16], ns[:, 15:288:16], A.subtract, ["ns"], ["df0"])
-        for k in (1, 2, 0):
-            tt(T.dg[:, k18(k)], T.df[:, k18(k)], T.al[:], A.mult, ["df0" if k == 0 else "df1", "al"], ["dg%d" % k])
+    def escan():
+        scan(T.es[:], T.mn[:], T.er[:], ["mn", "er"], ["es"])
 
-    def base():
-        tt(T.base[:], T.dg[:], T.ns[:, 15:864:16], A.add, ["dg0", "dg1", "dg2", "ns"], ["base"])
+    def ahead3():
+        tt(T.dc[:, 18:54], T.es[:, 15:2 * C:16], T.bc[:, 18:54], A.subtract, ["es", "bc"], ["dc1"])
 
-    def halves(r):
+    def thr():
+        ac(T.thr[:], T.t3[:, 0:3 * C].indirect(T.eo[:, 0:18]), ["eo"] + keys("t3", 0, 1, 2), ["thr"])
+
+    def halves(r, i):
+        a, e = CUT[i]
         for b in range(4):
-            ac(T.xh[:, kc(b)], T["x%d" % r][:, b:4 * C:4], ["x%d.%d" % (r, b)], ["xh%d" % b], 0.5)
+            ac(T.xh[:, C * b + a:C * b + e], T["x%d" % r][:, 4 * a + b:4 * e:4], ["x%d.%d%d" % (r, i, b)], ["xh%d%d" % (i, b)], 0.5)
 
-    def qstate(r):
-        quant(T.qx[:, 0:C], T.sx[:, 0:C], T["x%d" % r][:, 0:4 * C], ["x%d.%d" % (r, b) for b in range(4)], ["qx"])
+    def qstate(r, i):
+        a, e = CUT[i]
+        quant(T.qx[:, a:e], T.sx[:, a:e], T["x%d" % r][:, 4 * a:4 * e], xkeys(r, i), ["qx%d" % i])
 
-    def scores():
-        for k in (1, 0):
-            mm(k, C, T.u2[:, 128 * k:128 * k + 128], T.u2s[:, 128 * k:128 * k + 128], T.qx[:, 0:C], T.sx[:, 0:C],
-               ["u2", "u2s", "qx"])
+    def scores(i):
+        a, e = CUT[i]
+        for k in (0, 1):
+            mm(2 * i + k, e - a, T.u2[:, 128 * k:128 * k + 128], T.u2s[:, 128 * k:128 * k + 128], T.qx[:, a:e], T.sx[:, a:e],
+               ["u2", "u2s", "qx%d" % i])
 
-    lists(0)
-    cp(T.off0[:], T.new0[:], ["new0"], ["off0"])
-    lists2()
-    thr()
+    def sign_a(i):
+        a, e = CUT[i]
+        tt(T.am[:, a:e], bank(2 * i, e - a), T.thr[:, a:e], A.is_gt, ["b%d" % (2 * i), "thr"], ["am%d" % i])
+        if i == 0:
+            ac(T.a2[:, k3(1, a, e)], T.am[:, a:e], ["am%d" % i], ["a2a%d" % i])
+        else:
+            ts(T.a2[:, k3(1, a, e)], bank(2 * i, e - a), 0.0, A.is_gt, ["b%d" % (2 * i)], ["a2a%d" % i])
+
+    def sign_b(i):
+        a, e = CUT[i]
+        ac(T.a2[:, k3(0, a, e)], bank(2 * i + 1, e - a), ["b%d" % (2 * i + 1)], ["a2b%d" % i], func=F.Relu)
+
+    agents(T.zi[:], 0, 0, "zi")
+    for k in (1, 2):
+        ac(T.gw[:, k3(k)], T.idn[:, 0:3 * C].indirect(T.off[:, k18(k)]), ["idn", "off"], ["gw%d" % k])
+    ts(T.c31[:], T.c3[:], 1.0, A.add, ["c3"], ["c31"])
+    ahead1(0, T.zi[:], "zi")
+    cp(T.uo[:], T.ui[:], ["ui"], ["uo"])
     quant(T.uq[:, 0:128], T.us[:, 0:128], T.ut[:, 0:512], ["ut"], ["uq"])
+    cp(T.gw[:, k3(0)], T.idn[:, 0:3 * C].indirect(T.off[:, k18(0)]), ["idn", "off"], ["gw0"])
     op("s", lambda e: e.activation(T.u2s[:, 0:256], T.us[:, 0:128].indirect(T.uo[:, 0:16]), F.Copy), ["uq", "uo"], ["u2s"])
-    pis()
-    nrow(0)
+    erow()
+    thr()
     op("v", lambda e: e.tensor_copy(T.u2[:, 0:256].bitcast(dt.uint32), T.uq[:, 0:128].bitcast(dt.uint32).indirect(T.uo[:, 0:16])),
        ["uq", "uo"], ["u2"])
-    qstate(0)
-    scores()
-    erow()
-    prep1()
-    base()
+    for i in range(2):
+        qstate(0, i)
+        scores(i)
+    ts(T.mf[:], T.mn[:, 0:C], 1.0 / B, A.mult, ["mn"], ["mf"])
+    ahead2(0)
+    escan()
+    for i in range(2):
+        sign_b(i)
+        sign_a(i)
+    ahead3()
+    for i in range(2):
+        halves(0, i)
 
     for r in range(3):
         peer = T.cores[rank ^ STEP[r]]
@@ -286,146 +298,172 @@ def rank_program(g, core, T, topo):
             snap[(sem, arrive)] = {}
             total[sem] = arrive
         arrival("ra%d" % r, "la")
-        arrival("rb%d" % r, "lb")
+        if not OPT["one"]:
+            arrival("rb%d" % r, "lb")
         for i in range(2):
             arrival("rq%d%d" % (i, r), "lq%d" % i)
-        arrival("rs%d" % r, "ls")
-        n = (r + 1) % 2
-        new, off, za, zb = T["new%d" % n], T["off%d" % n], T["za%d" % r], T["zb%d" % r]
+            arrival("rs%d%d" % (i if OPT["s2"] else 1, r), "ls%d" % i)
+        zl, la, lb = T["zl%d" % r], T["la%d" % r], T["lb%d" % r]
         lq, ls, qh, sh = T["lq%d" % r], T["ls%d" % r], T["qh%d" % r], T["sh%d" % r]
 
-        ac(T.a2[:, C:2 * C], bank(1), ["b1"], ["a2b"], func=F.Relu)
-        halves(r)
-        scan(T.es[:], T.mn[:, 0:2 * C], T.er[:], ["mn", "er"], ["es"])
-        tt(T.am[:], bank(0), T.thr[:], A.is_gt, ["b0", "thr"], ["am"])
-        tt(T.dl[:, 18:54], T.es[:, 15:576:16], T.base[:, 18:54], A.subtract, ["es", "base"], ["dl1"])
-        tt(T.dl[:, 0:18], T.base[:, 18:36], T.base[:, 0:18], A.subtract, ["base"], ["dl0"])
-        cp(T.a2[:, 0:C], T.am[:], ["am"], ["a2a"])
-        ts(T.bd[:], T.dl[:], bp2, A.mult, ["dl0", "dl1", "bp2", "bpn"], ["bd"], bpn, A.add)
-        tt(T.base2[:], T.base[:], T.bd[:], A.subtract, ["base", "bd"], ["base2"])
-        tt(T.fr[:], T.a2[:, 0:2 * C].indirect(T.do[:, 0:18]), T.am[:], A.not_equal, ["a2a", "a2b", "am", "do"], ["fr"])
+        tt(T.fr[:], T.a2[:, 0:3 * C].indirect(T.eo[:, 0:18]), T.am[:], A.not_equal,
+           ["am0", "am1", "a2a0", "a2a1", "a2b0", "a2b1", "a2c", "eo"], ["fr"])
         scan(T.fs[:], T.mf[:], T.fr[:], ["mf", "fr"], ["fs"])
 
-        for k in (1, 2, 0):
-            tt(T.st[:, k18(k)], T.fs[:, 15:C:16], T.dl[:, k18(k)], A.mult, ["fs", "dl0", "dl1"], ["st%d" % k])
-        tt(T.sel[:], T.st[:], T.base2[:], A.add, ["st0", "st1", "st2", "base2"], ["sel"])
-        ts(T.xi[:], T.sel[:], 511, A.bitwise_and, ["sel"], ["xi"])
-        cp(T.xo[:], T.xi[:], ["xi"], ["xo"])
-        for k in (1, 2, 0):
-            ac(T.fx[:, kc(k)], T.fr[:, 0:C].indirect(T.xo[:, k18(k)]), ["fr", "xo"], ["fx%d" % k])
-        ts(T.zn[:], T.sel[:], 11, A.logical_shift_right, ["sel"], ["zn"], 511, A.bitwise_and)
-        tt(T.dz[:], T.zn[:], T.xi[:], A.subtract, ["zn", "xi"], ["dz"])
-        ts(T.bb[:], T.dz[:], bp2, A.mult, ["dz", "bp2"], ["bb"])
-        tt(T.bz[:], T.xi[:], T.bb[:], A.subtract, ["xi", "bb"], ["bz"])
+        fl = T.fs[:, 15:C:16]
+        for k in range(3):
+            tt(T.sp[:, k18(k)], fl, T.dp[:, k18(k)], A.mult, ["fs", "dp%d" % k], ["sp%d" % k])
+        tt(T.sc[:, k18(1)], fl, T.dc[:, k18(1)], A.mult, ["fs", "dc1"], ["sc1"])
+        tt(T.pl[:], T.sp[:], T.ap[:], A.add, keys("sp", 0, 1, 2) + keys("ap", 0, 1, 2), ["pl"])
+        tt(T.sc[:, k18(2)], fl, T.dc[:, k18(2)], A.mult, ["fs", "dc1"], ["sc2"])
+        tt(T.sc[:, k18(0)], fl, T.dc[:, k18(0)], A.mult, ["fs", "dc0"], ["sc0"])
+        cp(T.po[:], T.pl[:], ["pl"], ["po"])
+        tt(T.cl[:, 18:54], T.sc[:, 18:54], T.es[:, 15:2 * C:16], A.add, ["sc1", "sc2", "es"], ["cl1"])
+        tt(T.cl[:, 0:18], T.sc[:, 0:18], T.bc[:, k18(1)], A.add, ["sc0", "bc"], ["cl0"])
+        idn = T.idn[:, 0:3 * C]
+        half = 192
+        ac(T.tab[:, k3(0)], idn.indirect(T.po[:, k18(0)]), ["idn", "po"], ["tab0"])
+        ac(T.tab[:, k3(1, 0, half)], idn.indirect(T.po[:, 18:18 + half // 16]), ["idn", "po"], ["tab1"])
+        cp(T.tab[:, k3(2)], idn.indirect(T.po[:, k18(2)]), ["idn", "po"], ["tab2"])
+        ts(T.co[:], T.cl[:], B, A.add, ["cl0", "cl1"], ["co"])
+        cp(T.tab[:, k3(1, half, C)], idn.indirect(T.po[:, 18 + half // 16:36]), ["idn", "po"], ["tab3"])
+        tab = T.tab[:, 0:3 * C]
+        tk = keys("tab", 0, 1, 2, 3) + ["co"]
+        cp(T.gw[:, k3(1)], tab.indirect(T.co[:, k18(1)]), tk, ["gw1"])
+        for k in (2, 0):
+            ac(T.gw[:, k3(k)], tab.indirect(T.co[:, k18(k)]), tk, ["gw%d" % k])
 
-        def fscan(k):
-            scan(T.fxs[:, kc(k)], T.mf[:], T.fx[:, kc(k)], ["mf", "fx%d" % k], ["fxs%d" % k])
-
-        def zmul(k):
-            tt(T.zf[:, k18(k)], T.fxs[:, C * k + 15:C * k + C:16], T.dz[:, k18(k)], A.mult, ["fxs%d" % k, "dz"], ["zm%d" % k])
-
-        def zadd(k):
-            tt(T.zf[:, k18(k)], T.zf[:, k18(k)], T.bz[:, k18(k)], A.add, ["zm%d" % k, "bz"], ["zf%d" % k])
+        def gscan(k):
+            scan(T.gs[:, kc(k)], T.mn[:, 0:C], T.gw[:, k3(k)], ["mn", "gw%d" % k], ["gs%d" % k])
 
         def zout(k):
-            cp(zb[:] if k == 0 else za[:, k18(k - 1)], T.zf[:, k18(k)], ["zf%d" % k], ["zo%d" % k])
-        fscan(1)
-        zmul(1)
-        fscan(2)
-        zadd(1)
-        zmul(2)
+            agents(zl[:, k18(k)], r + 1, k, "zo%d" % k)
+        gscan(1)
         zout(1)
-        zadd(2)
+        gscan(2)
+        if OPT["one"]:
+            gscan(0)
         zout(2)
-        send(T["la%d" % r][:], za[:], "ra%d" % r, ["zo1", "zo2"])
+        if OPT["one"]:
+            zout(0)
+            send(la[:], zl[:], "ra%d" % r, ["zo0", "zo1", "zo2"])
+        else:
+            send(la[:, 18:54], zl[:, 18:54], "ra%d" % r, ["zo1", "zo2"])
 
         def hquant(i):
             a, e = CUT[i]
             quant(qh[:, a:e], sh[:, a:e], T.h[:, 4 * a:4 * e], ["h%d%d" % (i, b) for b in range(4)], ["qh%d" % i])
             send(lq[:, a:e].bitcast(dt.uint8), qh[:, a:e].bitcast(dt.uint8), "rq%d%d" % (i, r), ["qh%d" % i])
-            if i == 1:
-                send(ls[:, 0:C], sh[:, 0:C], "rs%d" % r, ["qh0", "qh1"])
-        for i, (a, e) in enumerate(CUT):
+            if OPT["s2"]:
+                send(ls[:, a:e], sh[:, a:e], "rs%d%d" % (i, r), ["qh%d" % i])
+            elif i == 1:
+                send(ls[:, 0:C], sh[:, 0:C], "rs%d%d" % (i, r), ["qh0", "qh1"])
+
+        def zquant(i):
+            a, e = CUT[i]
+            quant(T.qz[:, a:e], T.sz[:, a:e], T.z[:, 4 * a:4 * e], keys("z%d" % i, 0, 1, 2, 3), ["qz%d" % i])
             for b in range(4):
-                ac(T.zp[:, C * b + a:C * b + e], T.xh[:, kc(b)].indirect(za[:, a // 16:e // 16]),
-                   ["xh%d" % b, "zo1"], ["zp%d%d" % (i, b)])
-                tt(T.z[:, 4 * a + b:4 * e:4], T.xh[:, kc(b)].indirect(za[:, 18 + a // 16:18 + e // 16]),
-                   T.zp[:, C * b + a:C * b + e], A.add, ["xh%d" % b, "zo2", "zp%d%d" % (i, b)], ["z%d" % i])
-            quant(T.qz[:, a:e], T.sz[:, a:e], T.z[:, 4 * a:4 * e], ["z%d" % i], ["qz%d" % i])
-        for i, (a, e) in enumerate(CUT):
-            for b in range(4):
-                k = (2 + 4 * i + b) % 8
-                mm(k, e - a, T.wq[:, 128 * b:128 * b + 128], T.wsc[:, 128 * b:128 * b + 128], T.qz[:, a:e], T.sz[:, a:e],
-                   ["wq", "wsc", "qz%d" % i])
+                mm(4 - 4 * i + b, e - a, T.wq[:, 128 * b:128 * b + 128], T.wsc[:, 128 * b:128 * b + 128], T.qz[:, a:e],
+                   T.sz[:, a:e], ["wq", "wsc", "qz%d" % i])
+
+        def hcopy(i, b, q):
+            a, e = CUT[i]
+            k = 4 - 4 * i + b
+            if q == "s":
                 ac(T.h[:, 4 * a + b:4 * e:4], bank(k, e - a), ["b%d" % k], ["h%d%d" % (i, b)], 0.03125)
-        fscan(0)
-        ts(T.n0[:], T.sel[:], 2047, A.bitwise_and, ["sel"], ["n0"])
-        ts(T.n1[:], T.sel[:], 11, A.logical_shift_right, ["sel"], ["n1"])
-        zmul(0)
-        tt(T.dn[:], T.n1[:], T.n0[:], A.subtract, ["n1", "n0"], ["dn"])
-        hquant(0)
-        zadd(0)
-        ts(T.bb[:], T.dn[:], bp2, A.mult, ["dn", "bp2"], ["bb"])
-        tt(T.nt[:], T.fxs[:, 15:3 * C:16], T.dn[:], A.mult, ["fxs0", "fxs1", "fxs2", "dn"], ["nt"])
-        zout(0)
-        send(T["lb%d" % r][:], zb[:], "rb%d" % r, ["zo0"])
-        tt(T.b2[:], T.n0[:], T.bb[:], A.subtract, ["n0", "bb"], ["b2"])
-        hquant(1)
-        tt(new[:], T.nt[:], T.b2[:], A.add, ["nt", "b2"], ["new%d" % n])
-        cp(off[:], new[:], ["new%d" % n], ["off%d" % n])
-
-        if r == 0:
-            iota(T.pt[:], [[C, 3], [1, 512]], 0, 0, ["pt"], True)
-        if not last:
-            lists(r + 1)
-            pis()
-            lists2()
-            thr()
-        for k in (1, 2):
-            ac(T.zt[:, 512 * k:512 * k + C], T.cr[:, 0:C].indirect(T["la%d" % r][:, k18(k - 1)]), ["cr", "la"], ["zt%d" % k])
-        if r == 0:
-            quant(T.eq[:, 0:512], T.esc[:, 0:512], T.et[:, 0:2048], ["et%d" % b for b in range(4)], ["eq"])
-        if last:
-            quant(T.vq[:, 0:128], T.vs[:, 0:128], T.vt[:, 0:512], ["vt"], ["vq"])
-        if not last:
-            nrow(r + 1)
-        ac(T.zt[:, 0:C], T.cr[:, 0:C].indirect(T["lb%d" % r][:, 0:18]), ["cr", "lb"], ["zt0"])
-        ac(T.mr[:], T.zt[:, 0:1024 + C].indirect(off[:, 0:18]), ["zt0", "zt1", "zt2", "ztg0", "ztg1", "off%d" % n], ["mr"])
-        if not last:
-            prep1()
-        scan(T.ms[:], T.mn[:, 0:C], T.mr[:], ["mn", "mr"], ["ms"])
-        if not last:
-            base()
-        ts(T.mo[:], T.ms[:, 15:C:16], bpn, A.subtract, ["ms", "bpn"], ["mo"])
-        if last:
-            ac(T.owt[:], T.pt[:, 0:1024 + C].indirect(off[:, 0:54]), ["pt", "off%d" % n], ["owt"])
-            dma("y", "ow", T.ow[:], T.owt[0:128:16, :], ["owt"], [])
-
-        x, y = "x%d" % r, "x%d" % (r + 1)
+            else:
+                ts(T.h[:, 4 * a + b:4 * e:4], bank(k, e - a), 0.03125, A.mult, ["b%d" % k], ["h%d%d" % (i, b)])
+        for i, (a, e) in enumerate(CUT):
+            for b in range(4):
+                xh = T.xh[:, kc(b)]
+                xk = ["xh0%d" % b, "xh1%d" % b]
+                ac(T.zp[:, C * b + a:C * b + e], xh.indirect(zl[:, 18 + a // 16:18 + e // 16]), xk + ["zo1"], ["zp%d%d" % (i, b)])
+                tt(T.z[:, 4 * a + b:4 * e:4], xh.indirect(zl[:, 36 + a // 16:36 + e // 16]),
+                   T.zp[:, C * b + a:C * b + e], A.add, xk + ["zo2", "zp%d%d" % (i, b)], ["z%d%d" % (i, b)])
+                if (i, b) == (1, 0):
+                    zquant(0)
         for b in range(4):
-            k = 2 + b
-            mm(k, C, T.eq[:, 128 * b:128 * b + 128], T.esc[:, 128 * b:128 * b + 128], lq[:, 0:C], ls[:, 0:C],
-               ["eq", "lq0", "lq1", "ls"])
-            ac(T.d[:, kc(b)], bank(k), ["b%d" % k], ["d%d" % b])
+            hcopy(0, b, "s")
+        if not OPT["one"]:
+            gscan(0)
+        zquant(1)
+        if not OPT["one"]:
+            zout(0)
+            send(lb[:], zl[:, 0:18], "rb%d" % r, ["zo0"])
+        hquant(0)
+        if last:
+            ts(T.off[:], wired(r + 1, 0, 3), B, A.add, keys("gs", 0, 1, 2), ["off"])
+        else:
+            ts(T.off[:, 0:18], wired(r + 1, 0, 1), B, A.add, ["gs0"], ["off"])
+        for b, q in enumerate("svsv"):
+            hcopy(1, b, q)
+        hquant(1)
+
+        if r == 0:
+            iota(T.unp[:], [[1, C], [C, 3]], 0, 0, ["unp"], True)
+        if r == 0:
+            quant(T.eq[:, 0:512], T.esc[:, 0:512], T.et[:, 0:2048], ["et"], ["eq"])
+        if not last:
+            ahead1(r + 1, zl[:, 0:18], "zo0")
+        for k in (1, 2):
+            ac(T.zt[:, k3(k)], T.idn[:, 0:C].indirect(la[:, k18(k)]), ["idn", "la"], ["zt%d" % k])
         if not last:
             erow()
-        for b in range(4):
-            tt(T[y][:, b:4 * C:4], T.d[:, kc(b)].indirect(T.mo[:, 0:18]), T[x][:, b:4 * C:4], A.add,
-               ["d%d" % b, "mo", "%s.%d" % (x, b)], ["%s.%d" % (y, b)])
-        qstate(r + 1)
+        if last:
+            quant(T.vq[:, 0:128], T.vs[:, 0:128], T.vt[:, 0:512], ["vt"], ["vq"])
+        cp(T.zt[:, k3(0)], T.idn[:, 0:C].indirect(la[:, 0:18]), ["idn", "la"], ["zt0"])
         if not last:
-            scores()
+            ahead2(r + 1)
+        cp(T.mr[:], T.zt[:, 0:3 * C].indirect(T.off[:, 0:18]), keys("zt", 0, 1, 2) + ["off"], ["mr"])
+        if last:
+            ac(T.owt[:], T.unp[:, 0:3 * C].indirect(T.off[:, 0:54]), ["unp", "off"], ["owt"])
+            dma("y", "ow", T.ow[:], T.owt[0:128:16, :], ["owt"], [])
+        else:
+            escan()
+        scan(T.ms[:], T.mn[:, 0:C], T.mr[:], ["mn", "mr"], ["ms"])
+        if not last:
+            ahead3()
+        ts(T.mo[:], T.ms[:, 15:C:16], B, A.add, ["ms"], ["mo"])
 
-    h = C // 2
-    for i in range(2):
-        mm(2 + i, h, T.vq[:, 0:128], T.vs[:, 0:128], T.qx[:, h * i:h * i + h], T.sx[:, h * i:h * i + h], ["vq", "qx"])
-    dma("y", "oc", T.oc[:, 0:4 * C], T.qx[:, 0:C].bitcast(dt.uint8), ["qx"], [])
+        for i, (a, e) in enumerate(CUT):
+            for b in range(4):
+                k = 4 * i + b
+                mm(k, e - a, T.eq[:, 128 * b:128 * b + 128], T.esc[:, 128 * b:128 * b + 128], lq[:, a:e], ls[:, a:e],
+                   ["eq", "lq%d" % i, "ls%d" % i])
+                ac(T.d[:, C * b + a:C * b + e], bank(k, e - a), ["b%d" % k], ["d%d%d" % (i, b)])
+        if not last:
+            thr()
+        x, y = T["x%d" % r], T["x%d" % (r + 1)]
+        for i, (a, e) in enumerate(CUT):
+            for b in range(4):
+                tt(y[:, 4 * a + b:4 * e:4], T.d[:, kc(b)].indirect(T.mo[:, a // 16:e // 16]), x[:, 4 * a + b:4 * e:4], A.add,
+                   ["d0%d" % b, "d1%d" % b, "mo", "x%d.%d%d" % (r, i, b)], ["x%d.%d%d" % (r + 1, i, b)])
+                if (i, b) == (1, 0):
+                    qstate(r + 1, 0)
+                    if not last:
+                        scores(0)
+                        halves(r + 1, 0)
+                        sign_b(0)
+        if not last:
+            halves(r + 1, 1)
+            qstate(r + 1, 1)
+            sign_a(0)
+            scores(1)
+            sign_b(1)
+            sign_a(1)
+
+    for i, (a, e) in enumerate(CUT):
+        if i == 1:
+            qstate(3, 1)
+        mm(i, e - a, T.vq[:, 0:128], T.vs[:, 0:128], T.qx[:, a:e], T.sx[:, a:e], ["vq", "qx%d" % i])
+        dma("y", "oc%d" % i, T.oc[:, 4 * a:4 * e], T.qx[:, a:e].bitcast(dt.uint8), ["qx%d" % i], [])
+        if i == 0:
+            ac(T.yt[:, a:e], bank(i, e - a), ["b%d" % i], ["yt%d" % i])
+        else:
+            cp(T.yt[:, a:e], bank(i, e - a), ["b%d" % i], ["yt%d" % i])
+        dma("s", "y%d" % i, T.y[:, a:e], T.yt[:, a:e], ["yt%d" % i], [])
     for k in range(4):
-        dma("y", "os%d" % k, T.osc[4 * k:4 * k + 4, 0:C], T.sx[32 * k:32 * k + 4, 0:C], ["qx"], [])
-    cp(T.yt[:, h:C], bank(3, h), ["b3"], ["yt1"])
-    ac(T.yt[:, 0:h], bank(2, h), ["b2"], ["yt0"])
-    dma("s", "y0", T.y[:, 0:h], T.yt[:, 0:h], ["yt0"], [])
-    dma("s", "y1", T.y[:, h:C], T.yt[:, h:C], ["yt1"], [])
+        dma("y", "os%d" % k, T.osc[4 * k:4 * k + 4, 0:C], T.sx[32 * k:32 * k + 4, 0:C], ["qx0", "qx1"], [])
     for s, m in sorted(total.items()):
         if waited.get(s, 0) < m:
             g.wait_ge(T.sem[s], m)

@@ -4,8 +4,10 @@ C = 288
 STEP = [4, 1, 2]
 HUGE = 1e29
 B = 1024.0
+B4 = 2048.0
+M4 = 1.5 * 2 ** 25
 CUT = [(0, 160), (160, 288)]
-OPT = {"one": 1, "s2": 1}
+OPT = {"s2": 1, "sa": 80, "sb": 80, "late": (0, 0, 0), "e1": 0, "a0": 0, "hq": "vvss", "u2s": "s", "gv": 1, "go": "01oa2cbc"}
 
 _f, _b, _i, _u = "float32", "bfloat16", "int32", "uint16"
 _q, _s = "float8_e4m3fn_x4", "uint8"
@@ -20,27 +22,28 @@ def _scratch():
     sb("wq", 512, _q); sb("wsc", 512, _s)
     sb("uq", 128, _q); sb("us", 128, _s); sb("u2", 256, _q); sb("u2s", 256, _s)
     sb("vq", 128, _q); sb("vs", 128, _s)
-    sb("ones", 2048, _b); sb("et", 2048, _b); sb("eq", 512, _q); sb("esc", 512, _s)
+    sb("ones", 512, _b); sb("et", 2048, _b); sb("eq", 512, _q); sb("esc", 512, _s)
     sb("idn", 3 * C, _f); sb("unp", 3 * C, _f); sb("t3", 3 * C, _b)
     sb("ei", 16, _i); sb("ea", 16, _i); sb("e0", 16, _b); sb("e1", 16, _b); sb("m16", 16, _b)
-    sb("mf", C, _b); sb("mn", 2 * C, _b)
-    sb("i1", 36, _i); sb("i2", 18, _i); sb("i3", 36, _i); sb("i4", 18, _f); sb("io16", 36, _u)
+    sb("fa", 4, _i); sb("f0", 4, _b); sb("f1", 4, _b); sb("m4", 4, _b); sb("j4", 18, _i); sb("jo4", 18, _u); sb("bcol", 8, _f)
+    sb("mf", C, _b); sb("mn", C, _b); sb("mq", C, _b); sb("j3", C, _f); sb("conv", 3 * C, _f)
+    sb("i1", 18, _i); sb("i2", 18, _i); sb("i3", 18, _i); sb("i4", 18, _f); sb("io16", 18, _u)
     sb("c3", 18, _f); sb("c3m", 18, _f); sb("c31", 18, _f); sb("ui", 16, _i); sb("uo", 16, _u)
     sb("k1", 54, _f); sb("k2", 54, _f); sb("w3", 54, _f); sb("p0", 54, _f); sb("zi", 18, _u); sb("off", 54, _u)
     for n in ("e3", "act", "w0c", "tt", "qq", "a2x"):
         sb(n, 18, _f)
     for n in ("ap", "dp", "df", "dg", "bc", "dc", "sp", "sc", "pl", "cl"):
         sb(n, 54, _f)
-    sb("eo", 36, _u); sb("po", 54, _u); sb("co", 54, _u)
+    sb("eo", 36, _u); sb("po", 54, _u); sb("co", 54, _u); sb("zl", 36, _u)
     sb("thr", C, _b); sb("a2", 3 * C, _b); sb("am", C, _b); sb("fr", C, _b); sb("fs", C, _b)
     sb("tab", 3 * C, _f); sb("gw", 3 * C, _f); sb("gs", 3 * C, _f); sb("er", 2 * C, _f); sb("es", 2 * C, _f)
-    sb("zt", 3 * C, _f); sb("mr", C, _f); sb("ms", C, _f); sb("mo", 18, _u)
+    sb("mr", C, _f); sb("ms", C, _f); sb("mo", 72, _u)
     for r in range(4):
         sb("x%d" % r, 4 * C, _b)
     sb("qx", C, _q); sb("sx", C, _s); sb("qz", C, _q); sb("sz", C, _s)
-    sb("xh", 4 * C, _b); sb("zp", 4 * C, _b); sb("z", 4 * C, _b); sb("h", 4 * C, _b); sb("d", 4 * C, _b)
+    sb("xh", 4 * C, _b); sb("zp", 4 * C, _b); sb("z", 4 * C, _b); sb("h", 4 * C, _b); sb("hp", 4 * C, _b)
     for r in range(3):
-        sb("zl%d" % r, 54, _u); sb("la%d" % r, 54, _u); sb("lb%d" % r, 18, _u)
+        sb("ol%d" % r, 18, _u); sb("la%d" % r, 18, _u)
         sb("qh%d" % r, C, _q); sb("sh%d" % r, C, _s); sb("lq%d" % r, C, _q); sb("ls%d" % r, C, _s)
     sb("yt", C, _f); sb("owt", 3 * C, _f)
     d["ps"] = ("psum", [128, 4096], _f)
@@ -48,9 +51,9 @@ def _scratch():
 
 
 SCRATCH = _scratch()
-_DMAS = ["x", "u", "v", "w", "wc", "ws", "y0", "y1", "ow", "oc0", "oc1", "os0", "os1", "os2", "os3"]
+_DMAS = ["x", "u", "v", "w", "wc", "ws", "out"]
 SEMAPHORES = (["qv", "qs", "qt", "qg", "loc"] + ["d" + n for n in _DMAS] +
-              ["r%s%d" % (n, r) for n in ("a", "b", "q0", "q1", "s0", "s1") for r in range(3)])
+              ["r%s%d" % (n, r) for n in ("a", "q0", "q1", "s0", "s1") for r in range(3)])
 
 
 def rank_program(g, core, T, topo):
@@ -97,7 +100,7 @@ def rank_program(g, core, T, topo):
     def dma(q, name, out, in_, rd, wr):
         before(q, rd, wr)
         queue[q].dma_start(out, in_).then_inc(T.sem["d" + name], 16)
-        after(q, ("d" + name, 16), rd, wr)
+        after(q, ("d" + name, 16 + total.get("d" + name, 0)), rd, wr)
 
     def tt(out, a, b, o, rd, wr):
         op("v", lambda e: e.tensor_tensor(out, a, b, o), rd, wr)
@@ -118,7 +121,7 @@ def rank_program(g, core, T, topo):
         op("s", lambda e: e.activation(out, a, func, bias=bias, scale=scale), rd, wr)
 
     def scan(out, mask, v, rd, wr):
-        op("v", lambda e: e.tensor_tensor_scan(out, v, mask, 0.0, A.max, A.add), rd, wr)
+        op("v", lambda e: e.tensor_tensor_scan(out, v, mask, -B, A.max, A.add), rd, wr)
 
     def quant(q, s, x, rd, wr):
         op("v", lambda e: e.quantize_mx(q, s, x), rd, wr)
@@ -157,72 +160,94 @@ def rank_program(g, core, T, topo):
         else:
             op("g", lambda e: e.iota(out, pattern, base, cm), [], wr)
     iota(T.ei[:], [[1, 16]], 128, -1, ["ei"])
-    iota(T.i1[:], [[0, 36]], 0, 1, ["i1"])
-    iota(T.idn[:], [[1, 3 * C]], 0, 0, ["idn"], True)
+    iota(T.i1[:], [[0, 18]], 0, 1, ["i1"])
+    iota(T.j3[:], [[3, C]], -1, 0, ["j3"], True)
     iota(T.i2[:], [[48, 18]], 0, 0, ["i2"])
     iota(T.ui[:], [[1, 2], [16, 8]], 0, 0, ["ui"])
+    iota(T.idn[:], [[1, 3 * C]], -1, 0, ["idn"], True)
     fill(T.ones[:], 1.0, ["ones"])
-    op("g", lambda e: e.affine_select(T.et[:], T.ones[:], [[1, 4], [-1, 512]], A.is_equal, 0.0, 0, 4), ["ones"], ["et"])
-    ts(T.ea[:], T.ei[:], 15, A.bitwise_and, ["ei"], ["ea"])
-    ts(T.i3[:], T.i1[:], 15, A.bitwise_and, ["i1"], ["i3"])
-    ts(T.e0[:], T.ea[:], 0.0, A.is_equal, ["ea"], ["e0"], 2.0, A.mult)
-    ts(T.e1[:], T.ea[:], 15.0, A.is_equal, ["ea"], ["e1"], -4.0, A.mult)
-    cp(T.io16[:], T.i3[:], ["i3"], ["io16"])
-    tt(T.m16[:, 0:15], T.e0[:, 0:15], T.e1[:, 0:15], A.add, ["e0", "e1"], ["m16a"])
-    ts(T.m16[:, 15:16], T.e0[:, 15:16], -3.0, A.add, ["e0"], ["m16b"])
-    ac(T.mn[:], T.m16[:, 0:16].indirect(T.io16[:, 0:36]), ["m16a", "m16b", "io16"], ["mn"], B)
-    ts(T.i4[:], T.i3[:, 0:18], 3.0, A.mult, ["i3"], ["i4"])
-    for k in range(3):
-        fill(T.t3[:, k3(k)], 0.0 if k else HUGE, ["t3%d" % k])
-    fill(T.a2[:, k3(2)], 0.0, ["a2c"])
+    for b in range(4):
+        op("g", lambda e: e.affine_select(T.et[:, 512 * b:512 * b + 512], T.ones[:], [[-1, 512]], A.is_equal, 0.0, b, 4),
+           ["ones"], ["et%d" % b])
 
+    def mask(ahead, own, prev, m, n, key):
+        ts(own[:], ahead[:], 0.0, A.is_equal, [key], [key + "0"], 2.0, A.mult)
+        ts(prev[:], ahead[:], n - 1.0, A.is_equal, [key], [key + "1"], -4.0, A.mult)
+        ts(m[:, n - 1:n], own[:, n - 1:n], -3.0, A.add, [key + "0"], [key + "b"])
+        tt(m[:, 0:n - 1], own[:, 0:n - 1], prev[:, 0:n - 1], A.add, [key + "0", key + "1"], [key + "a"])
+    ts(T.ea[:], T.ei[:], 15, A.bitwise_and, ["ei"], ["ea"])
+    ts(T.fa[:], T.ei[:, 3:16:4], 15, A.bitwise_and, ["ei"], ["fa"], 2, A.logical_shift_right)
+    ts(T.i3[:], T.i1[:], 15, A.bitwise_and, ["i1"], ["i3"])
+    ts(T.j4[:], T.i1[:], 3, A.bitwise_and, ["i1"], ["j4"])
+    mask(T.ea, T.e0, T.e1, T.m16, 16, "ea")
+    cp(T.io16[:], T.i3[:], ["i3"], ["io16"])
+    for k in range(3):
+        ac(T.t3[:, k3(k)], T.ones[:, 0:C], ["ones"], ["t3%d" % k], 0.0 if k else HUGE)
+    for k in range(3):
+        ac(T.conv[:, kc(k)], T.j3[:], ["j3"], ["conv%d" % k], 1.0, float(k))
+    ts(T.i4[:], T.i3[:], 3.0, A.mult, ["i3"], ["i4"])
+    ts(T.mn[:], T.m16[:, 0:16].indirect(T.io16[:, 0:18]), B, A.mult, ["eaa", "eab", "io16"], ["mn"])
+    tt(T.c3[:], T.i4[:], T.i2[:], A.add, ["i4", "i2"], ["c3"])
+    cp(T.uo[:], T.ui[:], ["ui"], ["uo"])
+    ts(T.c3m[:], T.c3[:], -B - 1, A.add, ["c3"], ["c3m"])
+    ts(T.c31[:], T.c3[:], 1.0, A.add, ["c3"], ["c31"])
+
+    cp(T.off[:], T.wi[:], ["wi"], ["off"])
     ts(T.k1[:], T.wi[:], float(C), A.is_ge, ["wi"], ["k1"], 3.0 * C - 1, A.mult)
-    ts(T.w3[:], T.wi[:], 3.0, A.mult, ["wi"], ["w3"], -B, A.add)
+    ts(T.w3[:], T.wi[:], 3.0, A.mult, ["wi"], ["w3"], -B - 1, A.add)
     ts(T.k2[:], T.wi[:], 2.0 * C, A.is_ge, ["wi"], ["k2"], 3.0 * C - 1, A.mult)
     tt(T.w3[:], T.w3[:], T.k1[:], A.subtract, ["w3", "k1"], ["w3"])
-    tt(T.c3[:], T.i4[:], T.i2[:], A.add, ["i4", "i2"], ["c3"])
+    quant(T.uq[:, 0:128], T.us[:, 0:128], T.ut[:, 0:512], ["ut"], ["uq"])
     tt(T.p0[:], T.w3[:], T.k2[:], A.subtract, ["w3", "k2"], keys("gs", 0, 1, 2))
-    ts(T.c3m[:], T.c3[:], -B, A.add, ["c3"], ["c3m"])
-    ts(T.off[:], T.p0[:], B, A.add, keys("gs", 0, 1, 2), ["off"])
+    fill(T.a2[:, k3(2)], 0.0, ["a2c"])
 
     def wired(r, a, e):
         return T.p0[:, 18 * a:18 * e] if r == 0 else T.gs[:, C * a + 15:C * e:16]
 
     def agents(out, r, k, key):
-        ts(out, wired(r, k, k + 1), 1.0 / 3, A.mult, ["gs%d" % k], [key], (B - 1) / 3, A.add)
+        ts(out, wired(r, k, k + 1), 1.0 / 3, A.mult, ["gs%d" % k], [key], B / 3, A.add)
 
-    def ahead1(r, z0, key):
-        ts(T.e3[:], z0, 3.0, A.mult, [key], ["e3"], -B, A.add)
-        tt(T.w0c[:], wired(r, 0, 1), T.c3m[:], A.subtract, ["gs0", "c3m"], ["w0c"])
-        tt(T.act[:], wired(r, 0, 1), T.e3[:], A.is_equal, ["gs0", "e3"], ["act"])
-        tt(T.df[:, 18:54], wired(r, 0, 2), wired(r, 1, 3), A.subtract, keys("gs", 0, 1, 2), ["df1"])
-        tt(T.tt[:], T.w0c[:], T.act[:], A.mult, ["w0c", "act"], ["tt"])
-        tt(T.df[:, 0:18], wired(r, 2, 3), wired(r, 0, 1), A.subtract, keys("gs", 0, 2), ["df0"])
-        tt(T.qq[:], T.tt[:], T.c3[:], A.add, ["tt", "c3"], ["qq"])
-        tt(T.dg[:, k18(1)], T.df[:, k18(1)], T.act[:], A.mult, ["df1", "act"], ["dg1"])
-        tt(T.ap[:, k18(1)], T.qq[:], T.act[:], A.add, ["qq", "act"], ["ap1"])
-        ts(T.ap[:, k18(2)], T.qq[:], 2.0, A.add, ["qq"], ["ap2"])
-        tt(T.dg[:, k18(2)], T.df[:, k18(2)], T.act[:], A.mult, ["df1", "act"], ["dg2"])
-        cp(T.eo[:], T.ap[:, 18:54], ["ap1", "ap2"], ["eo"])
+    def places(r):
+        return [
+            lambda: agents(T.zi[:], r, 0, "zi"),
+            lambda: ts(T.e3[:], T.zi[:], 3.0, A.mult, ["zi"], ["e3"], -B - 1, A.add),
+            lambda: tt(T.act[:], wired(r, 0, 1), T.e3[:], A.is_equal, ["gs0", "e3"], ["act"]),
+            lambda: tt(T.tt[:], T.w0c[:], T.act[:], A.mult, ["w0c", "act"], ["tt"]),
+            lambda: tt(T.qq[:], T.tt[:], T.c3[:], A.add, ["tt", "c3"], ["qq"]),
+            lambda: tt(T.ap[:, k18(1)], T.qq[:], T.act[:], A.add, ["qq", "act"], ["ap1"]),
+            lambda: ts(T.ap[:, k18(2)], T.qq[:], 2.0, A.add, ["qq"], ["ap2"]),
+            lambda: cp(T.eo[:], T.ap[:, 18:54], ["ap1", "ap2"], ["eo"])]
 
-    def ahead2(r):
-        tt(T.dg[:, k18(0)], T.df[:, k18(0)], T.act[:], A.mult, ["df0", "act"], ["dg0"])
-        ts(T.a2x[:], T.act[:], 2.0, A.mult, ["act"], ["a2x"])
-        tt(T.ap[:, k18(0)], T.c31[:], T.act[:], A.subtract, ["c31", "act"], ["ap0"])
-        tt(T.bc[:], T.dg[:], wired(r, 0, 3), A.add, keys("dg", 0, 1, 2) + keys("gs", 0, 1, 2), ["bc"])
-        ts(T.dp[:, k18(0)], T.act[:], -2.0, A.mult, ["act"], ["dp0"], 1.0, A.add)
-        ts(T.dp[:, k18(1)], T.tt[:], -1.0, A.add, ["tt"], ["dp1"])
-        tt(T.dp[:, k18(2)], T.tt[:], T.a2x[:], A.add, ["tt", "a2x"], ["dp2"])
-        tt(T.dc[:, k18(0)], T.bc[:, k18(1)], T.bc[:, k18(0)], A.subtract, ["bc"], ["dc0"])
+    def beside(r):
+        return [
+            lambda: tt(T.w0c[:], wired(r, 0, 1), T.c3m[:], A.subtract, ["gs0", "c3m"], ["w0c"]),
+            lambda: tt(T.df[:, 18:54], wired(r, 0, 2), wired(r, 1, 3), A.subtract, keys("gs", 0, 1, 2), ["df1"]),
+            lambda: tt(T.df[:, 0:18], wired(r, 2, 3), wired(r, 0, 1), A.subtract, keys("gs", 0, 2), ["df0"]),
+            lambda: tt(T.dg[:, k18(1)], T.df[:, k18(1)], T.act[:], A.mult, ["df1", "act"], ["dg1"]),
+            lambda: tt(T.dg[:, k18(2)], T.df[:, k18(2)], T.act[:], A.mult, ["df1", "act"], ["dg2"]),
+            lambda: tt(T.dg[:, k18(0)], T.df[:, k18(0)], T.act[:], A.mult, ["df0", "act"], ["dg0"]),
+            lambda: ts(T.a2x[:], T.act[:], 2.0, A.mult, ["act"], ["a2x"]),
+            lambda: tt(T.bc[:], T.dg[:], wired(r, 0, 3), A.add, keys("dg", 0, 1, 2) + keys("gs", 0, 1, 2), ["bc"]),
+            lambda: tt(T.ap[:, k18(0)], T.c31[:], T.act[:], A.subtract, ["c31", "act"], ["ap0"]),
+            lambda: ts(T.dp[:, k18(0)], T.act[:], -2.0, A.mult, ["act"], ["dp0"], 1.0, A.add),
+            lambda: ts(T.dp[:, k18(1)], T.tt[:], -1.0, A.add, ["tt"], ["dp1"]),
+            lambda: tt(T.dp[:, k18(2)], T.tt[:], T.a2x[:], A.add, ["tt", "a2x"], ["dp2"]),
+            lambda: tt(T.dc[:, k18(0)], T.bc[:, k18(1)], T.bc[:, k18(0)], A.subtract, ["bc"], ["dc0"])]
+
+    def take(todo, n):
+        for call in todo[:n]:
+            call()
+        del todo[:n]
 
     def erow():
-        ac(T.er[:], T.gw[:, 0:3 * C].indirect(T.eo[:, 0:36]), keys("gw", 0, 1, 2) + ["eo"], ["er"])
+        for k in range(2):
+            ac(T.er[:, kc(k)], T.gw[:, 0:3 * C].indirect(T.eo[:, k18(k)]), keys("gw", 0, 1, 2) + ["eo"], ["er%d" % k])
 
-    def escan():
-        scan(T.es[:], T.mn[:], T.er[:], ["mn", "er"], ["es"])
+    def escan(k):
+        scan(T.es[:, kc(k)], T.mn[:], T.er[:, kc(k)], ["mn", "er%d" % k], ["es%d" % k])
 
     def ahead3():
-        tt(T.dc[:, 18:54], T.es[:, 15:2 * C:16], T.bc[:, 18:54], A.subtract, ["es", "bc"], ["dc1"])
+        tt(T.dc[:, 18:54], T.es[:, 15:2 * C:16], T.bc[:, 18:54], A.subtract, ["es0", "es1", "bc"], ["dc1"])
 
     def thr():
         ac(T.thr[:], T.t3[:, 0:3 * C].indirect(T.eo[:, 0:18]), ["eo"] + keys("t3", 0, 1, 2), ["thr"])
@@ -254,43 +279,46 @@ def rank_program(g, core, T, topo):
         a, e = CUT[i]
         ac(T.a2[:, k3(0, a, e)], bank(2 * i + 1, e - a), ["b%d" % (2 * i + 1)], ["a2b%d" % i], func=F.Relu)
 
-    agents(T.zi[:], 0, 0, "zi")
-    for k in (1, 2):
-        ac(T.gw[:, k3(k)], T.idn[:, 0:3 * C].indirect(T.off[:, k18(k)]), ["idn", "off"], ["gw%d" % k])
-    ts(T.c31[:], T.c3[:], 1.0, A.add, ["c3"], ["c31"])
-    ahead1(0, T.zi[:], "zi")
-    cp(T.uo[:], T.ui[:], ["ui"], ["uo"])
-    quant(T.uq[:, 0:128], T.us[:, 0:128], T.ut[:, 0:512], ["ut"], ["uq"])
-    cp(T.gw[:, k3(0)], T.idn[:, 0:3 * C].indirect(T.off[:, k18(0)]), ["idn", "off"], ["gw0"])
-    op("s", lambda e: e.activation(T.u2s[:, 0:256], T.us[:, 0:128].indirect(T.uo[:, 0:16]), F.Copy), ["uq", "uo"], ["u2s"])
-    erow()
+    for k in (1, 2, 0):
+        ac(T.gw[:, k3(k)], T.conv[:, 0:3 * C].indirect(T.off[:, k18(k)]), keys("conv", 0, 1, 2) + ["off"], ["gw%d" % k])
+    chain, rest = places(0), beside(0)
+    while chain:
+        take(chain, 1)
+        take(rest, 1 if len(chain) > 1 else 0)
+    if OPT["u2s"] == "s":
+        op("s", lambda e: e.activation(T.u2s[:, 0:256], T.us[:, 0:128].indirect(T.uo[:, 0:16]), F.Copy), ["uq", "uo"], ["u2s"])
     thr()
     op("v", lambda e: e.tensor_copy(T.u2[:, 0:256].bitcast(dt.uint32), T.uq[:, 0:128].bitcast(dt.uint32).indirect(T.uo[:, 0:16])),
        ["uq", "uo"], ["u2"])
+    if OPT["u2s"] == "v":
+        op("v", lambda e: e.tensor_copy(T.u2s[:, 0:256], T.us[:, 0:128].indirect(T.uo[:, 0:16])), ["uq", "uo"], ["u2s"])
     for i in range(2):
         qstate(0, i)
         scores(i)
-    ts(T.mf[:], T.mn[:, 0:C], 1.0 / B, A.mult, ["mn"], ["mf"])
-    ahead2(0)
-    escan()
+    ts(T.mf[:], T.mn[:], 1.0 / B, A.mult, ["mn"], ["mf"])
+    take(rest, 3)
     for i in range(2):
         sign_b(i)
         sign_a(i)
-    ahead3()
+    erow()
+    take(rest, 99)
     for i in range(2):
         halves(0, i)
+    first = [lambda: escan(0), lambda: escan(1), ahead3, lambda: mask(T.fa, T.f0, T.f1, T.m4, 4, "fa"),
+             lambda: cp(T.jo4[:], T.j4[:], ["j4"], ["jo4"]), lambda: cp(T.bcol[:, 0:1], T.j4[:, 0:1], ["j4"], ["bcol"]),
+             lambda: ac(T.mq[:], T.m4[:, 0:4].indirect(T.jo4[:, 0:18]), ["faa", "fab", "jo4"], ["mq"], B4)]
 
     for r in range(3):
         peer = T.cores[rank ^ STEP[r]]
         rid, pid = topo.addr(peer, core)
-        mask = topo.mask(core, peer)
+        engines = topo.mask(core, peer)
         arrive = len(topo.engines(peer, core))
         last = r == 2
 
         def send(dst, src, sem, rd):
             before("g", rd, [])
             g.remote_dma(out_ap=dst, in_ap=src, remote_sem=T.sem[sem], local_sem=T.sem.loc, pid=pid, routing_id=rid,
-                         dma_engine_mask=mask)
+                         dma_engine_mask=engines)
             total["loc"] = total.get("loc", 0) + len(topo.engines(core, peer))
 
         def arrival(sem, key):
@@ -298,66 +326,59 @@ def rank_program(g, core, T, topo):
             snap[(sem, arrive)] = {}
             total[sem] = arrive
         arrival("ra%d" % r, "la")
-        if not OPT["one"]:
-            arrival("rb%d" % r, "lb")
         for i in range(2):
             arrival("rq%d%d" % (i, r), "lq%d" % i)
             arrival("rs%d%d" % (i if OPT["s2"] else 1, r), "ls%d" % i)
-        zl, la, lb = T["zl%d" % r], T["la%d" % r], T["lb%d" % r]
+        ol, la, zl = T["ol%d" % r], T["la%d" % r], T.zl
         lq, ls, qh, sh = T["lq%d" % r], T["ls%d" % r], T["qh%d" % r], T["sh%d" % r]
 
         tt(T.fr[:], T.a2[:, 0:3 * C].indirect(T.eo[:, 0:18]), T.am[:], A.not_equal,
            ["am0", "am1", "a2a0", "a2a1", "a2b0", "a2b1", "a2c", "eo"], ["fr"])
+        take(first, 1)
         scan(T.fs[:], T.mf[:], T.fr[:], ["mf", "fr"], ["fs"])
+        take(first, 1)
 
         fl = T.fs[:, 15:C:16]
         for k in range(3):
             tt(T.sp[:, k18(k)], fl, T.dp[:, k18(k)], A.mult, ["fs", "dp%d" % k], ["sp%d" % k])
+        take(first, 1)
         tt(T.sc[:, k18(1)], fl, T.dc[:, k18(1)], A.mult, ["fs", "dc1"], ["sc1"])
         tt(T.pl[:], T.sp[:], T.ap[:], A.add, keys("sp", 0, 1, 2) + keys("ap", 0, 1, 2), ["pl"])
         tt(T.sc[:, k18(2)], fl, T.dc[:, k18(2)], A.mult, ["fs", "dc1"], ["sc2"])
         tt(T.sc[:, k18(0)], fl, T.dc[:, k18(0)], A.mult, ["fs", "dc0"], ["sc0"])
         cp(T.po[:], T.pl[:], ["pl"], ["po"])
-        tt(T.cl[:, 18:54], T.sc[:, 18:54], T.es[:, 15:2 * C:16], A.add, ["sc1", "sc2", "es"], ["cl1"])
+        tt(T.cl[:, 18:54], T.sc[:, 18:54], T.es[:, 15:2 * C:16], A.add, ["sc1", "sc2", "es0", "es1"], ["cl1"])
         tt(T.cl[:, 0:18], T.sc[:, 0:18], T.bc[:, k18(1)], A.add, ["sc0", "bc"], ["cl0"])
         idn = T.idn[:, 0:3 * C]
         half = 192
         ac(T.tab[:, k3(0)], idn.indirect(T.po[:, k18(0)]), ["idn", "po"], ["tab0"])
         ac(T.tab[:, k3(1, 0, half)], idn.indirect(T.po[:, 18:18 + half // 16]), ["idn", "po"], ["tab1"])
         cp(T.tab[:, k3(2)], idn.indirect(T.po[:, k18(2)]), ["idn", "po"], ["tab2"])
-        ts(T.co[:], T.cl[:], B, A.add, ["cl0", "cl1"], ["co"])
+        ts(T.co[:], T.cl[:], B + 1, A.add, ["cl0", "cl1"], ["co"])
         cp(T.tab[:, k3(1, half, C)], idn.indirect(T.po[:, 18 + half // 16:36]), ["idn", "po"], ["tab3"])
         tab = T.tab[:, 0:3 * C]
         tk = keys("tab", 0, 1, 2, 3) + ["co"]
-        cp(T.gw[:, k3(1)], tab.indirect(T.co[:, k18(1)]), tk, ["gw1"])
-        for k in (2, 0):
+        take(first, 2)
+        gv = OPT["gv"]
+        cp(T.gw[:, k3(gv)], tab.indirect(T.co[:, k18(gv)]), tk, ["gw%d" % gv])
+        for k in (1 - gv, 2):
             ac(T.gw[:, k3(k)], tab.indirect(T.co[:, k18(k)]), tk, ["gw%d" % k])
+        take(first, 2)
 
         def gscan(k):
             scan(T.gs[:, kc(k)], T.mn[:, 0:C], T.gw[:, k3(k)], ["mn", "gw%d" % k], ["gs%d" % k])
 
         def zout(k):
-            agents(zl[:, k18(k)], r + 1, k, "zo%d" % k)
-        gscan(1)
-        zout(1)
-        gscan(2)
-        if OPT["one"]:
-            gscan(0)
-        zout(2)
-        if OPT["one"]:
-            zout(0)
-            send(la[:], zl[:], "ra%d" % r, ["zo0", "zo1", "zo2"])
-        else:
-            send(la[:, 18:54], zl[:, 18:54], "ra%d" % r, ["zo1", "zo2"])
+            agents(zl[:, k18(k - 1)], r + 1, k, "zo%d" % k)
+        chain, rest = ([], []) if last else (places(r + 1), beside(r + 1))
 
-        def hquant(i):
-            a, e = CUT[i]
-            quant(qh[:, a:e], sh[:, a:e], T.h[:, 4 * a:4 * e], ["h%d%d" % (i, b) for b in range(4)], ["qh%d" % i])
-            send(lq[:, a:e].bitcast(dt.uint8), qh[:, a:e].bitcast(dt.uint8), "rq%d%d" % (i, r), ["qh%d" % i])
-            if OPT["s2"]:
-                send(ls[:, a:e], sh[:, a:e], "rs%d%d" % (i, r), ["qh%d" % i])
-            elif i == 1:
-                send(ls[:, 0:C], sh[:, 0:C], "rs%d%d" % (i, r), ["qh0", "qh1"])
+        def olist():
+            ts(ol[:], wired(r + 1, 0, 1), B + 1, A.add, ["gs0"], ["ol"])
+            send(la[:], ol[:], "ra%d" % r, ["ol"])
+        steps = {"0": lambda: gscan(0), "1": lambda: gscan(1), "2": lambda: gscan(2), "o": olist, "a": lambda: zout(1),
+                 "b": lambda: zout(2), "c": lambda: take(chain, 1)}
+        for ch in OPT["go"]:
+            steps[ch]()
 
         def zquant(i):
             a, e = CUT[i]
@@ -373,97 +394,120 @@ def rank_program(g, core, T, topo):
                 ac(T.h[:, 4 * a + b:4 * e:4], bank(k, e - a), ["b%d" % k], ["h%d%d" % (i, b)], 0.03125)
             else:
                 ts(T.h[:, 4 * a + b:4 * e:4], bank(k, e - a), 0.03125, A.mult, ["b%d" % k], ["h%d%d" % (i, b)])
+
+        def mrow():
+            ac(T.mr[:], T.gw[:, 0:3 * C].indirect(la[:, 0:18]), keys("gw", 0, 1, 2) + ["la"], ["mr"], 4.0 / 3, M4)
         for i, (a, e) in enumerate(CUT):
             for b in range(4):
                 xh = T.xh[:, kc(b)]
                 xk = ["xh0%d" % b, "xh1%d" % b]
-                ac(T.zp[:, C * b + a:C * b + e], xh.indirect(zl[:, 18 + a // 16:18 + e // 16]), xk + ["zo1"], ["zp%d%d" % (i, b)])
-                tt(T.z[:, 4 * a + b:4 * e:4], xh.indirect(zl[:, 36 + a // 16:36 + e // 16]),
+                ac(T.zp[:, C * b + a:C * b + e], xh.indirect(zl[:, a // 16:e // 16]), xk + ["zo1"], ["zp%d%d" % (i, b)])
+                tt(T.z[:, 4 * a + b:4 * e:4], xh.indirect(zl[:, 18 + a // 16:18 + e // 16]),
                    T.zp[:, C * b + a:C * b + e], A.add, xk + ["zo2", "zp%d%d" % (i, b)], ["z%d%d" % (i, b)])
                 if (i, b) == (1, 0):
                     zquant(0)
+        if not OPT["late"][r]:
+            mrow()
         for b in range(4):
             hcopy(0, b, "s")
-        if not OPT["one"]:
-            gscan(0)
+        if OPT["late"][r]:
+            mrow()
+        take(rest, 1)
         zquant(1)
-        if not OPT["one"]:
-            zout(0)
-            send(lb[:], zl[:, 0:18], "rb%d" % r, ["zo0"])
-        hquant(0)
-        if last:
-            ts(T.off[:], wired(r + 1, 0, 3), B, A.add, keys("gs", 0, 1, 2), ["off"])
-        else:
-            ts(T.off[:, 0:18], wired(r + 1, 0, 1), B, A.add, ["gs0"], ["off"])
-        for b, q in enumerate("svsv"):
+        scan(T.ms[:], T.mq[:], T.mr[:], ["mq", "mr"], ["ms"])
+        take(chain, 1)
+        ts(T.mo[:], T.ms[:, 3:C:4], B4 - M4, A.add, ["ms", "bcol"], ["mo"], T.bcol[:, 0:1], A.add)
+        for b, q in enumerate(OPT["hq"]):
             hcopy(1, b, q)
-        hquant(1)
+        take(chain, 1)
+
+        hk = ["h%d%d" % (i, b) for i in range(2) for b in range(4)] + ["mo"]
+
+        def hlay(q, a, e):
+            (ac if q == "s" else cp)(T.hp[:, 4 * a:4 * e], T.h[:, 0:4 * C].indirect(T.mo[:, a // 4:e // 4]), hk, ["hp%d" % a])
+
+        def hquant(i, parts):
+            a, e = CUT[i]
+            quant(qh[:, a:e], sh[:, a:e], T.hp[:, 4 * a:4 * e], keys("hp", *parts), ["qh%d" % i])
+            send(lq[:, a:e].bitcast(dt.uint8), qh[:, a:e].bitcast(dt.uint8), "rq%d%d" % (i, r), ["qh%d" % i])
+            if OPT["s2"]:
+                send(ls[:, a:e], sh[:, a:e], "rs%d%d" % (i, r), ["qh%d" % i])
+            elif i == 1:
+                send(ls[:, 0:C], sh[:, 0:C], "rs%d%d" % (i, r), ["qh0", "qh1"])
+        c0, c1, c2, c3 = 0, OPT["sa"], CUT[1][0], CUT[1][0] + OPT["sb"]
+        hlay("s", c0, c1)
+        hlay("v", c1, c2)
+        hlay("s", c2, c3)
+        take(chain, 1)
+        hquant(0, (c0, c1))
+        hlay("v", c3, C)
+        take(chain, 1)
+        hquant(1, (c2, c3))
 
         if r == 0:
             iota(T.unp[:], [[1, C], [C, 3]], 0, 0, ["unp"], True)
-        if r == 0:
-            quant(T.eq[:, 0:512], T.esc[:, 0:512], T.et[:, 0:2048], ["et"], ["eq"])
-        if not last:
-            ahead1(r + 1, zl[:, 0:18], "zo0")
-        for k in (1, 2):
-            ac(T.zt[:, k3(k)], T.idn[:, 0:C].indirect(la[:, k18(k)]), ["idn", "la"], ["zt%d" % k])
-        if not last:
-            erow()
         if last:
+            ts(T.off[:], wired(r + 1, 0, 3), B + 1, A.add, keys("gs", 0, 1, 2), ["off"])
             quant(T.vq[:, 0:128], T.vs[:, 0:128], T.vt[:, 0:512], ["vt"], ["vq"])
-        cp(T.zt[:, k3(0)], T.idn[:, 0:C].indirect(la[:, 0:18]), ["idn", "la"], ["zt0"])
-        if not last:
-            ahead2(r + 1)
-        cp(T.mr[:], T.zt[:, 0:3 * C].indirect(T.off[:, 0:18]), keys("zt", 0, 1, 2) + ["off"], ["mr"])
-        if last:
             ac(T.owt[:], T.unp[:, 0:3 * C].indirect(T.off[:, 0:54]), ["unp", "off"], ["owt"])
-            dma("y", "ow", T.ow[:], T.owt[0:128:16, :], ["owt"], [])
+            dma("y", "out", T.ow[:], T.owt[0:128:16, :], ["owt"], [])
         else:
-            escan()
-        scan(T.ms[:], T.mn[:, 0:C], T.mr[:], ["mn", "mr"], ["ms"])
-        if not last:
-            ahead3()
-        ts(T.mo[:], T.ms[:, 15:C:16], B, A.add, ["ms"], ["mo"])
+            take(chain, 1)
+            take(rest, 1)
+            take(chain, 1)
+            erow()
+            thr()
+            if r == 0:
+                quant(T.eq[:, 0:512], T.esc[:, 0:512], T.et[:, 0:2048], keys("et", 0, 1, 2, 3), ["eq"])
+            take(rest, 99)
+            escan(0)
+            if not OPT["e1"]:
+                escan(1)
 
+        x, y = T["x%d" % r], T["x%d" % (r + 1)]
         for i, (a, e) in enumerate(CUT):
             for b in range(4):
                 k = 4 * i + b
                 mm(k, e - a, T.eq[:, 128 * b:128 * b + 128], T.esc[:, 128 * b:128 * b + 128], lq[:, a:e], ls[:, a:e],
                    ["eq", "lq%d" % i, "ls%d" % i])
-                ac(T.d[:, C * b + a:C * b + e], bank(k, e - a), ["b%d" % k], ["d%d%d" % (i, b)])
-        if not last:
-            thr()
-        x, y = T["x%d" % r], T["x%d" % (r + 1)]
         for i, (a, e) in enumerate(CUT):
             for b in range(4):
-                tt(y[:, 4 * a + b:4 * e:4], T.d[:, kc(b)].indirect(T.mo[:, a // 16:e // 16]), x[:, 4 * a + b:4 * e:4], A.add,
-                   ["d0%d" % b, "d1%d" % b, "mo", "x%d.%d%d" % (r, i, b)], ["x%d.%d%d" % (r + 1, i, b)])
-                if (i, b) == (1, 0):
-                    qstate(r + 1, 0)
-                    if not last:
-                        scores(0)
-                        halves(r + 1, 0)
-                        sign_b(0)
-        if not last:
-            halves(r + 1, 1)
-            qstate(r + 1, 1)
-            sign_a(0)
-            scores(1)
-            sign_b(1)
-            sign_a(1)
+                k = 4 * i + b
+                tt(y[:, 4 * a + b:4 * e:4], bank(k, e - a), x[:, 4 * a + b:4 * e:4], A.add,
+                   ["b%d" % k, "x%d.%d%d" % (r, i, b)], ["x%d.%d%d" % (r + 1, i, b)])
+            if not last and i == 0:
+                if OPT["e1"]:
+                    escan(1)
+                else:
+                    ahead3()
+            if not last and i == 1:
+                if OPT["e1"]:
+                    ahead3()
+                if OPT["a0"]:
+                    sign_a(0)
+            qstate(r + 1, i)
+            if not last:
+                scores(i)
+                if i == 0:
+                    halves(r + 1, i)
+                if i == 1:
+                    if not OPT["a0"]:
+                        sign_a(0)
+                    sign_a(1)
+                sign_b(i)
+                if i == 1:
+                    halves(r + 1, i)
 
     for i, (a, e) in enumerate(CUT):
-        if i == 1:
-            qstate(3, 1)
         mm(i, e - a, T.vq[:, 0:128], T.vs[:, 0:128], T.qx[:, a:e], T.sx[:, a:e], ["vq", "qx%d" % i])
-        dma("y", "oc%d" % i, T.oc[:, 4 * a:4 * e], T.qx[:, a:e].bitcast(dt.uint8), ["qx%d" % i], [])
+        dma("y", "out", T.oc[:, 4 * a:4 * e], T.qx[:, a:e].bitcast(dt.uint8), ["qx%d" % i], [])
         if i == 0:
             ac(T.yt[:, a:e], bank(i, e - a), ["b%d" % i], ["yt%d" % i])
         else:
             cp(T.yt[:, a:e], bank(i, e - a), ["b%d" % i], ["yt%d" % i])
-        dma("s", "y%d" % i, T.y[:, a:e], T.yt[:, a:e], ["yt%d" % i], [])
+        dma("s", "out", T.y[:, a:e], T.yt[:, a:e], ["yt%d" % i], [])
     for k in range(4):
-        dma("y", "os%d" % k, T.osc[4 * k:4 * k + 4, 0:C], T.sx[32 * k:32 * k + 4, 0:C], ["qx0", "qx1"], [])
+        dma("y", "out", T.osc[4 * k:4 * k + 4, 0:C], T.sx[32 * k:32 * k + 4, 0:C], ["qx0", "qx1"], [])
     for s, m in sorted(total.items()):
         if waited.get(s, 0) < m:
             g.wait_ge(T.sem[s], m)

@@ -2,12 +2,13 @@ from concourse.mybir import dt, AluOpType as A, ActivationFunctionType as F
 
 C = 288
 STEP = [4, 1, 2]
-HUGE = 1e29
+LANE = (0, 2, 1)
+TINY = 2.0 ** -93
 B = 1024.0
 B4 = 2048.0
 M4 = 1.5 * 2 ** 25
 CUT = [(0, 160), (160, 288)]
-OPT = {"s2": 1, "sa": 80, "sb": 80, "late": (0, 0, 0), "e1": 0, "a0": 0, "hq": "vvss", "u2s": "s", "gv": 1, "go": "01oa2cbc"}
+OPT = {"sa": 80, "sb": 80, "hq": "vvss", "fs": 160, "go": "01oa2cbc", "l0": 1, "t0": 128}
 
 _f, _b, _i, _u = "float32", "bfloat16", "int32", "uint16"
 _q, _s = "float8_e4m3fn_x4", "uint8"
@@ -23,20 +24,21 @@ def _scratch():
     sb("uq", 128, _q); sb("us", 128, _s); sb("u2", 256, _q); sb("u2s", 256, _s)
     sb("vq", 128, _q); sb("vs", 128, _s)
     sb("ones", 512, _b); sb("et", 2048, _b); sb("eq", 512, _q); sb("esc", 512, _s)
-    sb("idn", 3 * C, _f); sb("unp", 3 * C, _f); sb("t3", 3 * C, _b)
+    sb("j3", C, _f); sb("conv", 3 * C, _f); sb("unp", 3 * C, _f)
     sb("ei", 16, _i); sb("ea", 16, _i); sb("e0", 16, _b); sb("e1", 16, _b); sb("m16", 16, _b)
     sb("fa", 4, _i); sb("f0", 4, _b); sb("f1", 4, _b); sb("m4", 4, _b); sb("j4", 18, _i); sb("jo4", 18, _u); sb("bcol", 8, _f)
-    sb("mf", C, _b); sb("mn", C, _b); sb("mq", C, _b); sb("j3", C, _f); sb("conv", 3 * C, _f)
+    sb("mf", C, _b); sb("mn", C, _b); sb("mq", C, _b)
     sb("i1", 18, _i); sb("i2", 18, _i); sb("i3", 18, _i); sb("i4", 18, _f); sb("io16", 18, _u)
-    sb("c3", 18, _f); sb("c3m", 18, _f); sb("c31", 18, _f); sb("ui", 16, _i); sb("uo", 16, _u)
-    sb("k1", 54, _f); sb("k2", 54, _f); sb("w3", 54, _f); sb("p0", 54, _f); sb("zi", 18, _u); sb("off", 54, _u)
-    for n in ("e3", "act", "w0c", "tt", "qq", "a2x"):
+    sb("c3", 18, _f); sb("c3m", 18, _f); sb("cb", 36, _f); sb("ui", 16, _i); sb("uo", 16, _u)
+    sb("k1", 54, _f); sb("k2", 54, _f); sb("w3", 54, _f); sb("w4", 54, _f); sb("p0", 54, _f); sb("zi", 18, _u); sb("off", 54, _u)
+    for n in ("e3", "w0c", "tt", "qq", "a2x", "cap", "own", "d0"):
         sb(n, 18, _f)
-    for n in ("ap", "dp", "df", "dg", "bc", "dc", "sp", "sc", "pl", "cl"):
+    for n in ("act", "df", "dg"):
         sb(n, 54, _f)
-    sb("eo", 36, _u); sb("po", 54, _u); sb("co", 54, _u); sb("zl", 36, _u)
-    sb("thr", C, _b); sb("a2", 3 * C, _b); sb("am", C, _b); sb("fr", C, _b); sb("fs", C, _b)
-    sb("tab", 3 * C, _f); sb("gw", 3 * C, _f); sb("gs", 3 * C, _f); sb("er", 2 * C, _f); sb("es", 2 * C, _f)
+    sb("ap", 36, _f); sb("fl", 36, _f); sb("pp", 72, _f); sb("pl", 72, _f); sb("pc", 108, _f); sb("cl", 108, _f)
+    sb("eo", 36, _u); sb("po", 36, _u); sb("co", 54, _u); sb("zl", 36, _u)
+    sb("a2", 3 * C, _b); sb("am", C, _b); sb("fr", C, _b); sb("fs", C, _b)
+    sb("tab", 6 * C, _f); sb("gw", 3 * C, _f); sb("gs", 3 * C, _f); sb("er", 2 * C, _f); sb("es", 2 * C, _f)
     sb("mr", C, _f); sb("ms", C, _f); sb("mo", 72, _u)
     for r in range(4):
         sb("x%d" % r, 4 * C, _b)
@@ -92,6 +94,7 @@ def rank_program(g, core, T, topo):
             read[k] = []
 
     def op(q, fn, rd, wr):
+        assert all(k in wrote for k in rd), rd
         before(q, rd, wr)
         count[q] += 1
         fn(queue[q]).then_inc(T.sem["q" + q], 1)
@@ -114,14 +117,11 @@ def rank_program(g, core, T, topo):
     def cp(out, a, rd, wr):
         op("v", lambda e: e.tensor_copy(out, a), rd, wr)
 
-    def fill(out, c, wr):
-        op("v", lambda e: e.memset(out, c), [], wr)
-
     def ac(out, a, rd, wr, scale=1.0, bias=0.0, func=F.Copy):
         op("s", lambda e: e.activation(out, a, func, bias=bias, scale=scale), rd, wr)
 
-    def scan(out, mask, v, rd, wr):
-        op("v", lambda e: e.tensor_tensor_scan(out, v, mask, -B, A.max, A.add), rd, wr)
+    def scan(out, v, add, rd, wr):
+        op("v", lambda e: e.tensor_tensor_scan(out, v, add, -B, A.max, A.add), rd, wr)
 
     def quant(q, s, x, rd, wr):
         op("v", lambda e: e.quantize_mx(q, s, x), rd, wr)
@@ -129,7 +129,7 @@ def rank_program(g, core, T, topo):
     def mm(bank, n, w, ws, x, xs, rd):
         op("t", lambda e: e.matmul_mx(T.ps[:, 512 * bank:512 * bank + n], w, ws, x, xs, True, True), rd, ["b%d" % bank])
 
-    def bank(b, n=C):
+    def bank(b, n):
         return T.ps[:, 512 * b:512 * b + n]
 
     def k18(k):
@@ -138,14 +138,19 @@ def rank_program(g, core, T, topo):
     def kc(k):
         return slice(C * k, C * k + C)
 
-    def k3(k, a=0, e=C):
-        return slice(3 * a + k, 3 * e, 3)
+    def lane(k, a=0, e=C):
+        return slice(3 * a + LANE[k], 3 * e, 3)
 
     def keys(name, *ks):
         return ["%s%s" % (name, k) for k in ks]
 
     def xkeys(r, i):
         return ["x%d.%d%d" % (r, i, b) for b in range(4)]
+
+    def take(todo, n):
+        for call in todo[:n]:
+            call()
+        del todo[:n]
 
     dma("s", "w", T.wi[:], T.wl[:], [], ["wi"])
     dma("y", "u", T.ut[:], T.u[:], [], ["ut"])
@@ -159,20 +164,21 @@ def rank_program(g, core, T, topo):
             op("g", lambda e: e.iota(out, pattern, base, cm, allow_small_or_imprecise_dtypes=True), [], wr)
         else:
             op("g", lambda e: e.iota(out, pattern, base, cm), [], wr)
+    idn = T.tab[:, 3 * C:6 * C]
     iota(T.ei[:], [[1, 16]], 128, -1, ["ei"])
     iota(T.i1[:], [[0, 18]], 0, 1, ["i1"])
-    iota(T.j3[:], [[3, C]], -1, 0, ["j3"], True)
+    iota(T.j3[:], [[3, C]], 0, 0, ["j3"], True)
     iota(T.i2[:], [[48, 18]], 0, 0, ["i2"])
     iota(T.ui[:], [[1, 2], [16, 8]], 0, 0, ["ui"])
-    iota(T.idn[:], [[1, 3 * C]], -1, 0, ["idn"], True)
-    fill(T.ones[:], 1.0, ["ones"])
+    iota(idn, [[1, 3 * C]], -1, 0, ["idn"], True)
+    op("v", lambda e: e.memset(T.ones[:], 1.0), [], ["ones"])
     for b in range(4):
         op("g", lambda e: e.affine_select(T.et[:, 512 * b:512 * b + 512], T.ones[:], [[-1, 512]], A.is_equal, 0.0, b, 4),
            ["ones"], ["et%d" % b])
 
-    def mask(ahead, own, prev, m, n, key):
-        ts(own[:], ahead[:], 0.0, A.is_equal, [key], [key + "0"], 2.0, A.mult)
-        ts(prev[:], ahead[:], n - 1.0, A.is_equal, [key], [key + "1"], -4.0, A.mult)
+    def mask(behind, own, prev, m, n, key):
+        ts(own[:], behind[:], 0.0, A.is_equal, [key], [key + "0"], 2.0, A.mult)
+        ts(prev[:], behind[:], n - 1.0, A.is_equal, [key], [key + "1"], -4.0, A.mult)
         ts(m[:, n - 1:n], own[:, n - 1:n], -3.0, A.add, [key + "0"], [key + "b"])
         tt(m[:, 0:n - 1], own[:, 0:n - 1], prev[:, 0:n - 1], A.add, [key + "0", key + "1"], [key + "a"])
     ts(T.ea[:], T.ei[:], 15, A.bitwise_and, ["ei"], ["ea"])
@@ -181,25 +187,26 @@ def rank_program(g, core, T, topo):
     ts(T.j4[:], T.i1[:], 3, A.bitwise_and, ["i1"], ["j4"])
     mask(T.ea, T.e0, T.e1, T.m16, 16, "ea")
     cp(T.io16[:], T.i3[:], ["i3"], ["io16"])
+    ac(T.a2[:, lane(2)], T.ones[:, 0:C], ["ones"], ["a2c"])
+    ac(T.fl[:, 0:36:2], T.ones[:, 0:18], ["ones"], ["fl0"], 0.0)
+    ac(T.mn[:], T.m16[:, 0:16].indirect(T.io16[:, 0:18]), ["eaa", "eab", "io16"], ["mn"], B)
     for k in range(3):
-        ac(T.t3[:, k3(k)], T.ones[:, 0:C], ["ones"], ["t3%d" % k], 0.0 if k else HUGE)
-    for k in range(3):
-        ac(T.conv[:, kc(k)], T.j3[:], ["j3"], ["conv%d" % k], 1.0, float(k))
+        ac(T.conv[:, kc(k)], T.j3[:], ["j3"], ["conv%d" % k], 1.0, LANE[k] - 1.0)
     ts(T.i4[:], T.i3[:], 3.0, A.mult, ["i3"], ["i4"])
-    ts(T.mn[:], T.m16[:, 0:16].indirect(T.io16[:, 0:18]), B, A.mult, ["eaa", "eab", "io16"], ["mn"])
+    mask(T.fa, T.f0, T.f1, T.m4, 4, "fa")
+    cp(T.jo4[:], T.j4[:], ["j4"], ["jo4"])
+    cp(T.bcol[:, 0:1], T.j4[:, 0:1], ["j4"], ["bcol"])
     tt(T.c3[:], T.i4[:], T.i2[:], A.add, ["i4", "i2"], ["c3"])
     cp(T.uo[:], T.ui[:], ["ui"], ["uo"])
     ts(T.c3m[:], T.c3[:], -B - 1, A.add, ["c3"], ["c3m"])
-    ts(T.c31[:], T.c3[:], 1.0, A.add, ["c3"], ["c31"])
+    ts(T.cb[:, k18(1)], T.c3[:], float(LANE[2]), A.add, ["c3"], ["cb1"])
 
     cp(T.off[:], T.wi[:], ["wi"], ["off"])
-    ts(T.k1[:], T.wi[:], float(C), A.is_ge, ["wi"], ["k1"], 3.0 * C - 1, A.mult)
     ts(T.w3[:], T.wi[:], 3.0, A.mult, ["wi"], ["w3"], -B - 1, A.add)
-    ts(T.k2[:], T.wi[:], 2.0 * C, A.is_ge, ["wi"], ["k2"], 3.0 * C - 1, A.mult)
-    tt(T.w3[:], T.w3[:], T.k1[:], A.subtract, ["w3", "k1"], ["w3"])
-    quant(T.uq[:, 0:128], T.us[:, 0:128], T.ut[:, 0:512], ["ut"], ["uq"])
-    tt(T.p0[:], T.w3[:], T.k2[:], A.subtract, ["w3", "k2"], keys("gs", 0, 1, 2))
-    fill(T.a2[:, k3(2)], 0.0, ["a2c"])
+    ts(T.act[:, k18(0)], T.wi[:, 0:18], float(C), A.is_lt, ["wi"], ["act"])
+    ts(T.k1[:], T.wi[:], float(C), A.is_ge, ["wi"], ["k1"], 3.0 * C - LANE[1], A.mult)
+    tt(T.w0c[:], T.w3[:, 0:18], T.c3m[:], A.subtract, ["w3", "c3m"], ["w0c"])
+    ts(T.k2[:], T.wi[:], 2.0 * C, A.is_ge, ["wi"], ["k2"], 3.0 * C + LANE[1] - LANE[2], A.mult)
 
     def wired(r, a, e):
         return T.p0[:, 18 * a:18 * e] if r == 0 else T.gs[:, C * a + 15:C * e:16]
@@ -207,55 +214,61 @@ def rank_program(g, core, T, topo):
     def agents(out, r, k, key):
         ts(out, wired(r, k, k + 1), 1.0 / 3, A.mult, ["gs%d" % k], [key], B / 3, A.add)
 
+    def step(t, a, e):
+        return t[:, 36 * a:36 * e:2]
+
+    def base(t, a, e):
+        return t[:, 36 * a + 1:36 * e:2]
+
+    act = T.act[:, k18(0)]
+
     def places(r):
         return [
             lambda: agents(T.zi[:], r, 0, "zi"),
             lambda: ts(T.e3[:], T.zi[:], 3.0, A.mult, ["zi"], ["e3"], -B - 1, A.add),
-            lambda: tt(T.act[:], wired(r, 0, 1), T.e3[:], A.is_equal, ["gs0", "e3"], ["act"]),
-            lambda: tt(T.tt[:], T.w0c[:], T.act[:], A.mult, ["w0c", "act"], ["tt"]),
-            lambda: tt(T.qq[:], T.tt[:], T.c3[:], A.add, ["tt", "c3"], ["qq"]),
-            lambda: tt(T.ap[:, k18(1)], T.qq[:], T.act[:], A.add, ["qq", "act"], ["ap1"]),
-            lambda: ts(T.ap[:, k18(2)], T.qq[:], 2.0, A.add, ["qq"], ["ap2"]),
-            lambda: cp(T.eo[:], T.ap[:, 18:54], ["ap1", "ap2"], ["eo"])]
+            lambda: tt(act, wired(r, 0, 1), T.e3[:], A.is_equal, ["gs0", "e3"], ["act"]),
+            lambda: tt(T.tt[:], T.w0c[:], act, A.mult, ["w0c", "act"], ["tt"]),
+            lambda: ts(T.qq[:], act, 2.0, A.mult, ["act"], ["qq"], -1.0, A.add),
+            lambda: tt(T.ap[:, k18(1)], T.tt[:], T.cb[:, k18(1)], A.add, ["tt", "cb1"], ["ap1"]),
+            lambda: tt(T.ap[:, k18(0)], T.ap[:, k18(1)], T.qq[:], A.add, ["qq", "ap1"], ["ap0"]),
+            lambda: cp(T.eo[:], T.ap[:], ["ap0", "ap1"], ["eo"])]
 
     def beside(r):
         return [
             lambda: tt(T.w0c[:], wired(r, 0, 1), T.c3m[:], A.subtract, ["gs0", "c3m"], ["w0c"]),
             lambda: tt(T.df[:, 18:54], wired(r, 0, 2), wired(r, 1, 3), A.subtract, keys("gs", 0, 1, 2), ["df1"]),
-            lambda: tt(T.df[:, 0:18], wired(r, 2, 3), wired(r, 0, 1), A.subtract, keys("gs", 0, 2), ["df0"]),
-            lambda: tt(T.dg[:, k18(1)], T.df[:, k18(1)], T.act[:], A.mult, ["df1", "act"], ["dg1"]),
-            lambda: tt(T.dg[:, k18(2)], T.df[:, k18(2)], T.act[:], A.mult, ["df1", "act"], ["dg2"]),
-            lambda: tt(T.dg[:, k18(0)], T.df[:, k18(0)], T.act[:], A.mult, ["df0", "act"], ["dg0"]),
-            lambda: ts(T.a2x[:], T.act[:], 2.0, A.mult, ["act"], ["a2x"]),
-            lambda: tt(T.bc[:], T.dg[:], wired(r, 0, 3), A.add, keys("dg", 0, 1, 2) + keys("gs", 0, 1, 2), ["bc"]),
-            lambda: tt(T.ap[:, k18(0)], T.c31[:], T.act[:], A.subtract, ["c31", "act"], ["ap0"]),
-            lambda: ts(T.dp[:, k18(0)], T.act[:], -2.0, A.mult, ["act"], ["dp0"], 1.0, A.add),
-            lambda: ts(T.dp[:, k18(1)], T.tt[:], -1.0, A.add, ["tt"], ["dp1"]),
-            lambda: tt(T.dp[:, k18(2)], T.tt[:], T.a2x[:], A.add, ["tt", "a2x"], ["dp2"]),
-            lambda: tt(T.dc[:, k18(0)], T.bc[:, k18(1)], T.bc[:, k18(0)], A.subtract, ["bc"], ["dc0"])]
+            lambda: tt(T.df[:, k18(0)], wired(r, 2, 3), wired(r, 0, 1), A.subtract, keys("gs", 0, 2), ["df0"]),
+            lambda: ts(T.df[:, k18(1)], T.df[:, k18(1)], 3.0 * C + LANE[1], A.add, ["df1"], ["df1"]),
+            lambda: tt(base(T.pp, 0, 2), T.cb[:], T.act[:, 0:36], A.subtract, ["cb0", "cb1", "act", "act1"], ["bp"]),
+            lambda: tt(T.dg[:], T.df[:], T.act[:], A.mult, ["df0", "df1", "act", "act1", "act2"], ["dg"]),
+            lambda: tt(step(T.pp, 0, 2), T.ap[:], base(T.pp, 0, 2), A.subtract, ["ap0", "ap1", "bp"], ["dp"]),
+            lambda: tt(base(T.pc, 0, 3), T.dg[:], wired(r, 0, 3), A.add, ["dg"] + keys("gs", 0, 1, 2), ["bc"]),
+            lambda: tt(T.d0[:], base(T.pc, 1, 2), base(T.pc, 0, 1), A.subtract, ["bc"], ["d0"]),
+            lambda: tt(step(T.pc, 0, 1), T.d0[:], T.a2x[:], A.subtract, ["d0", "a2x"], ["dc0"])]
 
-    def take(todo, n):
-        for call in todo[:n]:
-            call()
-        del todo[:n]
+    def scaled():
+        for k in (1, 2):
+            ac(T.act[:, k18(k)], act, ["act"], ["act%d" % k])
+        ac(T.a2x[:], act, ["act"], ["a2x"], 2.0)
+        ac(T.cap[:], act, ["act"], ["cap"], 4.0, -3.0)
 
-    def erow():
-        for k in range(2):
-            ac(T.er[:, kc(k)], T.gw[:, 0:3 * C].indirect(T.eo[:, k18(k)]), keys("gw", 0, 1, 2) + ["eo"], ["er%d" % k])
+    def erow(k):
+        ac(T.er[:, kc(k)], T.gw[:, 0:3 * C].indirect(T.eo[:, k18(k)]), keys("gw", 0, 1, 2) + ["eo"], ["er%d" % k])
 
     def escan(k):
-        scan(T.es[:, kc(k)], T.mn[:], T.er[:, kc(k)], ["mn", "er%d" % k], ["es%d" % k])
+        scan(T.es[:, kc(k)], T.er[:, kc(k)], T.mn[:], ["mn", "er%d" % k], ["es%d" % k])
 
-    def ahead3():
-        tt(T.dc[:, 18:54], T.es[:, 15:2 * C:16], T.bc[:, 18:54], A.subtract, ["es0", "es1", "bc"], ["dc1"])
+    def esteps():
+        tt(step(T.pc, 1, 3), T.es[:, 15:2 * C:16], base(T.pc, 1, 3), A.subtract, ["es0", "es1", "bc"], ["dc1"])
 
-    def thr():
-        ac(T.thr[:], T.t3[:, 0:3 * C].indirect(T.eo[:, 0:18]), ["eo"] + keys("t3", 0, 1, 2), ["thr"])
-
-    def halves(r, i):
+    def halves(r, i, q="s"):
         a, e = CUT[i]
         for b in range(4):
-            ac(T.xh[:, C * b + a:C * b + e], T["x%d" % r][:, 4 * a + b:4 * e:4], ["x%d.%d%d" % (r, i, b)], ["xh%d%d" % (i, b)], 0.5)
+            out, x, rd, wr = T.xh[:, C * b + a:C * b + e], T["x%d" % r][:, 4 * a + b:4 * e:4], ["x%d.%d%d" % (r, i, b)], ["xh%d%d" % (i, b)]
+            if q == "s":
+                ac(out, x, rd, wr, 0.5)
+            else:
+                ts(out, x, 0.5, A.mult, rd, wr)
 
     def qstate(r, i):
         a, e = CUT[i]
@@ -269,44 +282,62 @@ def rank_program(g, core, T, topo):
 
     def sign_a(i):
         a, e = CUT[i]
-        tt(T.am[:, a:e], bank(2 * i, e - a), T.thr[:, a:e], A.is_gt, ["b%d" % (2 * i), "thr"], ["am%d" % i])
-        if i == 0:
-            ac(T.a2[:, k3(1, a, e)], T.am[:, a:e], ["am%d" % i], ["a2a%d" % i])
-        else:
-            ts(T.a2[:, k3(1, a, e)], bank(2 * i, e - a), 0.0, A.is_gt, ["b%d" % (2 * i)], ["a2a%d" % i])
+        ts(T.a2[:, lane(1, a, e)], bank(2 * i, e - a), 0.0, A.is_gt, ["b%d" % (2 * i)], ["a2a%d" % i])
 
     def sign_b(i):
         a, e = CUT[i]
-        ac(T.a2[:, k3(0, a, e)], bank(2 * i + 1, e - a), ["b%d" % (2 * i + 1)], ["a2b%d" % i], func=F.Relu)
+        ac(T.a2[:, lane(0, a, e)], bank(2 * i + 1, e - a), ["b%d" % (2 * i + 1)], ["a2b%d" % i], bias=-TINY, func=F.Sign)
 
-    for k in (1, 2, 0):
-        ac(T.gw[:, k3(k)], T.conv[:, 0:3 * C].indirect(T.off[:, k18(k)]), keys("conv", 0, 1, 2) + ["off"], ["gw%d" % k])
-    chain, rest = places(0), beside(0)
+    def principal(i):
+        a, e = CUT[i]
+        scan(T.tab[:, lane(0, a, e)], T.j3[:, a:e], T.a2[:, lane(0, a, e)], ["j3", "a2b%d" % i], ["tab0%d" % i])
+
+    def far(q, cut=OPT["fs"]):
+        a, e = (0, cut) if q == "s" else (cut, C)
+        (ac if q == "s" else cp)(T.fr[:, a:e], T.a2[:, 0:3 * C].indirect(T.eo[:, a // 16:e // 16]),
+                                 ["a2a0", "a2a1", "a2b0", "a2b1", "a2c", "eo"], ["fr" + q])
+
+    def arrived(k):
+        (ac if k else cp)(T.gw[:, lane(k)], T.conv[:, 0:3 * C].indirect(T.off[:, k18(k)]), keys("conv", 0, 1, 2) + ["off"],
+                          ["gw%d" % k])
+    arrived(1)
+    arrived(2)
+    chain = places(0)[3:]
+    rest = [lambda: None,
+            lambda: None,
+            lambda: tt(T.w4[:], T.w3[:], T.k1[:], A.subtract, ["w3", "k1"], ["w4"]),
+            lambda: quant(T.uq[:, 0:128], T.us[:, 0:128], T.ut[:, 0:512], ["ut"], ["uq"]),
+            lambda: tt(T.p0[:], T.w4[:], T.k2[:], A.subtract, ["w4", "k2"], keys("gs", 0, 1, 2))] + beside(0)[1:]
     while chain:
         take(chain, 1)
-        take(rest, 1 if len(chain) > 1 else 0)
-    if OPT["u2s"] == "s":
-        op("s", lambda e: e.activation(T.u2s[:, 0:256], T.us[:, 0:128].indirect(T.uo[:, 0:16]), F.Copy), ["uq", "uo"], ["u2s"])
-    thr()
+        take(rest, 1 if chain else 0)
+    op("s", lambda e: e.activation(T.u2s[:, 0:256], T.us[:, 0:128].indirect(T.uo[:, 0:16]), F.Copy), ["uq", "uo"], ["u2s"])
+    scaled()
+    ac(T.cb[:, k18(0)], T.c3[:], ["c3"], ["cb0"], 1.0, float(LANE[1]))
     op("v", lambda e: e.tensor_copy(T.u2[:, 0:256].bitcast(dt.uint32), T.uq[:, 0:128].bitcast(dt.uint32).indirect(T.uo[:, 0:16])),
        ["uq", "uo"], ["u2"])
-    if OPT["u2s"] == "v":
-        op("v", lambda e: e.tensor_copy(T.u2s[:, 0:256], T.us[:, 0:128].indirect(T.uo[:, 0:16])), ["uq", "uo"], ["u2s"])
     for i in range(2):
+        take(rest, 1)
         qstate(0, i)
         scores(i)
-    ts(T.mf[:], T.mn[:], 1.0 / B, A.mult, ["mn"], ["mf"])
-    take(rest, 3)
+    take(rest, 1)
+    arrived(0)
+    take(rest, 1)
+    ts(T.mf[:], T.mn[:], 2.0 / B, A.mult, ["mn"], ["mf"])
     for i in range(2):
         sign_b(i)
-        sign_a(i)
-    erow()
-    take(rest, 99)
+    erow(0)
     for i in range(2):
-        halves(0, i)
-    first = [lambda: escan(0), lambda: escan(1), ahead3, lambda: mask(T.fa, T.f0, T.f1, T.m4, 4, "fa"),
-             lambda: cp(T.jo4[:], T.j4[:], ["j4"], ["jo4"]), lambda: cp(T.bcol[:, 0:1], T.j4[:, 0:1], ["j4"], ["bcol"]),
-             lambda: ac(T.mq[:], T.m4[:, 0:4].indirect(T.jo4[:, 0:18]), ["faa", "fab", "jo4"], ["mq"], B4)]
+        take(rest, 1)
+        sign_a(i)
+    take(rest, 2)
+    principal(0)
+    take(rest, 1)
+    far("s", C)
+    erow(1)
+    halves(0, 0)
+    first = rest + [lambda: escan(0), lambda: halves(0, 1, "v"), lambda: escan(1), esteps, lambda: principal(1),
+                    lambda: ac(T.mq[:], T.m4[:, 0:4].indirect(T.jo4[:, 0:18]), ["faa", "fab", "jo4"], ["mq"], B4)]
 
     for r in range(3):
         peer = T.cores[rank ^ STEP[r]]
@@ -328,45 +359,46 @@ def rank_program(g, core, T, topo):
         arrival("ra%d" % r, "la")
         for i in range(2):
             arrival("rq%d%d" % (i, r), "lq%d" % i)
-            arrival("rs%d%d" % (i if OPT["s2"] else 1, r), "ls%d" % i)
+            arrival("rs%d%d" % (i, r), "ls%d" % i)
         ol, la, zl = T["ol%d" % r], T["la%d" % r], T.zl
         lq, ls, qh, sh = T["lq%d" % r], T["ls%d" % r], T["qh%d" % r], T["sh%d" % r]
 
-        tt(T.fr[:], T.a2[:, 0:3 * C].indirect(T.eo[:, 0:18]), T.am[:], A.not_equal,
-           ["am0", "am1", "a2a0", "a2a1", "a2b0", "a2b1", "a2c", "eo"], ["fr"])
+        scan(T.am[:], T.a2[:, lane(1)], T.mf[:], ["mf", "a2a0", "a2a1"], ["am"])
+        if r:
+            far("v")
+        else:
+            take(first, 2)
+        tt(T.own[:], T.am[:, 15:C:16], T.cap[:], A.min, ["am", "cap"], ["own"])
+        scan(T.fs[:], T.fr[:], T.mf[:], ["mf", "frs"] + (["frv"] if r else []), ["fs"])
         take(first, 1)
-        scan(T.fs[:], T.mf[:], T.fr[:], ["mf", "fr"], ["fs"])
+        tt(T.fl[:, 1:36:2], T.fs[:, 15:C:16], T.own[:], A.not_equal, ["fs", "own"], ["fl"])
         take(first, 1)
+        if r:
+            principal(1)
 
-        fl = T.fs[:, 15:C:16]
-        for k in range(3):
-            tt(T.sp[:, k18(k)], fl, T.dp[:, k18(k)], A.mult, ["fs", "dp%d" % k], ["sp%d" % k])
+        def choose(out, pairs, k, rd, wr):
+            s = slice(36 * k, 36 * k + 36)
+            op("v", lambda e: e.tensor_tensor_scan(out[:, s], T.fl[:], pairs[:, s], 0.0, A.mult, A.add), ["fl", "fl0"] + rd, wr)
+        for k in range(2):
+            choose(T.pl, T.pp, k, ["dp", "bp"], ["pl%d" % k])
         take(first, 1)
-        tt(T.sc[:, k18(1)], fl, T.dc[:, k18(1)], A.mult, ["fs", "dc1"], ["sc1"])
-        tt(T.pl[:], T.sp[:], T.ap[:], A.add, keys("sp", 0, 1, 2) + keys("ap", 0, 1, 2), ["pl"])
-        tt(T.sc[:, k18(2)], fl, T.dc[:, k18(2)], A.mult, ["fs", "dc1"], ["sc2"])
-        tt(T.sc[:, k18(0)], fl, T.dc[:, k18(0)], A.mult, ["fs", "dc0"], ["sc0"])
-        cp(T.po[:], T.pl[:], ["pl"], ["po"])
-        tt(T.cl[:, 18:54], T.sc[:, 18:54], T.es[:, 15:2 * C:16], A.add, ["sc1", "sc2", "es0", "es1"], ["cl1"])
-        tt(T.cl[:, 0:18], T.sc[:, 0:18], T.bc[:, k18(1)], A.add, ["sc0", "bc"], ["cl0"])
-        idn = T.idn[:, 0:3 * C]
-        half = 192
-        ac(T.tab[:, k3(0)], idn.indirect(T.po[:, k18(0)]), ["idn", "po"], ["tab0"])
-        ac(T.tab[:, k3(1, 0, half)], idn.indirect(T.po[:, 18:18 + half // 16]), ["idn", "po"], ["tab1"])
-        cp(T.tab[:, k3(2)], idn.indirect(T.po[:, k18(2)]), ["idn", "po"], ["tab2"])
-        ts(T.co[:], T.cl[:], B + 1, A.add, ["cl0", "cl1"], ["co"])
-        cp(T.tab[:, k3(1, half, C)], idn.indirect(T.po[:, 18 + half // 16:36]), ["idn", "po"], ["tab3"])
-        tab = T.tab[:, 0:3 * C]
-        tk = keys("tab", 0, 1, 2, 3) + ["co"]
-        take(first, 2)
-        gv = OPT["gv"]
-        cp(T.gw[:, k3(gv)], tab.indirect(T.co[:, k18(gv)]), tk, ["gw%d" % gv])
-        for k in (1 - gv, 2):
-            ac(T.gw[:, k3(k)], tab.indirect(T.co[:, k18(k)]), tk, ["gw%d" % k])
+        choose(T.cl, T.pc, 0, ["dc0", "bc"], ["cl0"])
+        cp(T.po[:], T.pl[:, 1:72:2], keys("pl", 0, 1), ["po"])
+        take(first, 1)
+        for k in (1, 2):
+            choose(T.cl, T.pc, k, ["dc1", "bc"], ["cl%d" % k])
+        ac(T.tab[:, lane(1)], idn.indirect(T.po[:, k18(0)]), ["idn", "po"], ["tab1"])
+        cp(T.tab[:, lane(2)], idn.indirect(T.po[:, k18(1)]), ["idn", "po"], ["tab2"])
+        ts(T.co[:], T.cl[:, 1:108:2], B + 1, A.add, keys("cl", 0, 1, 2), ["co"])
+        tab = T.tab[:, 0:6 * C]
+        tk = keys("tab", "00", "01", 1, 2) + ["idn", "co"]
+        cp(T.gw[:, lane(1)], tab.indirect(T.co[:, k18(1)]), tk, ["gw1"])
+        for k in (0, 2):
+            ac(T.gw[:, lane(k)], tab.indirect(T.co[:, k18(k)]), tk, ["gw%d" % k])
         take(first, 2)
 
         def gscan(k):
-            scan(T.gs[:, kc(k)], T.mn[:, 0:C], T.gw[:, k3(k)], ["mn", "gw%d" % k], ["gs%d" % k])
+            scan(T.gs[:, kc(k)], T.gw[:, lane(k)], T.mn[:], ["mn", "gw%d" % k], ["gs%d" % k])
 
         def zout(k):
             agents(zl[:, k18(k - 1)], r + 1, k, "zo%d" % k)
@@ -394,9 +426,6 @@ def rank_program(g, core, T, topo):
                 ac(T.h[:, 4 * a + b:4 * e:4], bank(k, e - a), ["b%d" % k], ["h%d%d" % (i, b)], 0.03125)
             else:
                 ts(T.h[:, 4 * a + b:4 * e:4], bank(k, e - a), 0.03125, A.mult, ["b%d" % k], ["h%d%d" % (i, b)])
-
-        def mrow():
-            ac(T.mr[:], T.gw[:, 0:3 * C].indirect(la[:, 0:18]), keys("gw", 0, 1, 2) + ["la"], ["mr"], 4.0 / 3, M4)
         for i, (a, e) in enumerate(CUT):
             for b in range(4):
                 xh = T.xh[:, kc(b)]
@@ -406,15 +435,12 @@ def rank_program(g, core, T, topo):
                    T.zp[:, C * b + a:C * b + e], A.add, xk + ["zo2", "zp%d%d" % (i, b)], ["z%d%d" % (i, b)])
                 if (i, b) == (1, 0):
                     zquant(0)
-        if not OPT["late"][r]:
-            mrow()
-        for b in range(4):
-            hcopy(0, b, "s")
-        if OPT["late"][r]:
-            mrow()
+        ac(T.mr[:], T.gw[:, 0:3 * C].indirect(la[:, 0:18]), keys("gw", 0, 1, 2) + ["la"], ["mr"], 4.0 / 3, M4)
         take(rest, 1)
         zquant(1)
-        scan(T.ms[:], T.mq[:], T.mr[:], ["mq", "mr"], ["ms"])
+        for b in range(4):
+            hcopy(0, b, "s")
+        scan(T.ms[:], T.mr[:], T.mq[:], ["mq", "mr"], ["ms"])
         take(chain, 1)
         ts(T.mo[:], T.ms[:, 3:C:4], B4 - M4, A.add, ["ms", "bcol"], ["mo"], T.bcol[:, 0:1], A.add)
         for b, q in enumerate(OPT["hq"]):
@@ -430,45 +456,42 @@ def rank_program(g, core, T, topo):
             a, e = CUT[i]
             quant(qh[:, a:e], sh[:, a:e], T.hp[:, 4 * a:4 * e], keys("hp", *parts), ["qh%d" % i])
             send(lq[:, a:e].bitcast(dt.uint8), qh[:, a:e].bitcast(dt.uint8), "rq%d%d" % (i, r), ["qh%d" % i])
-            if OPT["s2"]:
-                send(ls[:, a:e], sh[:, a:e], "rs%d%d" % (i, r), ["qh%d" % i])
-            elif i == 1:
-                send(ls[:, 0:C], sh[:, 0:C], "rs%d%d" % (i, r), ["qh0", "qh1"])
+            send(ls[:, a:e], sh[:, a:e], "rs%d%d" % (i, r), ["qh%d" % i])
         c0, c1, c2, c3 = 0, OPT["sa"], CUT[1][0], CUT[1][0] + OPT["sb"]
         hlay("s", c0, c1)
         hlay("v", c1, c2)
         hlay("s", c2, c3)
-        take(chain, 1)
+        take(chain, 2)
         hquant(0, (c0, c1))
         hlay("v", c3, C)
         take(chain, 1)
         hquant(1, (c2, c3))
 
         if r == 0:
-            iota(T.unp[:], [[1, C], [C, 3]], 0, 0, ["unp"], True)
+            for k in range(3):
+                iota(T.unp[:, lane(k)], [[1, C]], C * k, 0, ["unp%d" % k], True)
         if last:
             ts(T.off[:], wired(r + 1, 0, 3), B + 1, A.add, keys("gs", 0, 1, 2), ["off"])
             quant(T.vq[:, 0:128], T.vs[:, 0:128], T.vt[:, 0:512], ["vt"], ["vq"])
-            ac(T.owt[:], T.unp[:, 0:3 * C].indirect(T.off[:, 0:54]), ["unp", "off"], ["owt"])
+            ac(T.owt[:], T.unp[:, 0:3 * C].indirect(T.off[:, 0:54]), keys("unp", 0, 1, 2) + ["off"], ["owt"])
             dma("y", "out", T.ow[:], T.owt[0:128:16, :], ["owt"], [])
         else:
+            scaled()
             take(chain, 1)
-            take(rest, 1)
-            take(chain, 1)
-            erow()
-            thr()
+            erow(0)
+            erow(1)
             if r == 0:
                 quant(T.eq[:, 0:512], T.esc[:, 0:512], T.et[:, 0:2048], keys("et", 0, 1, 2, 3), ["eq"])
-            take(rest, 99)
+            take(rest, 7)
             escan(0)
-            if not OPT["e1"]:
-                escan(1)
+            take(rest, 1)
+            escan(1)
+            take(rest, 1)
 
         x, y = T["x%d" % r], T["x%d" % (r + 1)]
         for i, (a, e) in enumerate(CUT):
             for b in range(4):
-                k = 4 * i + b
-                mm(k, e - a, T.eq[:, 128 * b:128 * b + 128], T.esc[:, 128 * b:128 * b + 128], lq[:, a:e], ls[:, a:e],
+                mm(4 * i + b, e - a, T.eq[:, 128 * b:128 * b + 128], T.esc[:, 128 * b:128 * b + 128], lq[:, a:e], ls[:, a:e],
                    ["eq", "lq%d" % i, "ls%d" % i])
         for i, (a, e) in enumerate(CUT):
             for b in range(4):
@@ -476,38 +499,28 @@ def rank_program(g, core, T, topo):
                 tt(y[:, 4 * a + b:4 * e:4], bank(k, e - a), x[:, 4 * a + b:4 * e:4], A.add,
                    ["b%d" % k, "x%d.%d%d" % (r, i, b)], ["x%d.%d%d" % (r + 1, i, b)])
             if not last and i == 0:
-                if OPT["e1"]:
-                    escan(1)
-                else:
-                    ahead3()
-            if not last and i == 1:
-                if OPT["e1"]:
-                    ahead3()
-                if OPT["a0"]:
-                    sign_a(0)
+                esteps()
             qstate(r + 1, i)
             if not last:
                 scores(i)
                 if i == 0:
-                    halves(r + 1, i)
-                if i == 1:
-                    if not OPT["a0"]:
-                        sign_a(0)
+                    halves(r + 1, 0)
+                    sign_b(0)
+                else:
+                    sign_a(0)
+                    principal(0)
                     sign_a(1)
-                sign_b(i)
-                if i == 1:
-                    halves(r + 1, i)
+                    sign_b(1)
+                    far("s")
+                    halves(r + 1, 1)
 
     for i, (a, e) in enumerate(CUT):
         mm(i, e - a, T.vq[:, 0:128], T.vs[:, 0:128], T.qx[:, a:e], T.sx[:, a:e], ["vq", "qx%d" % i])
         dma("y", "out", T.oc[:, 4 * a:4 * e], T.qx[:, a:e].bitcast(dt.uint8), ["qx%d" % i], [])
-        if i == 0:
-            ac(T.yt[:, a:e], bank(i, e - a), ["b%d" % i], ["yt%d" % i])
-        else:
-            cp(T.yt[:, a:e], bank(i, e - a), ["b%d" % i], ["yt%d" % i])
+        (cp if i else ac)(T.yt[:, a:e], bank(i, e - a), ["b%d" % i], ["yt%d" % i])
         dma("s", "out", T.y[:, a:e], T.yt[:, a:e], ["yt%d" % i], [])
     for k in range(4):
         dma("y", "out", T.osc[4 * k:4 * k + 4, 0:C], T.sx[32 * k:32 * k + 4, 0:C], ["qx0", "qx1"], [])
-    for s, m in sorted(total.items()):
+    for s, m in sorted(total.items(), reverse=True):
         if waited.get(s, 0) < m:
             g.wait_ge(T.sem[s], m)

@@ -5,12 +5,20 @@ STEP = [4, 1, 2]
 LANE = (0, 2, 1)
 TINY = 2.0 ** -93
 B = 1024.0
+B1 = 4.0
 B4 = 2048.0
-M4 = 1.5 * 2 ** 25
-CUT = [(0, 160), (160, 288)]
-OPT = {"sa": 80, "sb": 80, "hq": "vvss", "fs": 160, "go": "01oa2cbc", "l0": 1, "t0": 128}
+H4 = 4104.0
+H1 = 1100.0
+CUT = [160, 144, 144, 144]
+LAY = [(0, 160), (160, 288)]
+OPT = {"sb": [64, 64, 56], "sm": [0, 0, 0], "fs": 160, "vw": 26, "x": [(0,), (1, 2, 3), (), (0, 1), (2, 3)], "hv": 4, "narrow": (),
+       "gw": [(0, 1, 2), (1, 2, 0), (1, 2, 0)], "g": ["01oa2nb", "12a0bon", "12a0bo"],
+       "z": ["", "", "", "", "", "zi", "e3", "", ""],
+       "h": ["mr s0 s1 s2 s3 tu -- q1 ms -- mo -- s4 v5 s6 v7 --"] * 2 + ["mr s0 s1 s2 s3 q1 ms mo v4 s5 v6 s7"],
+       "s": "sc", "early": "w0c act qq tt ap1 ap0 eo", "fly": ["df bp dg dp es1 bc es0 .. es2 p0 dc p1"] * 2,
+       "fill": {"l0": 1, "l1": 1, "fly": [6, 6], "a0": 1, "a1": 1, "mm": 1, "am": 0, "fs": 1, "fl": 1, "pl": 1}}
 
-_f, _b, _i, _u = "float32", "bfloat16", "int32", "uint16"
+_f, _b, _h, _i, _u = "float32", "bfloat16", "float16", "int32", "uint16"
 _q, _s = "float8_e4m3fn_x4", "uint8"
 
 
@@ -24,22 +32,22 @@ def _scratch():
     sb("uq", 128, _q); sb("us", 128, _s); sb("u2", 256, _q); sb("u2s", 256, _s)
     sb("vq", 128, _q); sb("vs", 128, _s)
     sb("ones", 512, _b); sb("et", 2048, _b); sb("eq", 512, _q); sb("esc", 512, _s)
-    sb("j3", C, _f); sb("conv", 3 * C, _f); sb("unp", 3 * C, _f)
+    sb("vw", 6 * C, _f); sb("unp", 3 * C, _f)
     sb("ei", 16, _i); sb("ea", 16, _i); sb("e0", 16, _b); sb("e1", 16, _b); sb("m16", 16, _b)
     sb("fa", 4, _i); sb("f0", 4, _b); sb("f1", 4, _b); sb("m4", 4, _b); sb("j4", 18, _i); sb("jo4", 18, _u); sb("bcol", 8, _f)
     sb("mf", C, _b); sb("mn", C, _b); sb("mq", C, _b)
-    sb("i1", 18, _i); sb("i2", 18, _i); sb("i3", 18, _i); sb("i4", 18, _f); sb("io16", 18, _u)
-    sb("c3", 18, _f); sb("c3m", 18, _f); sb("cb", 36, _f); sb("ui", 16, _i); sb("uo", 16, _u)
-    sb("k1", 54, _f); sb("k2", 54, _f); sb("w3", 54, _f); sb("w4", 54, _f); sb("p0", 54, _f); sb("zi", 18, _u); sb("off", 54, _u)
-    for n in ("e3", "w0c", "tt", "qq", "a2x", "cap", "own", "d0"):
+    sb("i1", 18, _i); sb("i2", 54, _i); sb("i3", 18, _i); sb("icol", 8, _f); sb("io16", 18, _u); sb("port", 54, _h)
+    sb("c3m", 18, _f); sb("cb", 36, _f); sb("ui", 16, _i); sb("uo", 16, _u)
+    sb("by", 90, _h); sb("zi", 18, _h); sb("off", 54, _u)
+    for n in ("e3", "w0c", "tt", "qq", "a2x", "cap", "own"):
         sb(n, 18, _f)
-    for n in ("act", "df", "dg"):
-        sb(n, 54, _f)
-    sb("ap", 36, _f); sb("fl", 36, _f); sb("pp", 72, _f); sb("pl", 72, _f); sb("pc", 108, _f); sb("cl", 108, _f)
+    for n in ("act", "src", "df", "dg"):
+        sb(n, 54, _h)
+    sb("ap", 36, _f); sb("fl", 108, _h); sb("pp", 72, _h); sb("pl", 72, _h); sb("pc", 108, _h); sb("cl", 108, _h)
     sb("eo", 36, _u); sb("po", 36, _u); sb("co", 54, _u); sb("zl", 36, _u)
-    sb("a2", 3 * C, _b); sb("am", C, _b); sb("fr", C, _b); sb("fs", C, _b)
-    sb("tab", 6 * C, _f); sb("gw", 3 * C, _f); sb("gs", 3 * C, _f); sb("er", 2 * C, _f); sb("es", 2 * C, _f)
-    sb("mr", C, _f); sb("ms", C, _f); sb("mo", 72, _u)
+    sb("a0", 2 * C, _b); sb("a2", 3 * C, _b); sb("am", C, _b); sb("fr", C, _b); sb("fs", C, _b)
+    sb("tab", 6 * C, _f); sb("gh", 3 * C, _h); sb("gw", 3 * C, _f); sb("gs", 3 * C, _h); sb("er", 2 * C, _h); sb("es", 3 * C, _h)
+    sb("mr", C, _h); sb("ms", C, _h); sb("mo", 72, _u)
     for r in range(4):
         sb("x%d" % r, 4 * C, _b)
     sb("qx", C, _q); sb("sx", C, _s); sb("qz", C, _q); sb("sz", C, _s)
@@ -53,7 +61,7 @@ def _scratch():
 
 
 SCRATCH = _scratch()
-_DMAS = ["x", "u", "v", "w", "wc", "ws", "out"]
+_DMAS = ["x0", "x1", "u", "v", "w", "wc", "ws", "out"]
 SEMAPHORES = (["qv", "qs", "qt", "qg", "loc"] + ["d" + n for n in _DMAS] +
               ["r%s%d" % (n, r) for n in ("a", "q0", "q1", "s0", "s1") for r in range(3)])
 
@@ -147,14 +155,18 @@ def rank_program(g, core, T, topo):
     def xkeys(r, i):
         return ["x%d.%d%d" % (r, i, b) for b in range(4)]
 
+    def runs(r):
+        return [(0, CUT[r]), (CUT[r], C)]
+
     def take(todo, n):
         for call in todo[:n]:
             call()
         del todo[:n]
 
-    dma("s", "w", T.wi[:], T.wl[:], [], ["wi"])
     dma("y", "u", T.ut[:], T.u[:], [], ["ut"])
-    dma("y", "x", T.x0[:], T.x[:], [], xkeys(0, 0) + xkeys(0, 1))
+    dma("y", "w", T.wi[:], T.wl[:], [], ["wi"])
+    for i, (a, e) in enumerate(runs(0)):
+        dma("y", "x%d" % i, T.x0[:, 4 * a:4 * e], T.x[:, 4 * a:4 * e], [], xkeys(0, i))
     dma("y", "wc", T.wq[:, 0:512].bitcast(dt.uint8), T.wc[:, 0:2048], ["ut"], ["wq"])
     dma("y", "ws", T.wsc[:, 0:512], T.ws[:, 0:512], [], ["wsc"])
     dma("y", "v", T.vt[:], T.v[:], [], ["vt"])
@@ -165,54 +177,46 @@ def rank_program(g, core, T, topo):
         else:
             op("g", lambda e: e.iota(out, pattern, base, cm), [], wr)
     idn = T.tab[:, 3 * C:6 * C]
+    conv = T.vw[:, 3 * C:6 * C]
     iota(T.ei[:], [[1, 16]], 128, -1, ["ei"])
     iota(T.i1[:], [[0, 18]], 0, 1, ["i1"])
-    iota(T.j3[:], [[3, C]], 0, 0, ["j3"], True)
-    iota(T.i2[:], [[48, 18]], 0, 0, ["i2"])
+    iota(T.i2[:], [[16, 54]], 0, 0, ["i2"])
     iota(T.ui[:], [[1, 2], [16, 8]], 0, 0, ["ui"])
-    iota(idn, [[1, 3 * C]], -1, 0, ["idn"], True)
-    op("v", lambda e: e.memset(T.ones[:], 1.0), [], ["ones"])
-    for b in range(4):
+    for k in (1, 2, 0):
+        iota(T.vw[:, kc(3 + k)], [[3, C]], LANE[k] - 1, 0, ["conv%d" % k], True)
+
+    def unit(b):
         op("g", lambda e: e.affine_select(T.et[:, 512 * b:512 * b + 512], T.ones[:], [[-1, 512]], A.is_equal, 0.0, b, 4),
            ["ones"], ["et%d" % b])
+    op("v", lambda e: e.memset(T.ones[:], 1.0), [], ["ones"])
+    for b in range(3):
+        unit(b)
 
     def mask(behind, own, prev, m, n, key):
-        ts(own[:], behind[:], 0.0, A.is_equal, [key], [key + "0"], 2.0, A.mult)
-        ts(prev[:], behind[:], n - 1.0, A.is_equal, [key], [key + "1"], -4.0, A.mult)
-        ts(m[:, n - 1:n], own[:, n - 1:n], -3.0, A.add, [key + "0"], [key + "b"])
-        tt(m[:, 0:n - 1], own[:, 0:n - 1], prev[:, 0:n - 1], A.add, [key + "0", key + "1"], [key + "a"])
+        return [lambda: ts(own[:], behind[:], 0.0, A.is_equal, [key], [key + "0"], 2.0, A.mult),
+                lambda: ts(prev[:], behind[:], n - 1.0, A.is_equal, [key], [key + "1"], -4.0, A.mult),
+                lambda: ts(m[:, n - 1:n], own[:, n - 1:n], -3.0, A.add, [key + "0"], [key + "b"]),
+                lambda: tt(m[:, 0:n - 1], own[:, 0:n - 1], prev[:, 0:n - 1], A.add, [key + "0", key + "1"], [key + "a"])]
     ts(T.ea[:], T.ei[:], 15, A.bitwise_and, ["ei"], ["ea"])
     ts(T.fa[:], T.ei[:, 3:16:4], 15, A.bitwise_and, ["ei"], ["fa"], 2, A.logical_shift_right)
+    m16, m4 = mask(T.ea, T.e0, T.e1, T.m16, 16, "ea"), mask(T.fa, T.f0, T.f1, T.m4, 4, "fa")
+    take(m16, 2)
     ts(T.i3[:], T.i1[:], 15, A.bitwise_and, ["i1"], ["i3"])
-    ts(T.j4[:], T.i1[:], 3, A.bitwise_and, ["i1"], ["j4"])
-    mask(T.ea, T.e0, T.e1, T.m16, 16, "ea")
+    take(m16, 2)
     cp(T.io16[:], T.i3[:], ["i3"], ["io16"])
-    ac(T.a2[:, lane(2)], T.ones[:, 0:C], ["ones"], ["a2c"])
-    ac(T.fl[:, 0:36:2], T.ones[:, 0:18], ["ones"], ["fl0"], 0.0)
-    ac(T.mn[:], T.m16[:, 0:16].indirect(T.io16[:, 0:18]), ["eaa", "eab", "io16"], ["mn"], B)
-    for k in range(3):
-        ac(T.conv[:, kc(k)], T.j3[:], ["j3"], ["conv%d" % k], 1.0, LANE[k] - 1.0)
-    ts(T.i4[:], T.i3[:], 3.0, A.mult, ["i3"], ["i4"])
-    mask(T.fa, T.f0, T.f1, T.m4, 4, "fa")
+    cp(T.icol[:, 0:1], T.i3[:, 0:1], ["i3"], ["icol"])
+    ts(T.j4[:], T.i1[:], 3, A.bitwise_and, ["i1"], ["j4"])
+    take(m4, 2)
     cp(T.jo4[:], T.j4[:], ["j4"], ["jo4"])
+    take(m4, 2)
+    ts(T.port[:], T.i2[:], T.icol[:, 0:1], A.add, ["i2", "icol"], ["port"])
     cp(T.bcol[:, 0:1], T.j4[:, 0:1], ["j4"], ["bcol"])
-    tt(T.c3[:], T.i4[:], T.i2[:], A.add, ["i4", "i2"], ["c3"])
     cp(T.uo[:], T.ui[:], ["ui"], ["uo"])
-    ts(T.c3m[:], T.c3[:], -B - 1, A.add, ["c3"], ["c3m"])
-    ts(T.cb[:, k18(1)], T.c3[:], float(LANE[2]), A.add, ["c3"], ["cb1"])
+    ac(T.mf[:], T.m16[:, 0:16].indirect(T.io16[:, 0:18]), ["eaa", "eab", "io16"], ["mf"], B1)
+    ac(T.mq[:], T.m4[:, 0:4].indirect(T.jo4[:, 0:18]), ["faa", "fab", "jo4"], ["mq"], B4)
 
-    cp(T.off[:], T.wi[:], ["wi"], ["off"])
-    ts(T.w3[:], T.wi[:], 3.0, A.mult, ["wi"], ["w3"], -B - 1, A.add)
-    ts(T.act[:, k18(0)], T.wi[:, 0:18], float(C), A.is_lt, ["wi"], ["act"])
-    ts(T.k1[:], T.wi[:], float(C), A.is_ge, ["wi"], ["k1"], 3.0 * C - LANE[1], A.mult)
-    tt(T.w0c[:], T.w3[:, 0:18], T.c3m[:], A.subtract, ["w3", "c3m"], ["w0c"])
-    ts(T.k2[:], T.wi[:], 2.0 * C, A.is_ge, ["wi"], ["k2"], 3.0 * C + LANE[1] - LANE[2], A.mult)
-
-    def wired(r, a, e):
-        return T.p0[:, 18 * a:18 * e] if r == 0 else T.gs[:, C * a + 15:C * e:16]
-
-    def agents(out, r, k, key):
-        ts(out, wired(r, k, k + 1), 1.0 / 3, A.mult, ["gs%d" % k], [key], B / 3, A.add)
+    def wired(a, e):
+        return T.gs[:, C * a + 15:C * e:16]
 
     def step(t, a, e):
         return t[:, 36 * a:36 * e:2]
@@ -220,50 +224,9 @@ def rank_program(g, core, T, topo):
     def base(t, a, e):
         return t[:, 36 * a + 1:36 * e:2]
 
-    act = T.act[:, k18(0)]
-
-    def places(r):
-        return [
-            lambda: agents(T.zi[:], r, 0, "zi"),
-            lambda: ts(T.e3[:], T.zi[:], 3.0, A.mult, ["zi"], ["e3"], -B - 1, A.add),
-            lambda: tt(act, wired(r, 0, 1), T.e3[:], A.is_equal, ["gs0", "e3"], ["act"]),
-            lambda: tt(T.tt[:], T.w0c[:], act, A.mult, ["w0c", "act"], ["tt"]),
-            lambda: ts(T.qq[:], act, 2.0, A.mult, ["act"], ["qq"], -1.0, A.add),
-            lambda: tt(T.ap[:, k18(1)], T.tt[:], T.cb[:, k18(1)], A.add, ["tt", "cb1"], ["ap1"]),
-            lambda: tt(T.ap[:, k18(0)], T.ap[:, k18(1)], T.qq[:], A.add, ["qq", "ap1"], ["ap0"]),
-            lambda: cp(T.eo[:], T.ap[:], ["ap0", "ap1"], ["eo"])]
-
-    def beside(r):
-        return [
-            lambda: tt(T.w0c[:], wired(r, 0, 1), T.c3m[:], A.subtract, ["gs0", "c3m"], ["w0c"]),
-            lambda: tt(T.df[:, 18:54], wired(r, 0, 2), wired(r, 1, 3), A.subtract, keys("gs", 0, 1, 2), ["df1"]),
-            lambda: tt(T.df[:, k18(0)], wired(r, 2, 3), wired(r, 0, 1), A.subtract, keys("gs", 0, 2), ["df0"]),
-            lambda: ts(T.df[:, k18(1)], T.df[:, k18(1)], 3.0 * C + LANE[1], A.add, ["df1"], ["df1"]),
-            lambda: tt(base(T.pp, 0, 2), T.cb[:], T.act[:, 0:36], A.subtract, ["cb0", "cb1", "act", "act1"], ["bp"]),
-            lambda: tt(T.dg[:], T.df[:], T.act[:], A.mult, ["df0", "df1", "act", "act1", "act2"], ["dg"]),
-            lambda: tt(step(T.pp, 0, 2), T.ap[:], base(T.pp, 0, 2), A.subtract, ["ap0", "ap1", "bp"], ["dp"]),
-            lambda: tt(base(T.pc, 0, 3), T.dg[:], wired(r, 0, 3), A.add, ["dg"] + keys("gs", 0, 1, 2), ["bc"]),
-            lambda: tt(T.d0[:], base(T.pc, 1, 2), base(T.pc, 0, 1), A.subtract, ["bc"], ["d0"]),
-            lambda: tt(step(T.pc, 0, 1), T.d0[:], T.a2x[:], A.subtract, ["d0", "a2x"], ["dc0"])]
-
-    def scaled():
-        for k in (1, 2):
-            ac(T.act[:, k18(k)], act, ["act"], ["act%d" % k])
-        ac(T.a2x[:], act, ["act"], ["a2x"], 2.0)
-        ac(T.cap[:], act, ["act"], ["cap"], 4.0, -3.0)
-
-    def erow(k):
-        ac(T.er[:, kc(k)], T.gw[:, 0:3 * C].indirect(T.eo[:, k18(k)]), keys("gw", 0, 1, 2) + ["eo"], ["er%d" % k])
-
-    def escan(k):
-        scan(T.es[:, kc(k)], T.er[:, kc(k)], T.mn[:], ["mn", "er%d" % k], ["es%d" % k])
-
-    def esteps():
-        tt(step(T.pc, 1, 3), T.es[:, 15:2 * C:16], base(T.pc, 1, 3), A.subtract, ["es0", "es1", "bc"], ["dc1"])
-
-    def halves(r, i, q="s"):
-        a, e = CUT[i]
-        for b in range(4):
+    def halves(r, i, planes=range(4), q="s"):
+        a, e = runs(r)[i]
+        for b in planes:
             out, x, rd, wr = T.xh[:, C * b + a:C * b + e], T["x%d" % r][:, 4 * a + b:4 * e:4], ["x%d.%d%d" % (r, i, b)], ["xh%d%d" % (i, b)]
             if q == "s":
                 ac(out, x, rd, wr, 0.5)
@@ -271,73 +234,136 @@ def rank_program(g, core, T, topo):
                 ts(out, x, 0.5, A.mult, rd, wr)
 
     def qstate(r, i):
-        a, e = CUT[i]
+        a, e = runs(r)[i]
         quant(T.qx[:, a:e], T.sx[:, a:e], T["x%d" % r][:, 4 * a:4 * e], xkeys(r, i), ["qx%d" % i])
 
-    def scores(i):
-        a, e = CUT[i]
+    def scores(r, i):
+        a, e = runs(r)[i]
         for k in (0, 1):
             mm(2 * i + k, e - a, T.u2[:, 128 * k:128 * k + 128], T.u2s[:, 128 * k:128 * k + 128], T.qx[:, a:e], T.sx[:, a:e],
                ["u2", "u2s", "qx%d" % i])
 
-    def sign_a(i):
-        a, e = CUT[i]
-        ts(T.a2[:, lane(1, a, e)], bank(2 * i, e - a), 0.0, A.is_gt, ["b%d" % (2 * i)], ["a2a%d" % i])
+    def ports(r, k, a=0, e=C):
+        return lane(k, a, e) if r else slice(C * k + a, C * k + e)
 
-    def sign_b(i):
-        a, e = CUT[i]
-        ac(T.a2[:, lane(0, a, e)], bank(2 * i + 1, e - a), ["b%d" % (2 * i + 1)], ["a2b%d" % i], bias=-TINY, func=F.Sign)
+    def signs(r):
+        return T.a2 if r else T.a0
 
-    def principal(i):
-        a, e = CUT[i]
-        scan(T.tab[:, lane(0, a, e)], T.j3[:, a:e], T.a2[:, lane(0, a, e)], ["j3", "a2b%d" % i], ["tab0%d" % i])
+    def sign_a(i, r):
+        a, e = runs(r)[i]
+        ac(signs(r)[:, ports(r, 1, a, e)], bank(2 * i, e - a), ["b%d" % (2 * i)], ["a2a%d" % i], bias=-TINY, func=F.Sign)
 
-    def far(q, cut=OPT["fs"]):
-        a, e = (0, cut) if q == "s" else (cut, C)
-        (ac if q == "s" else cp)(T.fr[:, a:e], T.a2[:, 0:3 * C].indirect(T.eo[:, a // 16:e // 16]),
-                                 ["a2a0", "a2a1", "a2b0", "a2b1", "a2c", "eo"], ["fr" + q])
+    def low(r, i):
+        return 1 if i or r == 0 else 0
 
-    def arrived(k):
-        (ac if k else cp)(T.gw[:, lane(k)], T.conv[:, 0:3 * C].indirect(T.off[:, k18(k)]), keys("conv", 0, 1, 2) + ["off"],
-                          ["gw%d" % k])
-    arrived(1)
-    arrived(2)
-    chain = places(0)[3:]
-    rest = [lambda: None,
-            lambda: None,
-            lambda: tt(T.w4[:], T.w3[:], T.k1[:], A.subtract, ["w3", "k1"], ["w4"]),
-            lambda: quant(T.uq[:, 0:128], T.us[:, 0:128], T.ut[:, 0:512], ["ut"], ["uq"]),
-            lambda: tt(T.p0[:], T.w4[:], T.k2[:], A.subtract, ["w4", "k2"], keys("gs", 0, 1, 2))] + beside(0)[1:]
-    while chain:
-        take(chain, 1)
-        take(rest, 1 if chain else 0)
+    def sign_b(i, r):
+        a, e = runs(r)[i]
+        out, score, rd, wr = signs(r)[:, ports(r, 0, a, e)], bank(2 * i + 1, e - a), ["b%d" % (2 * i + 1)], ["a2b%d" % i]
+        if low(r, i):
+            ts(out, score, 0.0, A.is_le, rd, wr, -2.0, A.mult)
+        else:
+            ac(out, score, rd, wr, bias=-TINY, func=F.Sign)
+
+    def capped(r):
+        for i, (a, e) in enumerate(runs(r)):
+            ac(T.cap[:, a // 16:e // 16], T.act[:, a // 16:e // 16], ["act"], ["cap%d" % i], 2 * B1, -B1 - 1 - low(r, i))
+
+    def principal(r, i):
+        a, e = runs(r)[i]
+        k = 2 - low(r, i)
+        scan(T.tab[:, ports(r, 0, a, e)], T.vw[:, (3 + k) * C + a:(3 + k) * C + e], signs(r)[:, ports(r, 0, a, e)],
+             ["conv%d" % k, "a2b%d" % i], ["tab0%d" % i])
+
+    def far(q, r):
+        a, e = (0, OPT["fs"]) if q == "s" else (OPT["fs"], C)
+        if a < e:
+            (ac if q == "s" else cp)(T.fr[:, a:e], signs(r)[:, 0:(3 if r else 2) * C].indirect(T.eo[:, a // 16:e // 16]),
+                                     ["a2a0", "a2a1", "a2b0", "a2b1", "eo"] + (["a2c"] if r else []), ["fr" + q])
+
+    act = T.act[:, k18(0)]
+    gs = keys("gs", 0, 1, 2)
+
+    def erow(k):
+        ac(T.er[:, kc(k - 1)], T.gw[:, 0:3 * C].indirect(T.eo[:, k18(k - 1)]), keys("gw", 0, 1, 2) + ["eo"], ["er%d" % k])
+
+    def escan(k):
+        scan(T.es[:, kc(k)], T.er[:, kc(k - 1)], T.mn[:], ["mn", "er%d" % k], ["es%d" % k])
+
+    def turned(k):
+        j = (k + 2) % 3
+        ac(T.src[:, k18(k)], wired(j, j + 1), ["gs%d" % j], ["src%d" % k], 1.0, 3.0 * C + LANE[1] if k == 1 else 0.0)
+
+    def ahead(r):
+        return {
+            "zi": lambda: ac(T.zi[:], wired(0, 1), ["gs0"], ["zi"], 1.0 / 3, B / 3 + H1),
+            "e3": lambda: ac(T.e3[:], T.zi[:], ["zi"], ["e3"], 3.0, -3 * H1 - B - 1),
+            "tu": lambda: [turned(k) for k in range(3)],
+            "zv": lambda: ts(T.zi[:], wired(0, 1), 1.0 / 3, A.mult, ["gs0"], ["zi"], B / 3 + H1, A.add),
+            "ev": lambda: ts(T.e3[:], T.zi[:], 3.0, A.mult, ["zi"], ["e3"], -3 * H1 - B - 1, A.add),
+            "qs": lambda: ac(T.qq[:], act, ["act"], ["qq"], 2.0, -1.0),
+            "qq": lambda: ts(T.qq[:], act, 2.0, A.mult, ["act"], ["qq"], -1.0, A.add),
+            "sc": lambda: [ac(T.act[:, k18(1)], act, ["act"], ["act1"]), ac(T.act[:, k18(2)], act, ["act"], ["act2"]),
+                           ac(T.a2x[:], act, ["act"], ["a2x"], 2.0)],
+            "act": lambda: tt(act, wired(0, 1), T.e3[:], A.is_equal, ["gs0", "e3"], ["act"]),
+            "w0c": lambda: tt(T.w0c[:], wired(0, 1), T.c3m[:], A.subtract, ["gs0", "c3m"], ["w0c"]),
+            "tt": lambda: tt(T.tt[:], T.w0c[:], act, A.mult, ["w0c", "act"], ["tt"]),
+            "ap1": lambda: tt(T.ap[:, k18(1)], T.tt[:], T.cb[:, k18(1)], A.add, ["tt", "cb1"], ["ap1"]),
+            "ap0": lambda: tt(T.ap[:, k18(0)], T.ap[:, k18(1)], T.qq[:], A.add, ["qq", "ap1"], ["ap0"]),
+            "eo": lambda: [cp(T.eo[:], T.ap[:], ["ap0", "ap1"], ["eo"]), erow(1), erow(2)],
+            "df": lambda: tt(T.df[:], T.src[:], wired(0, 3), A.subtract, keys("src", 0, 1, 2) + gs, ["df"]),
+            "bp": lambda: tt(base(T.pp, 0, 2), T.cb[:], T.act[:, 0:36], A.subtract, ["cb0", "cb1", "act", "act1"], ["bp"]),
+            "dg": lambda: tt(T.dg[:], T.df[:], T.act[:], A.mult, ["df", "act", "act1", "act2"], ["dg"]),
+            "dp": lambda: tt(step(T.pp, 0, 2), T.ap[:], base(T.pp, 0, 2), A.subtract, ["ap0", "ap1", "bp"], ["dp"]),
+            "bc": lambda: tt(base(T.pc, 0, 3), T.dg[:], wired(0, 3), A.add, ["dg"] + gs, ["bc"]),
+            "es0": lambda: tt(T.es[:, 15:C:16], base(T.pc, 1, 2), T.a2x[:], A.subtract, ["bc", "a2x"], ["es0"]),
+            "es1": lambda: escan(1),
+            "es2": lambda: escan(2),
+            "dc": lambda: tt(step(T.pc, 0, 3), T.es[:, 15:3 * C:16], base(T.pc, 0, 3), A.subtract, keys("es", 0, 1, 2) + ["bc"], ["dc"]),
+            "p0": lambda: principal(r, 0),
+            "p1": lambda: principal(r, 1),
+            "..": lambda: None}
+
+    ts(T.mn[:], T.mf[:], B / B1, A.mult, ["mf"], ["mn"])
+    quant(T.uq[:, 0:128], T.us[:, 0:128], T.ut[:, 0:512], ["ut"], ["uq"])
+    ts(act, T.wi[:, 0:18], float(C), A.is_lt, ["wi"], ["act"])
+    tt(T.w0c[:], T.wi[:, 0:18], T.port[:, k18(0)], A.subtract, ["wi", "port"], ["w0c"])
     op("s", lambda e: e.activation(T.u2s[:, 0:256], T.us[:, 0:128].indirect(T.uo[:, 0:16]), F.Copy), ["uq", "uo"], ["u2s"])
-    scaled()
-    ac(T.cb[:, k18(0)], T.c3[:], ["c3"], ["cb0"], 1.0, float(LANE[1]))
     op("v", lambda e: e.tensor_copy(T.u2[:, 0:256].bitcast(dt.uint32), T.uq[:, 0:128].bitcast(dt.uint32).indirect(T.uo[:, 0:16])),
        ["uq", "uo"], ["u2"])
-    for i in range(2):
-        take(rest, 1)
-        qstate(0, i)
-        scores(i)
-    take(rest, 1)
-    arrived(0)
-    take(rest, 1)
-    ts(T.mf[:], T.mn[:], 2.0 / B, A.mult, ["mn"], ["mf"])
-    for i in range(2):
-        sign_b(i)
-    erow(0)
-    for i in range(2):
-        take(rest, 1)
-        sign_a(i)
-    take(rest, 2)
-    principal(0)
-    take(rest, 1)
-    far("s", C)
-    erow(1)
-    halves(0, 0)
-    first = rest + [lambda: escan(0), lambda: halves(0, 1, "v"), lambda: escan(1), esteps, lambda: principal(1),
-                    lambda: ac(T.mq[:], T.m4[:, 0:4].indirect(T.jo4[:, 0:18]), ["faa", "fab", "jo4"], ["mq"], B4)]
+    qstate(0, 0)
+    scores(0, 0)
+    tt(T.tt[:], T.w0c[:], act, A.mult, ["w0c", "act"], ["tt"])
+    times = (1, -2, 2, 3, -1)
+    ac(T.by[:, k18(0)], act, ["act"], ["by0"], float(C))
+    qstate(0, 1)
+    scores(0, 1)
+    tt(T.own[:], T.tt[:], T.port[:, k18(0)], A.add, ["tt", "port"], ["own"])
+    cp(T.off[:], T.wi[:], ["wi"], ["off"])
+    for k in range(1, 5):
+        ac(T.by[:, k18(k)], act, ["act"], ["by%d" % k], float(times[k] * C))
+    ac(step(T.pp, 0, 1), T.tt[:], ["tt"], ["dp0"], 1.0, -float(C))
+    tt(T.ap[:, k18(0)], T.own[:], T.by[:, k18(0)], A.add, ["own", "by0"], ["ap0"])
+    sign_a(0, 0)
+    sign_b(0, 0)
+    cp(T.eo[:, k18(0)], T.ap[:, k18(0)], ["ap0"], ["eo"])
+    tt(base(T.pp, 0, 2), T.port[:, 18:54], T.by[:, 0:36], A.add, ["port", "by0", "by1"], ["bp"])
+    capped(0)
+    sign_a(1, 0)
+    sign_b(1, 0)
+    halves(0, 0, OPT["x"][0])
+    tt(step(T.pp, 1, 2), T.tt[:], T.by[:, k18(2)], A.add, ["tt", "by2", "dp0"], ["dp"])
+    far("s", 0)
+    ac(T.fl[:, 0:108:2], T.port[:], ["port"], ["fl0"], 0.0)
+    ac(step(T.pc, 0, 1), T.tt[:], ["tt"], ["dc0"], 1.0, float(C))
+    ac(step(T.pc, 1, 2), act, ["act"], ["dc1"], -2.0 * C, -float(C))
+    halves(0, 0, OPT["x"][1])
+    halves(0, 1, OPT["x"][2])
+    todo = [lambda: tt(base(T.pc, 0, 3), T.port[:], T.by[:, 36:90], A.add, ["port", "by2", "by3", "by4"], ["bc"]),
+            lambda: principal(0, 0),
+            lambda: tt(base(T.pc, 1, 2), base(T.pc, 1, 2), T.tt[:], A.add, ["bc", "tt"], ["bc"]),
+            lambda: tt(step(T.pc, 2, 3), T.tt[:], T.by[:, k18(0)], A.add, ["tt", "by0", "dc0", "dc1"], ["dc"]),
+            lambda: principal(0, 1)]
+    fill = OPT["fill"]
 
     for r in range(3):
         peer = T.cores[rank ^ STEP[r]]
@@ -363,70 +389,106 @@ def rank_program(g, core, T, topo):
         ol, la, zl = T["ol%d" % r], T["la%d" % r], T.zl
         lq, ls, qh, sh = T["lq%d" % r], T["ls%d" % r], T["qh%d" % r], T["sh%d" % r]
 
-        scan(T.am[:], T.a2[:, lane(1)], T.mf[:], ["mf", "a2a0", "a2a1"], ["am"])
-        if r:
-            far("v")
-        else:
-            take(first, 2)
-        tt(T.own[:], T.am[:, 15:C:16], T.cap[:], A.min, ["am", "cap"], ["own"])
-        scan(T.fs[:], T.fr[:], T.mf[:], ["mf", "frs"] + (["frv"] if r else []), ["fs"])
-        take(first, 1)
+        scan(T.am[:], signs(r)[:, ports(r, 1)], T.mf[:], ["mf", "a2a0", "a2a1"], ["am"])
+        far("v", r)
+        take(todo, fill["am"])
+        tt(T.own[:], T.am[:, 15:C:16], T.cap[:], A.min, ["am", "cap0", "cap1"], ["own"])
+        take(todo, 0 if r else 1)
+        scan(T.fs[:], T.fr[:], T.mf[:], ["mf", "frs"] + (["frv"] if OPT["fs"] < C else []), ["fs"])
+        take(todo, fill["fs"] if r else 1)
         tt(T.fl[:, 1:36:2], T.fs[:, 15:C:16], T.own[:], A.not_equal, ["fs", "own"], ["fl"])
-        take(first, 1)
-        if r:
-            principal(1)
-
-        def choose(out, pairs, k, rd, wr):
-            s = slice(36 * k, 36 * k + 36)
-            op("v", lambda e: e.tensor_tensor_scan(out[:, s], T.fl[:], pairs[:, s], 0.0, A.mult, A.add), ["fl", "fl0"] + rd, wr)
-        for k in range(2):
-            choose(T.pl, T.pp, k, ["dp", "bp"], ["pl%d" % k])
-        take(first, 1)
-        choose(T.cl, T.pc, 0, ["dc0", "bc"], ["cl0"])
-        cp(T.po[:], T.pl[:, 1:72:2], keys("pl", 0, 1), ["po"])
-        take(first, 1)
         for k in (1, 2):
-            choose(T.cl, T.pc, k, ["dc1", "bc"], ["cl%d" % k])
-        ac(T.tab[:, lane(1)], idn.indirect(T.po[:, k18(0)]), ["idn", "po"], ["tab1"])
-        cp(T.tab[:, lane(2)], idn.indirect(T.po[:, k18(1)]), ["idn", "po"], ["tab2"])
-        ts(T.co[:], T.cl[:, 1:108:2], B + 1, A.add, keys("cl", 0, 1, 2), ["co"])
-        tab = T.tab[:, 0:6 * C]
-        tk = keys("tab", "00", "01", 1, 2) + ["idn", "co"]
-        cp(T.gw[:, lane(1)], tab.indirect(T.co[:, k18(1)]), tk, ["gw1"])
-        for k in (0, 2):
-            ac(T.gw[:, lane(k)], tab.indirect(T.co[:, k18(k)]), tk, ["gw%d" % k])
-        take(first, 2)
+            ac(T.fl[:, 36 * k + 1:36 * k + 36:2], T.fl[:, 1:36:2], ["fl"], ["fl%d" % k])
+        take(todo, fill["fl"] if r else 2)
+        if r == 0:
+            halves(0, 1, OPT["x"][3])
+
+        def choose(out, f, pairs, rd, wr):
+            op("v", lambda e: e.tensor_tensor_scan(out, f, pairs, 0.0, A.mult, A.add), ["fl", "fl0"] + rd, wr)
+        for k in range(2):
+            s = slice(36 * k, 36 * k + 36)
+            choose(T.pl[:, s], T.fl[:, 0:36], T.pp[:, s], ["dp", "bp"], ["pl%d" % k])
+        take(todo, fill["pl"])
+        cp(T.po[:], T.pl[:, 1:72:2], keys("pl", 0, 1), ["po"])
+        own, ik = (idn, ["idn"]) if r else (conv, keys("conv", 0, 1, 2))
+        ac(T.tab[:, ports(r, 1)], own.indirect(T.po[:, k18(0)]), ik + ["po"], ["tab1"])
+        take(todo, 9)
+        choose(T.cl[:], T.fl[:], T.pc[:], ["fl1", "fl2", "dc", "bc"], ["cl"])
+        cp(T.tab[:, ports(r, 2)], own.indirect(T.po[:, k18(1)]), ik + ["po"], ["tab2"])
+        ts(T.co[:], T.cl[:, 1:108:2], B + 1 if r else 0.0, A.add, ["cl"], ["co"])
+        tab, tk = T.tab[:, 0:6 * C], keys("tab", "00", "01", 1, 2)
+        if r == 0:
+            cut = OPT["vw"]
+            ac(T.vw[:, 0:16 * cut], T.tab[:, 0:3 * C].indirect(T.off[:, 0:cut]), tk + ["off"], ["vws"])
+            cp(T.vw[:, 16 * cut:3 * C], T.tab[:, 0:3 * C].indirect(T.off[:, cut:54]), tk + ["off"], ["vwv"])
+            tab, tk = T.vw[:, 0:6 * C], ["vws", "vwv"]
+            halves(0, 1, OPT["x"][4], "v")
+        else:
+            halves(r, 1, range(OPT["hv"], 4))
+        for k, by in zip(OPT["gw"][r], (cp, ac, ac)):
+            out, key = (T.gh[:, kc(k)], "gh%d" % k) if k in OPT["narrow"] else (T.gw[:, lane(k)], "gw%d" % k)
+            by(out, tab.indirect(T.co[:, k18(k)]), tk + ik + ["co"], [key])
+        if r == 0:
+            ac(T.c3m[:], T.port[:, k18(0)], ["port"], ["c3m"], 3.0, -B - 1)
+            for k in (0, 1):
+                ac(T.cb[:, k18(k)], T.port[:, k18(0)], ["port"], ["cb%d" % k], 3.0, float(LANE[k + 1]))
+        nxt = {} if last else ahead(r + 1)
+        todo = [] if last else [nxt[n] for n in OPT["early"].split()]
 
         def gscan(k):
-            scan(T.gs[:, kc(k)], T.gw[:, lane(k)], T.mn[:], ["mn", "gw%d" % k], ["gs%d" % k])
+            row, key = (T.gh[:, kc(k)], "gh%d" % k) if k in OPT["narrow"] else (T.gw[:, lane(k)], "gw%d" % k)
+            scan(T.gs[:, kc(k)], row, T.mn[:], ["mn", key], ["gs%d" % k])
 
-        def zout(k):
-            agents(zl[:, k18(k - 1)], r + 1, k, "zo%d" % k)
-        chain, rest = ([], []) if last else (places(r + 1), beside(r + 1))
+        def agents(k):
+            ts(zl[:, k18(k - 1)], wired(k, k + 1), 1.0 / 3, A.mult, ["gs%d" % k], ["zo%d" % k], B / 3, A.add)
 
-        def olist():
-            ts(ol[:], wired(r + 1, 0, 1), B + 1, A.add, ["gs0"], ["ol"])
+        def ask():
+            ts(ol[:], wired(0, 1), B + 1, A.add, ["gs0"], ["ol"])
             send(la[:], ol[:], "ra%d" % r, ["ol"])
-        steps = {"0": lambda: gscan(0), "1": lambda: gscan(1), "2": lambda: gscan(2), "o": olist, "a": lambda: zout(1),
-                 "b": lambda: zout(2), "c": lambda: take(chain, 1)}
-        for ch in OPT["go"]:
-            steps[ch]()
+        steps = {"0": lambda: gscan(0), "1": lambda: gscan(1), "2": lambda: gscan(2), "o": ask, "n": lambda: take(todo, 1),
+                 "a": lambda: agents(1), "b": lambda: agents(2)}
+        for name in OPT["g"][r]:
+            steps[name]()
+        if r == 0:
+            unit(3)
 
         def zquant(i):
-            a, e = CUT[i]
+            a, e = LAY[i]
             quant(T.qz[:, a:e], T.sz[:, a:e], T.z[:, 4 * a:4 * e], keys("z%d" % i, 0, 1, 2, 3), ["qz%d" % i])
             for b in range(4):
                 mm(4 - 4 * i + b, e - a, T.wq[:, 128 * b:128 * b + 128], T.wsc[:, 128 * b:128 * b + 128], T.qz[:, a:e],
                    T.sz[:, a:e], ["wq", "wsc", "qz%d" % i])
 
-        def hcopy(i, b, q):
-            a, e = CUT[i]
+        def hcopy(q, n):
+            i, b = divmod(n, 4)
+            a, e = LAY[i]
             k = 4 - 4 * i + b
             if q == "s":
                 ac(T.h[:, 4 * a + b:4 * e:4], bank(k, e - a), ["b%d" % k], ["h%d%d" % (i, b)], 0.03125)
             else:
                 ts(T.h[:, 4 * a + b:4 * e:4], bank(k, e - a), 0.03125, A.mult, ["b%d" % k], ["h%d%d" % (i, b)])
-        for i, (a, e) in enumerate(CUT):
+
+        def widen(k):
+            if k in OPT["narrow"]:
+                ac(T.gw[:, lane(k)], T.gh[:, kc(k)], ["gh%d" % k], ["gw%d" % k])
+        steps = {
+            "mr": lambda: ac(T.mr[:], T.gw[:, 0:3 * C].indirect(la[:, 0:18]), keys("gw", 0, 1, 2) + ["la"], ["mr"], 4.0 / 3, H4),
+            "ms": lambda: scan(T.ms[:], T.mr[:], T.mq[:], ["mq", "mr"], ["ms"]),
+            "mo": lambda: ts(T.mo[:], T.ms[:, 3:C:4], B4 - H4, A.add, ["ms", "bcol"], ["mo"], T.bcol[:, 0:1], A.add),
+            "q1": lambda: zquant(1),
+            "w0": lambda: widen(0), "w1": lambda: widen(1), "w2": lambda: widen(2),
+            "--": lambda: take(todo, 1)}
+
+        def run(names):
+            for name in names.split():
+                if name in steps:
+                    steps[name]()
+                elif name[0] in "sv" and name[1].isdigit():
+                    hcopy(name[0], int(name[1]))
+                elif not last:
+                    nxt[name]()
+        run(OPT["z"][0])
+        for i, (a, e) in enumerate(LAY):
             for b in range(4):
                 xh = T.xh[:, kc(b)]
                 xk = ["xh0%d" % b, "xh1%d" % b]
@@ -435,17 +497,8 @@ def rank_program(g, core, T, topo):
                    T.zp[:, C * b + a:C * b + e], A.add, xk + ["zo2", "zp%d%d" % (i, b)], ["z%d%d" % (i, b)])
                 if (i, b) == (1, 0):
                     zquant(0)
-        ac(T.mr[:], T.gw[:, 0:3 * C].indirect(la[:, 0:18]), keys("gw", 0, 1, 2) + ["la"], ["mr"], 4.0 / 3, M4)
-        take(rest, 1)
-        zquant(1)
-        for b in range(4):
-            hcopy(0, b, "s")
-        scan(T.ms[:], T.mr[:], T.mq[:], ["mq", "mr"], ["ms"])
-        take(chain, 1)
-        ts(T.mo[:], T.ms[:, 3:C:4], B4 - M4, A.add, ["ms", "bcol"], ["mo"], T.bcol[:, 0:1], A.add)
-        for b, q in enumerate(OPT["hq"]):
-            hcopy(1, b, q)
-        take(chain, 1)
+                run(OPT["z"][4 * i + b + 1])
+        run(OPT["h"][r])
 
         hk = ["h%d%d" % (i, b) for i in range(2) for b in range(4)] + ["mo"]
 
@@ -453,74 +506,78 @@ def rank_program(g, core, T, topo):
             (ac if q == "s" else cp)(T.hp[:, 4 * a:4 * e], T.h[:, 0:4 * C].indirect(T.mo[:, a // 4:e // 4]), hk, ["hp%d" % a])
 
         def hquant(i, parts):
-            a, e = CUT[i]
+            a, e = runs(r + 1)[i]
             quant(qh[:, a:e], sh[:, a:e], T.hp[:, 4 * a:4 * e], keys("hp", *parts), ["qh%d" % i])
             send(lq[:, a:e].bitcast(dt.uint8), qh[:, a:e].bitcast(dt.uint8), "rq%d%d" % (i, r), ["qh%d" % i])
             send(ls[:, a:e], sh[:, a:e], "rs%d%d" % (i, r), ["qh%d" % i])
-        c0, c1, c2, c3 = 0, OPT["sa"], CUT[1][0], CUT[1][0] + OPT["sb"]
+        c0, c1, c2, c3 = 0, CUT[r + 1] // 16 * 8, CUT[r + 1], C - OPT["sb"][r]
         hlay("s", c0, c1)
         hlay("v", c1, c2)
         hlay("s", c2, c3)
-        take(chain, 2)
+        run(OPT["s"])
+        cm = C - OPT["sm"][r]
+        if cm < C:
+            hlay("v", cm, C)
+        take(todo, fill["l0"])
         hquant(0, (c0, c1))
-        hlay("v", c3, C)
-        take(chain, 1)
-        hquant(1, (c2, c3))
+        if c3 < cm:
+            hlay("v", c3, cm)
+        take(todo, fill["l1"])
+        hquant(1, [c for c in (c2, c3, cm) if c < C])
 
         if r == 0:
+            iota(idn, [[1, 3 * C]], -1, 0, ["idn"], True)
+        if r == 1:
             for k in range(3):
                 iota(T.unp[:, lane(k)], [[1, C]], C * k, 0, ["unp%d" % k], True)
         if last:
-            ts(T.off[:], wired(r + 1, 0, 3), B + 1, A.add, keys("gs", 0, 1, 2), ["off"])
+            ts(T.off[:], wired(0, 3), B + 1, A.add, gs, ["off"])
             quant(T.vq[:, 0:128], T.vs[:, 0:128], T.vt[:, 0:512], ["vt"], ["vq"])
             ac(T.owt[:], T.unp[:, 0:3 * C].indirect(T.off[:, 0:54]), keys("unp", 0, 1, 2) + ["off"], ["owt"])
             dma("y", "out", T.ow[:], T.owt[0:128:16, :], ["owt"], [])
         else:
-            scaled()
-            take(chain, 1)
-            erow(0)
-            erow(1)
+            take(todo, 9)
+            todo = [nxt[n] for n in OPT["fly"][r].split()]
             if r == 0:
                 quant(T.eq[:, 0:512], T.esc[:, 0:512], T.et[:, 0:2048], keys("et", 0, 1, 2, 3), ["eq"])
-            take(rest, 7)
-            escan(0)
-            take(rest, 1)
-            escan(1)
-            take(rest, 1)
+            take(todo, fill["fly"][r])
+            capped(r + 1)
+            if r == 0:
+                ac(T.a2[:, lane(2)], T.mf[:], ["mf"], ["a2c"])
 
         x, y = T["x%d" % r], T["x%d" % (r + 1)]
-        for i, (a, e) in enumerate(CUT):
+        for i, (a, e) in enumerate(runs(r + 1)):
             for b in range(4):
                 mm(4 * i + b, e - a, T.eq[:, 128 * b:128 * b + 128], T.esc[:, 128 * b:128 * b + 128], lq[:, a:e], ls[:, a:e],
                    ["eq", "lq%d" % i, "ls%d" % i])
-        for i, (a, e) in enumerate(CUT):
+        for i, (a, e) in enumerate(runs(r + 1)):
             for b in range(4):
                 k = 4 * i + b
                 tt(y[:, 4 * a + b:4 * e:4], bank(k, e - a), x[:, 4 * a + b:4 * e:4], A.add,
                    ["b%d" % k, "x%d.%d%d" % (r, i, b)], ["x%d.%d%d" % (r + 1, i, b)])
-            if not last and i == 0:
-                esteps()
+            take(todo, fill["a%d" % i])
             qstate(r + 1, i)
             if not last:
-                scores(i)
+                scores(r + 1, i)
                 if i == 0:
                     halves(r + 1, 0)
-                    sign_b(0)
+                    sign_b(0, r + 1)
+                    sign_a(0, r + 1)
                 else:
-                    sign_a(0)
-                    principal(0)
-                    sign_a(1)
-                    sign_b(1)
-                    far("s")
-                    halves(r + 1, 1)
+                    take(todo, fill["mm"])
+                    sign_a(1, r + 1)
+                    sign_b(1, r + 1)
+                    far("s", r + 1)
+                    halves(r + 1, 1, range(OPT["hv"]))
 
-    for i, (a, e) in enumerate(CUT):
+    for i, (a, e) in enumerate(runs(3)):
         mm(i, e - a, T.vq[:, 0:128], T.vs[:, 0:128], T.qx[:, a:e], T.sx[:, a:e], ["vq", "qx%d" % i])
         dma("y", "out", T.oc[:, 4 * a:4 * e], T.qx[:, a:e].bitcast(dt.uint8), ["qx%d" % i], [])
         (cp if i else ac)(T.yt[:, a:e], bank(i, e - a), ["b%d" % i], ["yt%d" % i])
+        if i:
+            for k in range(4):
+                dma("ys"[k % 2], "out", T.osc[4 * k:4 * k + 4, 0:C], T.sx[32 * k:32 * k + 4, 0:C], ["qx0", "qx1"], [])
         dma("s", "out", T.y[:, a:e], T.yt[:, a:e], ["yt%d" % i], [])
-    for k in range(4):
-        dma("y", "out", T.osc[4 * k:4 * k + 4, 0:C], T.sx[32 * k:32 * k + 4, 0:C], ["qx0", "qx1"], [])
     for s, m in sorted(total.items(), reverse=True):
         if waited.get(s, 0) < m:
             g.wait_ge(T.sem[s], m)

from concourse.mybir import dt, AluOpType as A, ActivationFunctionType as F

C = 288
STEP = [4, 1, 2]
LANE = (0, 2, 1)
TINY = 2.0 ** -93
B = 1024.0
B1 = 4.0
B4 = 2048.0
H4 = 4104.0
H1 = 1100.0
CUT = [160, 144, 144, 144]
LAY = [(0, 160), (160, 288)]
OPT = {"sb": [64, 64, 56], "sm": [0, 0, 0], "fs": 160, "vw": 26, "x": [(0,), (1, 2, 3), (), (0, 1), (2, 3)], "hv": 4, "narrow": (),
       "gw": [(0, 1, 2), (1, 2, 0), (1, 2, 0)], "g": ["01oa2nb", "12a0bon", "12a0bo"],
       "z": ["", "", "", "", "", "zi", "e3", "", ""],
       "h": ["mr s0 s1 s2 s3 tu -- q1 ms -- mo -- s4 v5 s6 v7 --"] * 2 + ["mr s0 s1 s2 s3 q1 ms mo v4 s5 v6 s7"],
       "s": "sc", "early": "w0c act qq tt ap1 ap0 eo", "fly": ["df bp dg dp es1 bc es0 .. es2 p0 dc p1"] * 2,
       "fill": {"l0": 1, "l1": 1, "fly": [6, 6], "a0": 1, "a1": 1, "mm": 1, "am": 0, "fs": 1, "fl": 1, "pl": 1}}

_f, _b, _h, _i, _u = "float32", "bfloat16", "float16", "int32", "uint16"
_q, _s = "float8_e4m3fn_x4", "uint8"


def _scratch():
    d = {}

    def sb(name, n, t):
        d[name] = ("sbuf", [128, n], t)
    sb("ut", 512, _b); sb("vt", 512, _b); sb("wi", 54, _i)
    sb("wq", 512, _q); sb("wsc", 512, _s)
    sb("uq", 128, _q); sb("us", 128, _s); sb("u2", 256, _q); sb("u2s", 256, _s)
    sb("vq", 128, _q); sb("vs", 128, _s)
    sb("ones", 512, _b); sb("et", 2048, _b); sb("eq", 512, _q); sb("esc", 512, _s)
    sb("vw", 6 * C, _f); sb("unp", 3 * C, _f)
    sb("ei", 16, _i); sb("ea", 16, _i); sb("e0", 16, _b); sb("e1", 16, _b); sb("m16", 16, _b)
    sb("fa", 4, _i); sb("f0", 4, _b); sb("f1", 4, _b); sb("m4", 4, _b); sb("j4", 18, _i); sb("jo4", 18, _u); sb("bcol", 8, _f)
    sb("mf", C, _b); sb("mn", C, _b); sb("mq", C, _b)
    sb("i1", 18, _i); sb("i2", 54, _i); sb("i3", 18, _i); sb("icol", 8, _f); sb("io16", 18, _u); sb("port", 54, _h)
    sb("c3m", 18, _f); sb("cb", 36, _f); sb("ui", 16, _i); sb("uo", 16, _u)
    sb("by", 90, _h); sb("zi", 18, _h); sb("off", 54, _u)
    for n in ("e3", "w0c", "tt", "qq", "a2x", "cap", "own"):
        sb(n, 18, _f)
    for n in ("act", "src", "df", "dg"):
        sb(n, 54, _h)
    sb("ap", 36, _f); sb("fl", 108, _h); sb("pp", 72, _h); sb("pl", 72, _h); sb("pc", 108, _h); sb("cl", 108, _h)
    sb("eo", 36, _u); sb("po", 36, _u); sb("co", 54, _u); sb("zl", 36, _u)
    sb("a0", 2 * C, _b); sb("a2", 3 * C, _b); sb("am", C, _b); sb("fr", C, _b); sb("fs", C, _b)
    sb("tab", 6 * C, _f); sb("gh", 3 * C, _h); sb("gw", 3 * C, _f); sb("gs", 3 * C, _h); sb("er", 2 * C, _h); sb("es", 3 * C, _h)
    sb("mr", C, _h); sb("ms", C, _h); sb("mo", 72, _u)
    for r in range(4):
        sb("x%d" % r, 4 * C, _b)
    sb("qx", C, _q); sb("sx", C, _s); sb("qz", C, _q); sb("sz", C, _s)
    sb("xh", 4 * C, _b); sb("zp", 4 * C, _b); sb("z", 4 * C, _b); sb("h", 4 * C, _b); sb("hp", 4 * C, _b)
    for r in range(3):
        sb("ol%d" % r, 18, _u); sb("la%d" % r, 18, _u)
        sb("qh%d" % r, C, _q); sb("sh%d" % r, C, _s); sb("lq%d" % r, C, _q); sb("ls%d" % r, C, _s)
    sb("yt", C, _f); sb("owt", 3 * C, _f)
    d["ps"] = ("psum", [128, 4096], _f)
    return d


SCRATCH = _scratch()
_DMAS = ["x0", "x1", "u", "v", "w", "wc", "ws", "out"]
SEMAPHORES = (["qv", "qs", "qt", "qg", "loc"] + ["d" + n for n in _DMAS] +
              ["r%s%d" % (n, r) for n in ("a", "q0", "q1", "s0", "s1") for r in range(3)])


def rank_program(g, core, T, topo):
    rank = T.rank_of(core)
    if rank is None:
        return
    queue = {"v": g.vector, "s": g.scalar, "t": g.tensor, "g": g, "y": g.sync}
    count = {"v": 0, "s": 0, "t": 0, "g": 0}
    known = {q: {} for q in queue}
    snap, wrote, read, total, waited = {}, {}, {}, {}, {}

    def before(q, rd, wr):
        deps = set(wrote[k] for k in rd if k in wrote)
        for k in wr:
            deps |= set(w for w in [wrote.get(k)] + read.get(k, []) if w)
        best = {}
        for s, n in deps:
            if n > known[q].get(s, 0):
                best[s] = max(n, best.get(s, 0))
        for s, n in sorted(best.items()):
            if any(o != s and snap.get((o, m), {}).get(s, 0) >= n for o, m in best.items()):
                continue
            queue[q].wait_ge(T.sem[s], n)
            waited[s] = max(n, waited.get(s, 0))
            known[q][s] = n
            for o, m in snap.get((s, n), {}).items():
                known[q][o] = max(m, known[q].get(o, 0))

    def after(q, tag, rd, wr):
        snap[tag] = dict(known[q])
        total[tag[0]] = max(total.get(tag[0], 0), tag[1])
        for k in rd:
            read.setdefault(k, []).append(tag)
        for k in wr:
            wrote[k] = tag
            read[k] = []

    def op(q, fn, rd, wr):
        assert all(k in wrote for k in rd), rd
        before(q, rd, wr)
        count[q] += 1
        fn(queue[q]).then_inc(T.sem["q" + q], 1)
        after(q, ("q" + q, count[q]), rd, wr)

    def dma(q, name, out, in_, rd, wr):
        before(q, rd, wr)
        queue[q].dma_start(out, in_).then_inc(T.sem["d" + name], 16)
        after(q, ("d" + name, 16 + total.get("d" + name, 0)), rd, wr)

    def tt(out, a, b, o, rd, wr):
        op("v", lambda e: e.tensor_tensor(out, a, b, o), rd, wr)

    def ts(out, a, s1, o1, rd, wr, s2=None, o2=None):
        if o2 is None:
            op("v", lambda e: e.tensor_scalar(out, a, s1, None, o1), rd, wr)
        else:
            op("v", lambda e: e.tensor_scalar(out, a, s1, s2, o1, o2), rd, wr)

    def cp(out, a, rd, wr):
        op("v", lambda e: e.tensor_copy(out, a), rd, wr)

    def ac(out, a, rd, wr, scale=1.0, bias=0.0, func=F.Copy):
        op("s", lambda e: e.activation(out, a, func, bias=bias, scale=scale), rd, wr)

    def scan(out, v, add, rd, wr):
        op("v", lambda e: e.tensor_tensor_scan(out, v, add, -B, A.max, A.add), rd, wr)

    def quant(q, s, x, rd, wr):
        op("v", lambda e: e.quantize_mx(q, s, x), rd, wr)

    def mm(bank, n, w, ws, x, xs, rd):
        op("t", lambda e: e.matmul_mx(T.ps[:, 512 * bank:512 * bank + n], w, ws, x, xs, True, True), rd, ["b%d" % bank])

    def bank(b, n):
        return T.ps[:, 512 * b:512 * b + n]

    def k18(k):
        return slice(18 * k, 18 * k + 18)

    def kc(k):
        return slice(C * k, C * k + C)

    def lane(k, a=0, e=C):
        return slice(3 * a + LANE[k], 3 * e, 3)

    def keys(name, *ks):
        return ["%s%s" % (name, k) for k in ks]

    def xkeys(r, i):
        return ["x%d.%d%d" % (r, i, b) for b in range(4)]

    def runs(r):
        return [(0, CUT[r]), (CUT[r], C)]

    def take(todo, n):
        for call in todo[:n]:
            call()
        del todo[:n]

    dma("y", "u", T.ut[:], T.u[:], [], ["ut"])
    dma("y", "w", T.wi[:], T.wl[:], [], ["wi"])
    for i, (a, e) in enumerate(runs(0)):
        dma("y", "x%d" % i, T.x0[:, 4 * a:4 * e], T.x[:, 4 * a:4 * e], [], xkeys(0, i))
    dma("y", "wc", T.wq[:, 0:512].bitcast(dt.uint8), T.wc[:, 0:2048], ["ut"], ["wq"])
    dma("y", "ws", T.wsc[:, 0:512], T.ws[:, 0:512], [], ["wsc"])
    dma("y", "v", T.vt[:], T.v[:], [], ["vt"])

    def iota(out, pattern, base, cm, wr, small=False):
        if small:
            op("g", lambda e: e.iota(out, pattern, base, cm, allow_small_or_imprecise_dtypes=True), [], wr)
        else:
            op("g", lambda e: e.iota(out, pattern, base, cm), [], wr)
    idn = T.tab[:, 3 * C:6 * C]
    conv = T.vw[:, 3 * C:6 * C]
    iota(T.ei[:], [[1, 16]], 128, -1, ["ei"])
    iota(T.i1[:], [[0, 18]], 0, 1, ["i1"])
    iota(T.i2[:], [[16, 54]], 0, 0, ["i2"])
    iota(T.ui[:], [[1, 2], [16, 8]], 0, 0, ["ui"])
    for k in (1, 2, 0):
        iota(T.vw[:, kc(3 + k)], [[3, C]], LANE[k] - 1, 0, ["conv%d" % k], True)

    def unit(b):
        op("g", lambda e: e.affine_select(T.et[:, 512 * b:512 * b + 512], T.ones[:], [[-1, 512]], A.is_equal, 0.0, b, 4),
           ["ones"], ["et%d" % b])
    op("v", lambda e: e.memset(T.ones[:], 1.0), [], ["ones"])
    for b in range(3):
        unit(b)

    def mask(behind, own, prev, m, n, key):
        return [lambda: ts(own[:], behind[:], 0.0, A.is_equal, [key], [key + "0"], 2.0, A.mult),
                lambda: ts(prev[:], behind[:], n - 1.0, A.is_equal, [key], [key + "1"], -4.0, A.mult),
                lambda: ts(m[:, n - 1:n], own[:, n - 1:n], -3.0, A.add, [key + "0"], [key + "b"]),
                lambda: tt(m[:, 0:n - 1], own[:, 0:n - 1], prev[:, 0:n - 1], A.add, [key + "0", key + "1"], [key + "a"])]
    ts(T.ea[:], T.ei[:], 15, A.bitwise_and, ["ei"], ["ea"])
    ts(T.fa[:], T.ei[:, 3:16:4], 15, A.bitwise_and, ["ei"], ["fa"], 2, A.logical_shift_right)
    m16, m4 = mask(T.ea, T.e0, T.e1, T.m16, 16, "ea"), mask(T.fa, T.f0, T.f1, T.m4, 4, "fa")
    take(m16, 2)
    ts(T.i3[:], T.i1[:], 15, A.bitwise_and, ["i1"], ["i3"])
    take(m16, 2)
    cp(T.io16[:], T.i3[:], ["i3"], ["io16"])
    cp(T.icol[:, 0:1], T.i3[:, 0:1], ["i3"], ["icol"])
    ts(T.j4[:], T.i1[:], 3, A.bitwise_and, ["i1"], ["j4"])
    take(m4, 2)
    cp(T.jo4[:], T.j4[:], ["j4"], ["jo4"])
    take(m4, 2)
    ts(T.port[:], T.i2[:], T.icol[:, 0:1], A.add, ["i2", "icol"], ["port"])
    cp(T.bcol[:, 0:1], T.j4[:, 0:1], ["j4"], ["bcol"])
    cp(T.uo[:], T.ui[:], ["ui"], ["uo"])
    ac(T.mf[:], T.m16[:, 0:16].indirect(T.io16[:, 0:18]), ["eaa", "eab", "io16"], ["mf"], B1)
    ac(T.mq[:], T.m4[:, 0:4].indirect(T.jo4[:, 0:18]), ["faa", "fab", "jo4"], ["mq"], B4)

    def wired(a, e):
        return T.gs[:, C * a + 15:C * e:16]

    def step(t, a, e):
        return t[:, 36 * a:36 * e:2]

    def base(t, a, e):
        return t[:, 36 * a + 1:36 * e:2]

    def halves(r, i, planes=range(4), q="s"):
        a, e = runs(r)[i]
        for b in planes:
            out, x, rd, wr = T.xh[:, C * b + a:C * b + e], T["x%d" % r][:, 4 * a + b:4 * e:4], ["x%d.%d%d" % (r, i, b)], ["xh%d%d" % (i, b)]
            if q == "s":
                ac(out, x, rd, wr, 0.5)
            else:
                ts(out, x, 0.5, A.mult, rd, wr)

    def qstate(r, i):
        a, e = runs(r)[i]
        quant(T.qx[:, a:e], T.sx[:, a:e], T["x%d" % r][:, 4 * a:4 * e], xkeys(r, i), ["qx%d" % i])

    def scores(r, i):
        a, e = runs(r)[i]
        for k in (0, 1):
            mm(2 * i + k, e - a, T.u2[:, 128 * k:128 * k + 128], T.u2s[:, 128 * k:128 * k + 128], T.qx[:, a:e], T.sx[:, a:e],
               ["u2", "u2s", "qx%d" % i])

    def ports(r, k, a=0, e=C):
        return lane(k, a, e) if r else slice(C * k + a, C * k + e)

    def signs(r):
        return T.a2 if r else T.a0

    def sign_a(i, r):
        a, e = runs(r)[i]
        ac(signs(r)[:, ports(r, 1, a, e)], bank(2 * i, e - a), ["b%d" % (2 * i)], ["a2a%d" % i], bias=-TINY, func=F.Sign)

    def low(r, i):
        return 1 if i or r == 0 else 0

    def sign_b(i, r):
        a, e = runs(r)[i]
        out, score, rd, wr = signs(r)[:, ports(r, 0, a, e)], bank(2 * i + 1, e - a), ["b%d" % (2 * i + 1)], ["a2b%d" % i]
        if low(r, i):
            ts(out, score, 0.0, A.is_le, rd, wr, -2.0, A.mult)
        else:
            ac(out, score, rd, wr, bias=-TINY, func=F.Sign)

    def capped(r):
        for i, (a, e) in enumerate(runs(r)):
            ac(T.cap[:, a // 16:e // 16], T.act[:, a // 16:e // 16], ["act"], ["cap%d" % i], 2 * B1, -B1 - 1 - low(r, i))

    def principal(r, i):
        a, e = runs(r)[i]
        k = 2 - low(r, i)
        scan(T.tab[:, ports(r, 0, a, e)], T.vw[:, (3 + k) * C + a:(3 + k) * C + e], signs(r)[:, ports(r, 0, a, e)],
             ["conv%d" % k, "a2b%d" % i], ["tab0%d" % i])

    def far(q, r):
        a, e = (0, OPT["fs"]) if q == "s" else (OPT["fs"], C)
        if a < e:
            (ac if q == "s" else cp)(T.fr[:, a:e], signs(r)[:, 0:(3 if r else 2) * C].indirect(T.eo[:, a // 16:e // 16]),
                                     ["a2a0", "a2a1", "a2b0", "a2b1", "eo"] + (["a2c"] if r else []), ["fr" + q])

    act = T.act[:, k18(0)]
    gs = keys("gs", 0, 1, 2)

    def erow(k):
        ac(T.er[:, kc(k - 1)], T.gw[:, 0:3 * C].indirect(T.eo[:, k18(k - 1)]), keys("gw", 0, 1, 2) + ["eo"], ["er%d" % k])

    def escan(k):
        scan(T.es[:, kc(k)], T.er[:, kc(k - 1)], T.mn[:], ["mn", "er%d" % k], ["es%d" % k])

    def turned(k):
        j = (k + 2) % 3
        ac(T.src[:, k18(k)], wired(j, j + 1), ["gs%d" % j], ["src%d" % k], 1.0, 3.0 * C + LANE[1] if k == 1 else 0.0)

    def ahead(r):
        return {
            "zi": lambda: ac(T.zi[:], wired(0, 1), ["gs0"], ["zi"], 1.0 / 3, B / 3 + H1),
            "e3": lambda: ac(T.e3[:], T.zi[:], ["zi"], ["e3"], 3.0, -3 * H1 - B - 1),
            "tu": lambda: [turned(k) for k in range(3)],
            "zv": lambda: ts(T.zi[:], wired(0, 1), 1.0 / 3, A.mult, ["gs0"], ["zi"], B / 3 + H1, A.add),
            "ev": lambda: ts(T.e3[:], T.zi[:], 3.0, A.mult, ["zi"], ["e3"], -3 * H1 - B - 1, A.add),
            "qs": lambda: ac(T.qq[:], act, ["act"], ["qq"], 2.0, -1.0),
            "qq": lambda: ts(T.qq[:], act, 2.0, A.mult, ["act"], ["qq"], -1.0, A.add),
            "sc": lambda: [ac(T.act[:, k18(1)], act, ["act"], ["act1"]), ac(T.act[:, k18(2)], act, ["act"], ["act2"]),
                           ac(T.a2x[:], act, ["act"], ["a2x"], 2.0)],
            "act": lambda: tt(act, wired(0, 1), T.e3[:], A.is_equal, ["gs0", "e3"], ["act"]),
            "w0c": lambda: tt(T.w0c[:], wired(0, 1), T.c3m[:], A.subtract, ["gs0", "c3m"], ["w0c"]),
            "tt": lambda: tt(T.tt[:], T.w0c[:], act, A.mult, ["w0c", "act"], ["tt"]),
            "ap1": lambda: tt(T.ap[:, k18(1)], T.tt[:], T.cb[:, k18(1)], A.add, ["tt", "cb1"], ["ap1"]),
            "ap0": lambda: tt(T.ap[:, k18(0)], T.ap[:, k18(1)], T.qq[:], A.add, ["qq", "ap1"], ["ap0"]),
            "eo": lambda: [cp(T.eo[:], T.ap[:], ["ap0", "ap1"], ["eo"]), erow(1), erow(2)],
            "df": lambda: tt(T.df[:], T.src[:], wired(0, 3), A.subtract, keys("src", 0, 1, 2) + gs, ["df"]),
            "bp": lambda: tt(base(T.pp, 0, 2), T.cb[:], T.act[:, 0:36], A.subtract, ["cb0", "cb1", "act", "act1"], ["bp"]),
            "dg": lambda: tt(T.dg[:], T.df[:], T.act[:], A.mult, ["df", "act", "act1", "act2"], ["dg"]),
            "dp": lambda: tt(step(T.pp, 0, 2), T.ap[:], base(T.pp, 0, 2), A.subtract, ["ap0", "ap1", "bp"], ["dp"]),
            "bc": lambda: tt(base(T.pc, 0, 3), T.dg[:], wired(0, 3), A.add, ["dg"] + gs, ["bc"]),
            "es0": lambda: tt(T.es[:, 15:C:16], base(T.pc, 1, 2), T.a2x[:], A.subtract, ["bc", "a2x"], ["es0"]),
            "es1": lambda: escan(1),
            "es2": lambda: escan(2),
            "dc": lambda: tt(step(T.pc, 0, 3), T.es[:, 15:3 * C:16], base(T.pc, 0, 3), A.subtract, keys("es", 0, 1, 2) + ["bc"], ["dc"]),
            "p0": lambda: principal(r, 0),
            "p1": lambda: principal(r, 1),
            "..": lambda: None}

    ts(T.mn[:], T.mf[:], B / B1, A.mult, ["mf"], ["mn"])
    quant(T.uq[:, 0:128], T.us[:, 0:128], T.ut[:, 0:512], ["ut"], ["uq"])
    ts(act, T.wi[:, 0:18], float(C), A.is_lt, ["wi"], ["act"])
    tt(T.w0c[:], T.wi[:, 0:18], T.port[:, k18(0)], A.subtract, ["wi", "port"], ["w0c"])
    op("s", lambda e: e.activation(T.u2s[:, 0:256], T.us[:, 0:128].indirect(T.uo[:, 0:16]), F.Copy), ["uq", "uo"], ["u2s"])
    op("v", lambda e: e.tensor_copy(T.u2[:, 0:256].bitcast(dt.uint32), T.uq[:, 0:128].bitcast(dt.uint32).indirect(T.uo[:, 0:16])),
       ["uq", "uo"], ["u2"])
    qstate(0, 0)
    scores(0, 0)
    tt(T.tt[:], T.w0c[:], act, A.mult, ["w0c", "act"], ["tt"])
    times = (1, -2, 2, 3, -1)
    ac(T.by[:, k18(0)], act, ["act"], ["by0"], float(C))
    qstate(0, 1)
    scores(0, 1)
    tt(T.own[:], T.tt[:], T.port[:, k18(0)], A.add, ["tt", "port"], ["own"])
    cp(T.off[:], T.wi[:], ["wi"], ["off"])
    for k in range(1, 5):
        ac(T.by[:, k18(k)], act, ["act"], ["by%d" % k], float(times[k] * C))
    ac(step(T.pp, 0, 1), T.tt[:], ["tt"], ["dp0"], 1.0, -float(C))
    tt(T.ap[:, k18(0)], T.own[:], T.by[:, k18(0)], A.add, ["own", "by0"], ["ap0"])
    sign_a(0, 0)
    sign_b(0, 0)
    cp(T.eo[:, k18(0)], T.ap[:, k18(0)], ["ap0"], ["eo"])
    tt(base(T.pp, 0, 2), T.port[:, 18:54], T.by[:, 0:36], A.add, ["port", "by0", "by1"], ["bp"])
    capped(0)
    sign_a(1, 0)
    sign_b(1, 0)
    halves(0, 0, OPT["x"][0])
    tt(step(T.pp, 1, 2), T.tt[:], T.by[:, k18(2)], A.add, ["tt", "by2", "dp0"], ["dp"])
    far("s", 0)
    ac(T.fl[:, 0:108:2], T.port[:], ["port"], ["fl0"], 0.0)
    ac(step(T.pc, 0, 1), T.tt[:], ["tt"], ["dc0"], 1.0, float(C))
    ac(step(T.pc, 1, 2), act, ["act"], ["dc1"], -2.0 * C, -float(C))
    halves(0, 0, OPT["x"][1])
    halves(0, 1, OPT["x"][2])
    todo = [lambda: tt(base(T.pc, 0, 3), T.port[:], T.by[:, 36:90], A.add, ["port", "by2", "by3", "by4"], ["bc"]),
            lambda: principal(0, 0),
            lambda: tt(base(T.pc, 1, 2), base(T.pc, 1, 2), T.tt[:], A.add, ["bc", "tt"], ["bc"]),
            lambda: tt(step(T.pc, 2, 3), T.tt[:], T.by[:, k18(0)], A.add, ["tt", "by0", "dc0", "dc1"], ["dc"]),
            lambda: principal(0, 1)]
    fill = OPT["fill"]

    for r in range(3):
        peer = T.cores[rank ^ STEP[r]]
        rid, pid = topo.addr(peer, core)
        engines = topo.mask(core, peer)
        arrive = len(topo.engines(peer, core))
        last = r == 2

        def send(dst, src, sem, rd):
            before("g", rd, [])
            g.remote_dma(out_ap=dst, in_ap=src, remote_sem=T.sem[sem], local_sem=T.sem.loc, pid=pid, routing_id=rid,
                         dma_engine_mask=engines)
            total["loc"] = total.get("loc", 0) + len(topo.engines(core, peer))

        def arrival(sem, key):
            wrote[key] = (sem, arrive)
            snap[(sem, arrive)] = {}
            total[sem] = arrive
        arrival("ra%d" % r, "la")
        for i in range(2):
            arrival("rq%d%d" % (i, r), "lq%d" % i)
            arrival("rs%d%d" % (i, r), "ls%d" % i)
        ol, la, zl = T["ol%d" % r], T["la%d" % r], T.zl
        lq, ls, qh, sh = T["lq%d" % r], T["ls%d" % r], T["qh%d" % r], T["sh%d" % r]

        scan(T.am[:], signs(r)[:, ports(r, 1)], T.mf[:], ["mf", "a2a0", "a2a1"], ["am"])
        far("v", r)
        take(todo, fill["am"])
        tt(T.own[:], T.am[:, 15:C:16], T.cap[:], A.min, ["am", "cap0", "cap1"], ["own"])
        take(todo, 0 if r else 1)
        scan(T.fs[:], T.fr[:], T.mf[:], ["mf", "frs"] + (["frv"] if OPT["fs"] < C else []), ["fs"])
        take(todo, fill["fs"] if r else 1)
        tt(T.fl[:, 1:36:2], T.fs[:, 15:C:16], T.own[:], A.not_equal, ["fs", "own"], ["fl"])
        for k in (1, 2):
            ac(T.fl[:, 36 * k + 1:36 * k + 36:2], T.fl[:, 1:36:2], ["fl"], ["fl%d" % k])
        take(todo, fill["fl"] if r else 2)
        if r == 0:
            halves(0, 1, OPT["x"][3])

        def choose(out, f, pairs, rd, wr):
            op("v", lambda e: e.tensor_tensor_scan(out, f, pairs, 0.0, A.mult, A.add), ["fl", "fl0"] + rd, wr)
        for k in range(2):
            s = slice(36 * k, 36 * k + 36)
            choose(T.pl[:, s], T.fl[:, 0:36], T.pp[:, s], ["dp", "bp"], ["pl%d" % k])
        take(todo, fill["pl"])
        cp(T.po[:], T.pl[:, 1:72:2], keys("pl", 0, 1), ["po"])
        own, ik = (idn, ["idn"]) if r else (conv, keys("conv", 0, 1, 2))
        ac(T.tab[:, ports(r, 1)], own.indirect(T.po[:, k18(0)]), ik + ["po"], ["tab1"])
        take(todo, 9)
        choose(T.cl[:], T.fl[:], T.pc[:], ["fl1", "fl2", "dc", "bc"], ["cl"])
        cp(T.tab[:, ports(r, 2)], own.indirect(T.po[:, k18(1)]), ik + ["po"], ["tab2"])
        ts(T.co[:], T.cl[:, 1:108:2], B + 1 if r else 0.0, A.add, ["cl"], ["co"])
        tab, tk = T.tab[:, 0:6 * C], keys("tab", "00", "01", 1, 2)
        if r == 0:
            cut = OPT["vw"]
            ac(T.vw[:, 0:16 * cut], T.tab[:, 0:3 * C].indirect(T.off[:, 0:cut]), tk + ["off"], ["vws"])
            cp(T.vw[:, 16 * cut:3 * C], T.tab[:, 0:3 * C].indirect(T.off[:, cut:54]), tk + ["off"], ["vwv"])
            tab, tk = T.vw[:, 0:6 * C], ["vws", "vwv"]
            halves(0, 1, OPT["x"][4], "v")
        else:
            halves(r, 1, range(OPT["hv"], 4))
        for k, by in zip(OPT["gw"][r], (cp, ac, ac)):
            out, key = (T.gh[:, kc(k)], "gh%d" % k) if k in OPT["narrow"] else (T.gw[:, lane(k)], "gw%d" % k)
            by(out, tab.indirect(T.co[:, k18(k)]), tk + ik + ["co"], [key])
        if r == 0:
            ac(T.c3m[:], T.port[:, k18(0)], ["port"], ["c3m"], 3.0, -B - 1)
            for k in (0, 1):
                ac(T.cb[:, k18(k)], T.port[:, k18(0)], ["port"], ["cb%d" % k], 3.0, float(LANE[k + 1]))
        nxt = {} if last else ahead(r + 1)
        todo = [] if last else [nxt[n] for n in OPT["early"].split()]

        def gscan(k):
            row, key = (T.gh[:, kc(k)], "gh%d" % k) if k in OPT["narrow"] else (T.gw[:, lane(k)], "gw%d" % k)
            scan(T.gs[:, kc(k)], row, T.mn[:], ["mn", key], ["gs%d" % k])

        def agents(k):
            ts(zl[:, k18(k - 1)], wired(k, k + 1), 1.0 / 3, A.mult, ["gs%d" % k], ["zo%d" % k], B / 3, A.add)

        def ask():
            ts(ol[:], wired(0, 1), B + 1, A.add, ["gs0"], ["ol"])
            send(la[:], ol[:], "ra%d" % r, ["ol"])
        steps = {"0": lambda: gscan(0), "1": lambda: gscan(1), "2": lambda: gscan(2), "o": ask, "n": lambda: take(todo, 1),
                 "a": lambda: agents(1), "b": lambda: agents(2)}
        for name in OPT["g"][r]:
            steps[name]()
        if r == 0:
            unit(3)

        def zquant(i):
            a, e = LAY[i]
            quant(T.qz[:, a:e], T.sz[:, a:e], T.z[:, 4 * a:4 * e], keys("z%d" % i, 0, 1, 2, 3), ["qz%d" % i])
            for b in range(4):
                mm(4 - 4 * i + b, e - a, T.wq[:, 128 * b:128 * b + 128], T.wsc[:, 128 * b:128 * b + 128], T.qz[:, a:e],
                   T.sz[:, a:e], ["wq", "wsc", "qz%d" % i])

        def hcopy(q, n):
            i, b = divmod(n, 4)
            a, e = LAY[i]
            k = 4 - 4 * i + b
            if q == "s":
                ac(T.h[:, 4 * a + b:4 * e:4], bank(k, e - a), ["b%d" % k], ["h%d%d" % (i, b)], 0.03125)
            else:
                ts(T.h[:, 4 * a + b:4 * e:4], bank(k, e - a), 0.03125, A.mult, ["b%d" % k], ["h%d%d" % (i, b)])

        def widen(k):
            if k in OPT["narrow"]:
                ac(T.gw[:, lane(k)], T.gh[:, kc(k)], ["gh%d" % k], ["gw%d" % k])
        steps = {
            "mr": lambda: ac(T.mr[:], T.gw[:, 0:3 * C].indirect(la[:, 0:18]), keys("gw", 0, 1, 2) + ["la"], ["mr"], 4.0 / 3, H4),
            "ms": lambda: scan(T.ms[:], T.mr[:], T.mq[:], ["mq", "mr"], ["ms"]),
            "mo": lambda: ts(T.mo[:], T.ms[:, 3:C:4], B4 - H4, A.add, ["ms", "bcol"], ["mo"], T.bcol[:, 0:1], A.add),
            "q1": lambda: zquant(1),
            "w0": lambda: widen(0), "w1": lambda: widen(1), "w2": lambda: widen(2),
            "--": lambda: take(todo, 1)}

        def run(names):
            for name in names.split():
                if name in steps:
                    steps[name]()
                elif name[0] in "sv" and name[1].isdigit():
                    hcopy(name[0], int(name[1]))
                elif not last:
                    nxt[name]()
        run(OPT["z"][0])
        for i, (a, e) in enumerate(LAY):
            for b in range(4):
                xh = T.xh[:, kc(b)]
                xk = ["xh0%d" % b, "xh1%d" % b]
                ac(T.zp[:, C * b + a:C * b + e], xh.indirect(zl[:, a // 16:e // 16]), xk + ["zo1"], ["zp%d%d" % (i, b)])
                tt(T.z[:, 4 * a + b:4 * e:4], xh.indirect(zl[:, 18 + a // 16:18 + e // 16]),
                   T.zp[:, C * b + a:C * b + e], A.add, xk + ["zo2", "zp%d%d" % (i, b)], ["z%d%d" % (i, b)])
                if (i, b) == (1, 0):
                    zquant(0)
                run(OPT["z"][4 * i + b + 1])
        run(OPT["h"][r])

        hk = ["h%d%d" % (i, b) for i in range(2) for b in range(4)] + ["mo"]

        def hlay(q, a, e):
            (ac if q == "s" else cp)(T.hp[:, 4 * a:4 * e], T.h[:, 0:4 * C].indirect(T.mo[:, a // 4:e // 4]), hk, ["hp%d" % a])

        def hquant(i, parts):
            a, e = runs(r + 1)[i]
            quant(qh[:, a:e], sh[:, a:e], T.hp[:, 4 * a:4 * e], keys("hp", *parts), ["qh%d" % i])
            send(lq[:, a:e].bitcast(dt.uint8), qh[:, a:e].bitcast(dt.uint8), "rq%d%d" % (i, r), ["qh%d" % i])
            send(ls[:, a:e], sh[:, a:e], "rs%d%d" % (i, r), ["qh%d" % i])
        c0, c1, c2, c3 = 0, CUT[r + 1] // 16 * 8, CUT[r + 1], C - OPT["sb"][r]
        hlay("s", c0, c1)
        hlay("v", c1, c2)
        hlay("s", c2, c3)
        run(OPT["s"])
        cm = C - OPT["sm"][r]
        if cm < C:
            hlay("v", cm, C)
        take(todo, fill["l0"])
        hquant(0, (c0, c1))
        if c3 < cm:
            hlay("v", c3, cm)
        take(todo, fill["l1"])
        hquant(1, [c for c in (c2, c3, cm) if c < C])

        if r == 0:
            iota(idn, [[1, 3 * C]], -1, 0, ["idn"], True)
        if r == 1:
            for k in range(3):
                iota(T.unp[:, lane(k)], [[1, C]], C * k, 0, ["unp%d" % k], True)
        if last:
            ts(T.off[:], wired(0, 3), B + 1, A.add, gs, ["off"])
            quant(T.vq[:, 0:128], T.vs[:, 0:128], T.vt[:, 0:512], ["vt"], ["vq"])
            ac(T.owt[:], T.unp[:, 0:3 * C].indirect(T.off[:, 0:54]), keys("unp", 0, 1, 2) + ["off"], ["owt"])
            dma("y", "out", T.ow[:], T.owt[0:128:16, :], ["owt"], [])
        else:
            take(todo, 9)
            todo = [nxt[n] for n in OPT["fly"][r].split()]
            if r == 0:
                quant(T.eq[:, 0:512], T.esc[:, 0:512], T.et[:, 0:2048], keys("et", 0, 1, 2, 3), ["eq"])
            take(todo, fill["fly"][r])
            capped(r + 1)
            if r == 0:
                ac(T.a2[:, lane(2)], T.mf[:], ["mf"], ["a2c"])

        x, y = T["x%d" % r], T["x%d" % (r + 1)]
        for i, (a, e) in enumerate(runs(r + 1)):
            for b in range(4):
                mm(4 * i + b, e - a, T.eq[:, 128 * b:128 * b + 128], T.esc[:, 128 * b:128 * b + 128], lq[:, a:e], ls[:, a:e],
                   ["eq", "lq%d" % i, "ls%d" % i])
        for i, (a, e) in enumerate(runs(r + 1)):
            for b in range(4):
                k = 4 * i + b
                tt(y[:, 4 * a + b:4 * e:4], bank(k, e - a), x[:, 4 * a + b:4 * e:4], A.add,
                   ["b%d" % k, "x%d.%d%d" % (r, i, b)], ["x%d.%d%d" % (r + 1, i, b)])
            take(todo, fill["a%d" % i])
            qstate(r + 1, i)
            if not last:
                scores(r + 1, i)
                if i == 0:
                    halves(r + 1, 0)
                    sign_b(0, r + 1)
                    sign_a(0, r + 1)
                else:
                    take(todo, fill["mm"])
                    sign_a(1, r + 1)
                    sign_b(1, r + 1)
                    far("s", r + 1)
                    halves(r + 1, 1, range(OPT["hv"]))

    for i, (a, e) in enumerate(runs(3)):
        mm(i, e - a, T.vq[:, 0:128], T.vs[:, 0:128], T.qx[:, a:e], T.sx[:, a:e], ["vq", "qx%d" % i])
        dma("y", "out", T.oc[:, 4 * a:4 * e], T.qx[:, a:e].bitcast(dt.uint8), ["qx%d" % i], [])
        (cp if i else ac)(T.yt[:, a:e], bank(i, e - a), ["b%d" % i], ["yt%d" % i])
        if i:
            for k in range(4):
                dma("ys"[k % 2], "out", T.osc[4 * k:4 * k + 4, 0:C], T.sx[32 * k:32 * k + 4, 0:C], ["qx0", "qx1"], [])
        dma("s", "out", T.y[:, a:e], T.yt[:, a:e], ["yt%d" % i], [])
    for s, m in sorted(total.items(), reverse=True):
        if waited.get(s, 0) < m:
            g.wait_ge(T.sem[s], m)
